import numpy as np
import ml_dtypes


def mxq(x, axis, fmt="e4m3"):
    dtype, down = {"e4m3": (ml_dtypes.float8_e4m3fn, 7), "e5m2": (ml_dtypes.float8_e5m2, 14)}[fmt]
    v = np.moveaxis(np.asarray(x, np.float32).astype(ml_dtypes.bfloat16).astype(np.float64), axis, -1)
    blocks = v.reshape(v.shape[:-1] + (-1, 32))
    amax = np.abs(blocks).max(-1, keepdims=True)
    byte = np.maximum(np.where(amax > 0, np.frexp(amax)[1] - 1 + 127, 0) - down, 1)
    scale = np.exp2(byte - 127.0)
    codes = (blocks / scale).astype(np.float32).astype(dtype).astype(np.float64)
    return np.moveaxis((codes * scale).reshape(v.shape), -1, axis)


WIDE = False


def mx_kscale(k):
    if not WIDE:
        return np.ones(k)
    levels = np.array([10, -10, 5, -5, 0])
    if k % 512:
        return np.exp2(np.random.permutation(np.resize(levels, k // 32))).repeat(32)
    a = np.empty((k // 512, 16))
    for p in range(k // 512):
        a[p, :8] = np.random.permutation(np.resize(levels, 8))
        for g in range(8):
            far = levels[np.abs(levels - a[p, g]) >= 10]
            a[p, g + 8] = far[np.random.randint(len(far))]
    return np.exp2(a.ravel()).repeat(32)


def f64(x):
    return np.asarray(x).astype(np.float64)


def striped(idx):
    return np.tile(idx.reshape(-1, 16).T, (8, 1)).astype(np.uint16)


def unstriped(offs):
    return offs[:16].T.reshape(-1).astype(np.int64)


E2M1 = np.array([0.0, 0.5, 1.0, 1.5, 2.0, 3.0, 4.0, 6.0, -0.0, -0.5, -1.0, -1.5, -2.0, -3.0, -4.0, -6.0])


def pack_weight(w, fmt):
    k, n = w.shape
    w = f64(np.asarray(w, np.float32).astype(ml_dtypes.bfloat16)).reshape(k // 32, 32, n)
    amax = np.abs(w).max(1)
    if fmt == "e4m3":
        byte = np.frexp(amax)[1] - 1 + 127 - 7
    else:
        mant, ex = np.frexp(amax / 6.0)
        byte = np.where(mant > 0.5, ex, ex - 1) + 127
    byte = np.clip(np.where(amax > 0, byte, 1), 1, 254)
    scaled = (w * np.exp2(127.0 - byte)[:, None, :]).reshape(k, n).astype(np.float32)
    by_word = np.ascontiguousarray(scaled.reshape(k // 512, 128, 4, n).transpose(0, 1, 3, 2))
    if fmt == "e4m3":
        words = by_word.astype(ml_dtypes.float8_e4m3fn).view(np.uint8)
    else:
        c = by_word.astype(ml_dtypes.float4_e2m1fn).view(np.uint8) & 0xF
        words = (c[..., 0::2] | (c[..., 1::2] << 4)).reshape(k // 512, 128, 2 * n)
    return np.ascontiguousarray(words), np.ascontiguousarray(byte.astype(np.uint8).reshape(k // 512, 16, n))


def unpack_weight(words, scales, fmt):
    g, _, n = scales.shape
    words = np.ascontiguousarray(words).reshape(g, 128, n, -1)
    if fmt == "e4m3":
        vals = words.view(ml_dtypes.float8_e4m3fn).astype(np.float64)
    else:
        nib = np.empty((g, 128, n, 4), np.uint8)
        nib[..., 0::2] = words & 0xF
        nib[..., 1::2] = words >> 4
        vals = E2M1[nib]
    vals = vals * np.repeat(np.exp2(scales.astype(np.float64) - 127.0), 8, axis=1)[..., None]
    return vals.transpose(0, 1, 3, 2).reshape(g * 512, n)


def gelu(v):
    return 0.5 * v * (1.0 + np.tanh(np.sqrt(2.0 / np.pi) * (v + 0.044715 * v**3)))


K, H, N, T, S, T2 = 1024, 512, 512, 4096, 1024, 2048

def setup_inputs():
    n = np.random.standard_normal
    s = mx_kscale(K)[:, None]
    u = mx_kscale(H)[:, None]
    e = mx_kscale(S)[:, None]
    tab_words, tab_scales = pack_weight(n((K, T)) * s, "e4m3")
    tab2_words, tab2_scales = pack_weight(n((K, T)) * s, "e4m3")
    w2_words, w2_scales = pack_weight(n((K, H)) / np.sqrt(K) / s * u.T, "e2m1")
    w3_words, w3_scales = pack_weight(n((H, N)) / np.sqrt(H) / u, "e4m3")
    perm = np.random.permutation(T2)
    return {
        "tab_words": tab_words, "tab_scales": tab_scales,
        "tab2_words": tab2_words, "tab2_scales": tab2_scales,
        "offs": striped(np.random.permutation(T)[:S]),
        "offs2": striped(np.random.permutation(T)[:S]),
        "offs3": striped(perm[:S]), "offs4": striped(perm[S:]),
        "w1": (n((K, H)) / np.sqrt(K) / s * u.T).astype(np.float32),
        "gain": (np.exp(0.3 * n(S)) * e[:, 0]).astype(np.float32),
        "blend": (n((S, S)) / np.sqrt(S) / e).astype(np.float32),
        "w2_words": w2_words, "w2_scales": w2_scales,
        "wg1": np.exp(0.3 * n((128, S))).astype(np.float32),
        "wg2": np.exp(0.3 * n((128, S))).astype(np.float32),
        "bias": (0.5 * n(H) * u[:, 0]).astype(np.float32),
        "w3_words": w3_words, "w3_scales": w3_scales,
    }

def reference(tab_words, tab_scales, tab2_words, tab2_scales, offs, offs2, offs3, offs4, w1, gain, blend,
              w2_words, w2_scales, wg1, wg2, bias, w3_words, w3_scales):
    v = unpack_weight(tab_words, tab_scales, "e4m3")[:, unstriped(offs)]
    v2 = unpack_weight(tab2_words, tab2_scales, "e4m3")[:, unstriped(offs2)]
    a = (v.T @ mxq(f64(w1), 0, "e4m3")) * f64(gain)[:, None]
    h1 = mxq(a, 0, "e4m3").T @ mxq(f64(blend), 0, "e4m3")
    h2 = np.abs(unpack_weight(w2_words, w2_scales, "e2m1").T @ v2)
    page = np.zeros((H, T2))
    page[:, unstriped(offs3)] = np.tile(f64(wg1), (H // 128, 1)) * h1
    page[:, unstriped(offs4)] = np.tile(f64(wg2), (H // 128, 1)) * h2
    z = np.maximum(page + f64(bias)[:, None], 0.0)
    return unpack_weight(w3_words, w3_scales, "e4m3").T @ mxq(z, 0, "e4m3")

@@ -1,0 +1,306 @@
+from contextlib import ExitStack
+
+import concourse.mybir as mybir
+from concourse.masks import make_identity
+
+K, H, N, T, S, T2 = 1024, 512, 512, 4096, 1024, 2048
+FLOPS = 2 * (K * S * H + S * H * S + K * H * S + H * N * T2)
+
+F32 = mybir.dt.float32
+BF16 = mybir.dt.bfloat16
+I32 = mybir.dt.int32
+U32 = mybir.dt.uint32
+U16 = mybir.dt.uint16
+U8 = mybir.dt.uint8
+FP8X4 = mybir.dt.float8_e4m3fn_x4
+FP4X4 = mybir.dt.float4_e2m1fn_x4
+ACT = mybir.ActivationFunctionType
+MULT = mybir.AluOpType.mult
+
+P = 128
+PACK = 4
+PASS = P * PACK
+BANK = 512
+QUADS = 4
+
+
+def tile_list_terrain_weave_kernel(
+    tc, tab_words, tab_scales, tab2_words, tab2_scales, offs, offs2, offs3, offs4, w1, gain, blend,
+    w2_words, w2_scales, wg1, wg2, bias, w3_words, w3_scales, out,
+):
+    nc = tc.nc
+    with ExitStack() as ctx:
+        lists = ctx.enter_context(tc.tile_pool(name="lists", bufs=1))
+        sb = ctx.enter_context(tc.tile_pool(name="sb", bufs=1))
+        psum = ctx.enter_context(tc.psum_pool(name="psum", bufs=8))
+
+        def held(name, shape, dtype):
+            return sb.tile(shape, dtype, name=name, align_bytes=64)
+
+        def shared(tag, bufs, name, shape, dtype):
+            return sb.tile(shape, dtype, name=name, tag=tag, bufs=bufs, align_bytes=64)
+
+        def bank(name):
+            return psum.tile([P, BANK], F32, name=name, tag="bank")
+
+        def load_list(name, src):
+            dst = lists.tile([P, S // 16], U16, name=name)
+            nc.sync.dma_start(dst[:], src)
+            return dst
+
+        def zeroed(name, shape):
+            dst = held(name, shape, U8)
+            nc.vector.memset(dst[:].bitcast(I32), 0)
+            return dst
+
+        def load_table_scales(dst, src):
+            for q in range(QUADS):
+                nc.gpsimd.dma_start(dst[32 * q : 32 * q + 8, :].bitcast(I32), src[:, 4 * q : 4 * q + 4, :].bitcast(I32))
+
+        def load_table_words(name, src, a):
+            dst = shared("table", 2, name, [P, T], U32)
+            nc.sync.dma_start(dst[:].bitcast(I32), src[a].rearrange("p t i -> p (t i)").bitcast(I32))
+            return dst
+
+        def load_factor(name, src, u):
+            dst = held(name, [P, S], F32)
+            rows = src.rearrange("(q t) m -> t q m", t=PACK)[u]
+            for q in (0, 2, 1, 3):
+                nc.sync.dma_start(dst[32 * q : 32 * q + 32, :], rows)
+            return dst
+
+        def interleave(engine_copy, name, planes):
+            dst = shared("woven", 3, name, [P, planes.shape[2] * PACK], BF16)
+            engine_copy(
+                dst[:].rearrange("p (c i t) -> p c t i", i=4, t=PACK),
+                planes.rearrange("p t (c i) -> p c t i", i=4),
+            )
+            return dst
+
+        def quantize(codes, scales, woven):
+            nc.vector.quantize_mx(out=codes[:].bitcast(FP8X4), scales=scales[:], in_=woven[:])
+
+        sc2 = zeroed("sc2", [P, T])
+        w2s_raw = zeroed("w2s_raw", [P, 2 * H])
+        v2_scale1 = zeroed("v2_scale1", [P, S])
+        sc1 = zeroed("sc1", [P, T])
+        w3s = zeroed("w3s", [P, N])
+        gain_rows = held("gain_rows", [P, P], F32)
+        nc.vector.memset(gain_rows[:], 0.0)
+        load_table_scales(sc2, tab2_scales)
+        for q in range(QUADS):
+            nc.gpsimd.dma_start(
+                w2s_raw[32 * q : 32 * q + 4, :].bitcast(I32).rearrange("r (a c) -> r a c", a=2),
+                w2_scales[:, 4 * q : 4 * q + 4, :].bitcast(I32).rearrange("a r c -> r a c"),
+            )
+        load_table_scales(sc1, tab_scales)
+        ident = held("ident", [P, P], F32)
+        make_identity(nc, ident[:])
+
+        list2 = load_list("list2", offs2)
+        tab2_0 = load_table_words("tab2_0", tab2_words, 0)
+        w2_raw = held("w2_raw", [P, 2, 2 * H], U8)
+        nc.sync.dma_start(w2_raw[:].bitcast(I32), w2_words.bitcast(I32).rearrange("a p c -> p a c"))
+        tab2_1 = load_table_words("tab2_1", tab2_words, 1)
+        list4 = load_list("list4", offs4)
+        wg2_t = {0: load_factor("wg2_0", wg2, 0)}
+        list1 = load_list("list1", offs)
+
+        v2_scale0 = held("v2_scale0", [P, S], U8)
+        nc.vector.tensor_copy(v2_scale0[:], sc2[:].indirect(list2[:]))
+        nc.scalar.dma_start(v2_scale1[0:112, :].bitcast(I32), v2_scale0[4:116, :].bitcast(I32))
+        v2_scale = [v2_scale0, v2_scale1]
+        v2 = [shared("picked", 5, "v2_%d" % a, [P, S], U32) for a in range(2)]
+        nc.vector.tensor_copy(v2[0][:], tab2_0[:].indirect(list2[:]))
+        w2c = held("w2c", [P, 2, 2 * H], U8)
+        nc.vector.tensor_copy(
+            w2c[:].bitcast(U16).rearrange("p a (u m) -> p a u m", u=PACK),
+            w2_raw[:].bitcast(U16).rearrange("p a (m u) -> p a u m", u=PACK),
+        )
+        w2s = held("w2s", [P, 2 * H], U8)
+        nc.vector.tensor_copy(
+            w2s[:].rearrange("p (a u m) -> p a u m", a=2, u=PACK),
+            w2s_raw[:].rearrange("p (a m u) -> p a u m", a=2, u=PACK),
+        )
+        for half in range(2):
+            nc.vector.tensor_copy(
+                v2[1][:, BANK * half : BANK * (half + 1)], tab2_1[:].indirect(list2[:, 32 * half : 32 * (half + 1)])
+            )
+
+        pages = [held("page%d" % u, [P, T2], F32) for u in range(PACK)]
+
+        def plain_rows(u):
+            h = shared("h", 5, "h2_%d" % u, [P, S], F32)
+            for half in range(2):
+                cols = slice(BANK * half, BANK * (half + 1))
+                acc = bank("acc_h2")
+                for a in range(2):
+                    nc.tensor.matmul_mx(
+                        out=acc[:],
+                        lhsT=w2c[:, a, 256 * u : 256 * (u + 1)].bitcast(FP4X4),
+                        lhsT_scale=w2s[:, H * a + P * u : H * a + P * (u + 1)],
+                        rhs=v2[a][:, cols].bitcast(FP8X4),
+                        rhs_scale=v2_scale[a][:, cols],
+                        start=(a == 0),
+                        stop=(a == 1),
+                    )
+                nc.scalar.activation(h[:, cols], acc[:], ACT.Abs)
+            return h
+
+        def place(u, h, factor, where, pieces):
+            width = S // pieces
+            for i in range(pieces):
+                cols = slice(width * i, width * (i + 1))
+                nc.vector.tensor_tensor(
+                    pages[u][:].indirect(where[:, width // 16 * i : width // 16 * (i + 1)]), h[:, cols], factor[:, cols], MULT
+                )
+
+        h2 = [plain_rows(u) for u in range(PACK)]
+        place(0, h2[0], wg2_t[0], list4, 2)
+
+        v_scale_picked = held("v_scale_picked", [P, S], U8)
+        nc.vector.tensor_copy(v_scale_picked[:], sc1[:].indirect(list1[:]))
+        v_scale = held("v_scale", [P, S], U8)
+        nc.vector.tensor_copy(
+            v_scale[:].bitcast(I32).rearrange("p (t q w) -> p t q w", t=PACK, w=2),
+            v_scale_picked[:].bitcast(I32).rearrange("p (q t w) -> p t q w", t=PACK, w=2),
+        )
+
+        w1_raw = shared("raw", 2, "w1_raw", [P, 2, PACK, H], F32)
+        for a in range(2):
+            nc.sync.dma_start(w1_raw[:, a], w1[PASS * a : PASS * (a + 1), :].rearrange("(p j) c -> p j c", j=PACK))
+        wg2_t[1] = load_factor("wg2_1", wg2, 1)
+        for b in range(2):
+            nc.sync.dma_start(
+                gain_rows[PACK * b : PACK * (b + 1), :].rearrange("t (q i) -> t q i", i=8),
+                gain[PASS * b : PASS * (b + 1)].rearrange("(q t i) -> t q i", t=PACK, i=8),
+            )
+        w1c, w1s = [], []
+        for a in range(2):
+            w1c.append(held("w1c%d" % a, [P, H], U32))
+            w1s.append(held("w1s%d" % a, [P, H], U8))
+            quantize(w1c[a], w1s[a], interleave(nc.scalar.copy, "w1_woven", w1_raw[:, a]))
+        place(1, h2[1], wg2_t[1], list4, 1)
+
+        gain_turned = bank("gain_turned")
+        nc.tensor.transpose(gain_turned[:, 0:P], gain_rows[:], ident[:])
+        gains = held("gains", [P, 2 * PACK], F32)
+        nc.scalar.copy(gains[:], gain_turned[:, 0 : 2 * PACK])
+
+        def load_blend(b):
+            raw = shared("raw", 2, "blend_raw%d" % b, [P, PACK, S], F32)
+            rows = blend[PASS * b : PASS * (b + 1), :].rearrange("(q t i) m -> t q i m", t=PACK, i=8)
+            for t in range(PACK):
+                nc.sync.dma_start(raw[:, t, :], rows[t])
+            return raw
+
+        bc, bs = {}, {}
+
+        def quantize_blend(b, raw):
+            for half in range(2):
+                bc[b, half] = held("bc%d%d" % (b, half), [P, BANK], U32)
+                bs[b, half] = held("bs%d%d" % (b, half), [P, BANK], U8)
+                woven = interleave(nc.scalar.copy, "blend_woven", raw[:, :, BANK * half : BANK * (half + 1)])
+                quantize(bc[b, half], bs[b, half], woven)
+
+        quantize_blend(0, load_blend(0))
+        v = []
+        for a in range(2):
+            words = load_table_words("tab_%d" % a, tab_words, a)
+            v.append(shared("picked", 5, "v_%d" % a, [P, S], U32))
+            nc.vector.tensor_copy(
+                v[a][:].rearrange("p (t q i) -> p q t i", t=PACK, i=8), words[:].indirect(list1[:])
+            )
+        wg2_t[2] = load_factor("wg2_2", wg2, 2)
+        place(2, h2[2], wg2_t[2], list4, 1)
+
+        ac, asc = [], []
+        for b in range(2):
+            planes = held("a_planes%d" % b, [P, PACK, H], BF16)
+            for t in range(PACK):
+                cols = slice(2 * P * t + P * b, 2 * P * t + P * (b + 1))
+                acc = bank("acc_a")
+                for a in range(2):
+                    nc.tensor.matmul_mx(
+                        out=acc[:],
+                        lhsT=v[a][:, cols].bitcast(FP8X4),
+                        lhsT_scale=v_scale[PACK * a : P, cols],
+                        rhs=w1c[a][:].bitcast(FP8X4),
+                        rhs_scale=w1s[a][:],
+                        start=(a == 0),
+                        stop=(a == 1),
+                    )
+                nc.scalar.activation(
+                    planes[:, t, :].rearrange("p (u m) -> p u m", u=PACK),
+                    acc[:].rearrange("p (m u) -> p u m", u=PACK),
+                    ACT.Copy,
+                    scale=gains[:, PACK * b + t : PACK * b + t + 1],
+                )
+            ac.append(held("ac%d" % b, [P, H], U32))
+            asc.append(held("asc%d" % b, [P, H], U8))
+            quantize(ac[b], asc[b], interleave(nc.scalar.copy, "a_woven", planes[:]))
+
+        blend_raw1 = load_blend(1)
+        quantize_blend(1, blend_raw1)
+        list3 = load_list("list3", offs3)
+        wg1_t = {0: load_factor("wg1_0", wg1, 0)}
+        wg2_t[3] = load_factor("wg2_3", wg2, 3)
+        place(3, h2[3], wg2_t[3], list4, 1)
+        biases = held("biases", [P, PACK], F32)
+        nc.sync.dma_start(biases[:], bias.rearrange("(p t) -> p t", t=PACK))
+        for u in range(1, PACK):
+            wg1_t[u] = load_factor("wg1_%d" % u, wg1, u)
+        w3c = held("w3c", [P, N], U32)
+        nc.sync.dma_start(w3c[:].bitcast(I32), w3_words[0].rearrange("p c i -> p (c i)").bitcast(I32))
+        for q in range(QUADS):
+            nc.sync.dma_start(w3s[32 * q : 32 * q + 4, :].bitcast(I32), w3_scales[0, 4 * q : 4 * q + 4, :].bitcast(I32))
+
+        widths = [BANK // 2, BANK // 2, BANK, BANK, BANK]
+        chunks = [slice(sum(widths[:c]), sum(widths[: c + 1])) for c in range(len(widths))]
+        z_planes = [shared("picked", 5, "z_planes%d" % c, [P, PACK, w], BF16) for c, w in enumerate(widths)]
+        h1 = []
+        for u in range(PACK):
+            h = shared("h", 5, "h1_%d" % u, [P, S], F32)
+            h1.append(h)
+            for half in range(2):
+                acc = bank("acc_h1")
+                for b in range(2):
+                    nc.tensor.matmul_mx(
+                        out=acc[:],
+                        lhsT=ac[b][:, P * u : P * (u + 1)].bitcast(FP8X4),
+                        lhsT_scale=asc[b][:, P * u : P * (u + 1)],
+                        rhs=bc[b, half][:].bitcast(FP8X4),
+                        rhs_scale=bs[b, half][:],
+                        start=(b == 0),
+                        stop=(b == 1),
+                    )
+                nc.scalar.copy(h[:, BANK * half : BANK * (half + 1)], acc[:])
+        for u in range(PACK):
+            place(u, h1[u], wg1_t[u], list3, 2 if u == 0 else 1)
+            for c, cols in enumerate(chunks):
+                nc.scalar.activation(z_planes[c][:, u, :], pages[u][:, cols], ACT.Relu, bias=biases[:, u : u + 1])
+
+        staged = [shared("table", 2, "staged%d" % g, [P, 2, T2], F32) for g in range(2)]
+        out_rows = out.rearrange("(nb p) t -> p nb t", p=P)
+        for c, cols in enumerate(chunks):
+            zc = shared("zc", 2, "zc", [P, widths[c]], U32)
+            zs = shared("zs", 2, "zs", [P, widths[c]], U8)
+            quantize(zc, zs, interleave(nc.vector.tensor_copy, "z_woven", z_planes[c][:]))
+            for nb in range(N // P):
+                acc = bank("acc_out")[:, 0 : widths[c]]
+                nc.tensor.matmul_mx(
+                    out=acc,
+                    lhsT=w3c[:, P * nb : P * (nb + 1)].bitcast(FP8X4),
+                    lhsT_scale=w3s[:, P * nb : P * (nb + 1)],
+                    rhs=zc[:].bitcast(FP8X4),
+                    rhs_scale=zs[:],
+                    start=True,
+                    stop=True,
+                )
+                dst = staged[nb // 2]
+                if nb == 3:
+                    nc.vector.tensor_copy(dst[:, nb % 2, cols], acc)
+                else:
+                    nc.scalar.copy(dst[:, nb % 2, cols], acc)
+                if nb % 2 == 1:
+                    nc.sync.dma_start(out_rows[:, nb - 1 : nb + 1, cols], dst[:, :, cols])

@@ -23,6 +23,16 @@ PASS = P * PACK
 BANK = 512
 QUADS = 4
 
+AT_TAB2 = 0
+AT_TAB = 32
+AT_W1 = 64
+AT_BLEND0 = 80
+AT_W2 = 96
+AT_V2 = 104
+AT_WG2_1 = 112
+AT_H = 116
+AT_WG2_0 = 132
+
 
 def tile_list_terrain_weave_kernel(
     tc, tab_words, tab_scales, tab2_words, tab2_scales, offs, offs2, offs3, offs4, w1, gain, blend,
@@ -32,6 +42,7 @@ def tile_list_terrain_weave_kernel(
     with ExitStack() as ctx:
         lists = ctx.enter_context(tc.tile_pool(name="lists", bufs=1))
         sb = ctx.enter_context(tc.tile_pool(name="sb", bufs=1))
+        reuse = ctx.enter_context(tc.tile_pool(name="reuse", bufs=1))
         psum = ctx.enter_context(tc.psum_pool(name="psum", bufs=8))
 
         def held(name, shape, dtype):
@@ -39,6 +50,9 @@ def tile_list_terrain_weave_kernel(
 
         def shared(tag, bufs, name, shape, dtype):
             return sb.tile(shape, dtype, name=name, tag=tag, bufs=bufs, align_bytes=64)
+
+        def placed(name, kib, shape, dtype):
+            return reuse.tile(shape, dtype, name=name, align_bytes=64, offset=kib * 1024)
 
         def bank(name):
             return psum.tile([P, BANK], F32, name=name, tag="bank")
@@ -49,28 +63,37 @@ def tile_list_terrain_weave_kernel(
             return dst
 
         def zeroed(name, shape):
-            dst = held(name, shape, U8)
+            dst = shared(name, 1, name, shape, U8)
             nc.vector.memset(dst[:].bitcast(I32), 0)
             return dst
 
-        def load_table_scales(dst, src):
-            for q in range(QUADS):
-                nc.gpsimd.dma_start(dst[32 * q : 32 * q + 8, :].bitcast(I32), src[:, 4 * q : 4 * q + 4, :].bitcast(I32))
+        def load_table_scales(name, src):
+            dst = shared(name, 1, name, [P, T], U8)
+            nc.sync.dma_start(dst[0:32, :].bitcast(I32), src.bitcast(I32).rearrange("a q t -> q a t"))
+            nc.vector.memset(dst[32:64, :].bitcast(I32), 0)
+            nc.vector.memset(dst[64:P, :].bitcast(I32), 0)
+            return dst
 
-        def load_table_words(name, src, a):
-            dst = shared("table", 2, name, [P, T], U32)
+        def spread_scales(queue, dst, src):
+            for q in range(QUADS):
+                queue.dma_start(
+                    dst[32 * q : 32 * q + 4, :].bitcast(I32).rearrange("r (a c) -> r a c", a=2),
+                    src[8 * q : 8 * q + 8, :].bitcast(I32),
+                )
+
+        def load_table_words(name, src, a, at):
+            dst = placed(name, at + 16 * a, [P, T], U32)
             nc.sync.dma_start(dst[:].bitcast(I32), src[a].rearrange("p t i -> p (t i)").bitcast(I32))
             return dst
 
-        def load_factor(name, src, u):
-            dst = held(name, [P, S], F32)
-            rows = src.rearrange("(q t) m -> t q m", t=PACK)[u]
+        def load_factor(dst, src, u, count):
+            rows = src.rearrange("(q t) m -> q (t m)", t=PACK)[:, S * u : S * (u + count)]
             for q in (0, 2, 1, 3):
                 nc.sync.dma_start(dst[32 * q : 32 * q + 32, :], rows)
             return dst
 
-        def interleave(engine_copy, name, planes):
-            dst = shared("woven", 3, name, [P, planes.shape[2] * PACK], BF16)
+        def interleave(engine_copy, name, at, planes):
+            dst = placed(name, at, [P, planes.shape[2] * PACK], BF16)
             engine_copy(
                 dst[:].rearrange("p (c i t) -> p c t i", i=4, t=PACK),
                 planes.rearrange("p t (c i) -> p c t i", i=4),
@@ -80,44 +103,44 @@ def tile_list_terrain_weave_kernel(
         def quantize(codes, scales, woven):
             nc.vector.quantize_mx(out=codes[:].bitcast(FP8X4), scales=scales[:], in_=woven[:])
 
-        sc2 = zeroed("sc2", [P, T])
         w2s_raw = zeroed("w2s_raw", [P, 2 * H])
-        v2_scale1 = zeroed("v2_scale1", [P, S])
-        sc1 = zeroed("sc1", [P, T])
-        w3s = zeroed("w3s", [P, N])
-        gain_rows = held("gain_rows", [P, P], F32)
-        nc.vector.memset(gain_rows[:], 0.0)
-        load_table_scales(sc2, tab2_scales)
+        list2 = load_list("list2", offs2)
+        sc2 = load_table_scales("sc2", tab2_scales)
+        tab2_0 = load_table_words("tab2_0", tab2_words, 0, AT_TAB2)
         for q in range(QUADS):
-            nc.gpsimd.dma_start(
+            nc.sync.dma_start(
                 w2s_raw[32 * q : 32 * q + 4, :].bitcast(I32).rearrange("r (a c) -> r a c", a=2),
                 w2_scales[:, 4 * q : 4 * q + 4, :].bitcast(I32).rearrange("a r c -> r a c"),
             )
-        load_table_scales(sc1, tab_scales)
+        w2_raw = held("w2_raw", [P, 2, 2 * H], U8)
+        nc.sync.dma_start(w2_raw[:].bitcast(I32), w2_words.bitcast(I32).rearrange("a p c -> p a c"))
+        tab2_1 = load_table_words("tab2_1", tab2_words, 1, AT_TAB2)
+
+        v2_scale = zeroed("v2_scale", [P, 2 * S])
+        v2_scale_picked = held("v2_scale_picked", [P, S], U8)
+        nc.vector.tensor_copy(v2_scale_picked[:], sc2[:].indirect(list2[:]))
+        list1 = load_list("list1", offs)
+        sc1 = load_table_scales("sc1", tab_scales)
+        w1_raw = placed("w1_raw", AT_W1, [P, 2, PACK, H], F32)
+        w1_rows = w1.rearrange("(a p j) c -> a p j c", a=2, j=PACK)
+        spread_scales(nc.gpsimd, v2_scale, v2_scale_picked)
+        list4 = load_list("list4", offs4)
+        wg2_t = {0: load_factor(placed("wg2_0", AT_WG2_0, [P, S], F32), wg2, 0, 1)}
+        v_scale = zeroed("v_scale", [P, 2 * S])
+        w3s = zeroed("w3s", [P, N])
+        gain_rows = held("gain_rows", [P, P], F32)
+        nc.vector.memset(gain_rows[:], 0.0)
         ident = held("ident", [P, P], F32)
         make_identity(nc, ident[:])
 
-        list2 = load_list("list2", offs2)
-        tab2_0 = load_table_words("tab2_0", tab2_words, 0)
-        w2_raw = held("w2_raw", [P, 2, 2 * H], U8)
-        nc.sync.dma_start(w2_raw[:].bitcast(I32), w2_words.bitcast(I32).rearrange("a p c -> p a c"))
-        tab2_1 = load_table_words("tab2_1", tab2_words, 1)
-        list4 = load_list("list4", offs4)
-        wg2_t = {0: load_factor("wg2_0", wg2, 0)}
-        list1 = load_list("list1", offs)
-
-        v2_scale0 = held("v2_scale0", [P, S], U8)
-        nc.vector.tensor_copy(v2_scale0[:], sc2[:].indirect(list2[:]))
-        nc.scalar.dma_start(v2_scale1[0:112, :].bitcast(I32), v2_scale0[4:116, :].bitcast(I32))
-        v2_scale = [v2_scale0, v2_scale1]
-        v2 = [shared("picked", 5, "v2_%d" % a, [P, S], U32) for a in range(2)]
+        v2 = [placed("v2_%d" % a, AT_V2 + 4 * a, [P, S], U32) for a in range(2)]
         nc.vector.tensor_copy(v2[0][:], tab2_0[:].indirect(list2[:]))
-        w2c = held("w2c", [P, 2, 2 * H], U8)
+        w2c = placed("w2c", AT_W2, [P, 2, 2 * H], U8)
         nc.vector.tensor_copy(
             w2c[:].bitcast(U16).rearrange("p a (u m) -> p a u m", u=PACK),
             w2_raw[:].bitcast(U16).rearrange("p a (m u) -> p a u m", u=PACK),
         )
-        w2s = held("w2s", [P, 2 * H], U8)
+        w2s = placed("w2s", AT_W2 + 2, [P, 2 * H], U8)
         nc.vector.tensor_copy(
             w2s[:].rearrange("p (a u m) -> p a u m", a=2, u=PACK),
             w2s_raw[:].rearrange("p (a m u) -> p a u m", a=2, u=PACK),
@@ -127,96 +150,106 @@ def tile_list_terrain_weave_kernel(
                 v2[1][:, BANK * half : BANK * (half + 1)], tab2_1[:].indirect(list2[:, 32 * half : 32 * (half + 1)])
             )
 
-        pages = [held("page%d" % u, [P, T2], F32) for u in range(PACK)]
-
-        def plain_rows(u):
-            h = shared("h", 5, "h2_%d" % u, [P, S], F32)
-            for half in range(2):
-                cols = slice(BANK * half, BANK * (half + 1))
-                acc = bank("acc_h2")
-                for a in range(2):
-                    nc.tensor.matmul_mx(
-                        out=acc[:],
-                        lhsT=w2c[:, a, 256 * u : 256 * (u + 1)].bitcast(FP4X4),
-                        lhsT_scale=w2s[:, H * a + P * u : H * a + P * (u + 1)],
-                        rhs=v2[a][:, cols].bitcast(FP8X4),
-                        rhs_scale=v2_scale[a][:, cols],
-                        start=(a == 0),
-                        stop=(a == 1),
-                    )
-                nc.scalar.activation(h[:, cols], acc[:], ACT.Abs)
-            return h
-
-        def place(u, h, factor, where, pieces):
-            width = S // pieces
-            for i in range(pieces):
-                cols = slice(width * i, width * (i + 1))
-                nc.vector.tensor_tensor(
-                    pages[u][:].indirect(where[:, width // 16 * i : width // 16 * (i + 1)]), h[:, cols], factor[:, cols], MULT
-                )
-
-        h2 = [plain_rows(u) for u in range(PACK)]
-        place(0, h2[0], wg2_t[0], list4, 2)
-
         v_scale_picked = held("v_scale_picked", [P, S], U8)
         nc.vector.tensor_copy(v_scale_picked[:], sc1[:].indirect(list1[:]))
-        v_scale = held("v_scale", [P, S], U8)
+        v_scale_sorted = held("v_scale_sorted", [P, S], U8)
         nc.vector.tensor_copy(
-            v_scale[:].bitcast(I32).rearrange("p (t q w) -> p t q w", t=PACK, w=2),
+            v_scale_sorted[:].bitcast(I32).rearrange("p (t q w) -> p t q w", t=PACK, w=2),
             v_scale_picked[:].bitcast(I32).rearrange("p (q t w) -> p t q w", t=PACK, w=2),
         )
 
-        w1_raw = shared("raw", 2, "w1_raw", [P, 2, PACK, H], F32)
+        spread_scales(nc.gpsimd, v_scale, v_scale_sorted)
+
+        page_at = [AT_TAB2, AT_TAB2 + 8, AT_W2, AT_V2]
+        pages = [placed("page%d" % u, page_at[u], [P, T2], F32) for u in range(PACK)]
+
+        def plain_product(u, half):
+            cols = slice(BANK * half, BANK * (half + 1))
+            acc = bank("acc_h2")
+            for a in range(2):
+                nc.tensor.matmul_mx(
+                    out=acc[:],
+                    lhsT=w2c[:, a, 256 * u : 256 * (u + 1)].bitcast(FP4X4),
+                    lhsT_scale=w2s[:, H * a + P * u : H * a + P * (u + 1)],
+                    rhs=v2[a][:, cols].bitcast(FP8X4),
+                    rhs_scale=v2_scale[:, S * a + cols.start : S * a + cols.stop],
+                    start=(a == 0),
+                    stop=(a == 1),
+                )
+            return acc
+
+        def place(u, h, factor, where, first, width):
+            nc.vector.tensor_tensor(
+                pages[u][:].indirect(where[:, first // 16 : (first + width) // 16]), h, factor[:, first : first + width], MULT
+            )
+
+        h2 = []
+        for u in range(PACK):
+            h2.append(placed("h2_%d" % u, AT_H + 4 * u, [P, S if u < PACK - 1 else BANK], F32))
+            for half in range(2):
+                acc = plain_product(u, half)
+                if (u, half) == (PACK - 1, 1):
+                    last_acc = acc
+                else:
+                    nc.scalar.activation(h2[u][:, BANK * half : BANK * (half + 1)], acc[:], ACT.Abs)
+        for half in range(2):
+            place(0, h2[0][:, BANK * half : BANK * (half + 1)], wg2_t[0], list4, BANK * half, BANK)
+
         for a in range(2):
-            nc.sync.dma_start(w1_raw[:, a], w1[PASS * a : PASS * (a + 1), :].rearrange("(p j) c -> p j c", j=PACK))
-        wg2_t[1] = load_factor("wg2_1", wg2, 1)
+            nc.sync.dma_start(w1_raw[:, a], w1_rows[a])
+        wg2_t[1] = load_factor(placed("wg2_1", AT_WG2_1, [P, S], F32), wg2, 1, 1)
         for b in range(2):
             nc.sync.dma_start(
                 gain_rows[PACK * b : PACK * (b + 1), :].rearrange("t (q i) -> t q i", i=8),
                 gain[PASS * b : PASS * (b + 1)].rearrange("(q t i) -> t q i", t=PACK, i=8),
             )
-        w1c, w1s = [], []
-        for a in range(2):
-            w1c.append(held("w1c%d" % a, [P, H], U32))
-            w1s.append(held("w1s%d" % a, [P, H], U8))
-            quantize(w1c[a], w1s[a], interleave(nc.scalar.copy, "w1_woven", w1_raw[:, a]))
-        place(1, h2[1], wg2_t[1], list4, 1)
+        w1_woven = placed("w1_woven", AT_W2, [P, 2 * H * PACK], BF16)
+        nc.scalar.copy(
+            w1_woven[:].rearrange("p (a c i t) -> p a c t i", a=2, i=4, t=PACK),
+            w1_raw[:].rearrange("p a t (c i) -> p a c t i", i=4),
+        )
+        w1c = held("w1c", [P, 2 * H], U32)
+        w1s = held("w1s", [P, 2 * H], U8)
+        place(1, h2[1][:], wg2_t[1], list4, 0, S)
+        quantize(w1c, w1s, w1_woven)
 
         gain_turned = bank("gain_turned")
         nc.tensor.transpose(gain_turned[:, 0:P], gain_rows[:], ident[:])
         gains = held("gains", [P, 2 * PACK], F32)
         nc.scalar.copy(gains[:], gain_turned[:, 0 : 2 * PACK])
 
-        def load_blend(b):
-            raw = shared("raw", 2, "blend_raw%d" % b, [P, PACK, S], F32)
-            rows = blend[PASS * b : PASS * (b + 1), :].rearrange("(q t i) m -> t q i m", t=PACK, i=8)
+        def load_blend(b, half):
+            name = "blend_raw%d%d" % (b, half)
+            raw = held(name, [P, PACK, BANK], F32) if half else placed(name, AT_BLEND0 + 8 * b, [P, PACK, BANK], F32)
+            rows = blend[PASS * b : PASS * (b + 1), BANK * half : BANK * (half + 1)]
+            rows = rows.rearrange("(q t i) m -> t q i m", t=PACK, i=8)
             for t in range(PACK):
                 nc.sync.dma_start(raw[:, t, :], rows[t])
             return raw
 
         bc, bs = {}, {}
 
-        def quantize_blend(b, raw):
-            for half in range(2):
-                bc[b, half] = held("bc%d%d" % (b, half), [P, BANK], U32)
-                bs[b, half] = held("bs%d%d" % (b, half), [P, BANK], U8)
-                woven = interleave(nc.scalar.copy, "blend_woven", raw[:, :, BANK * half : BANK * (half + 1)])
-                quantize(bc[b, half], bs[b, half], woven)
+        def quantize_blend(b, half, raw, at):
+            bc[b, half] = held("bc%d%d" % (b, half), [P, BANK], U32)
+            bs[b, half] = held("bs%d%d" % (b, half), [P, BANK], U8)
+            quantize(bc[b, half], bs[b, half], interleave(nc.scalar.copy, "blend_woven%d%d" % (b, half), at, raw[:]))
 
-        quantize_blend(0, load_blend(0))
+        for b in range(2):
+            quantize_blend(b, 0, load_blend(b, 0), AT_V2 + 4 * b)
         v = []
         for a in range(2):
-            words = load_table_words("tab_%d" % a, tab_words, a)
-            v.append(shared("picked", 5, "v_%d" % a, [P, S], U32))
+            words = load_table_words("tab_%d" % a, tab_words, a, AT_TAB)
+            v.append(placed("v_%d" % a, (AT_WG2_1, AT_H + 4)[a], [P, S], U32))
             nc.vector.tensor_copy(
                 v[a][:].rearrange("p (t q i) -> p q t i", t=PACK, i=8), words[:].indirect(list1[:])
             )
-        wg2_t[2] = load_factor("wg2_2", wg2, 2)
-        place(2, h2[2], wg2_t[2], list4, 1)
+        wg2_rest = load_factor(held("wg2_rest", [P, 2 * S], F32), wg2, 2, 2)
+        wg2_t[2], wg2_t[3] = wg2_rest[:, 0:S], wg2_rest[:, S : 2 * S]
+        place(2, h2[2][:], wg2_t[2], list4, 0, S)
 
         ac, asc = [], []
         for b in range(2):
-            planes = held("a_planes%d" % b, [P, PACK, H], BF16)
+            planes = placed("a_planes%d" % b, AT_W1 + 4 * b, [P, PACK, H], BF16)
             for t in range(PACK):
                 cols = slice(2 * P * t + P * b, 2 * P * t + P * (b + 1))
                 acc = bank("acc_a")
@@ -224,9 +257,9 @@ def tile_list_terrain_weave_kernel(
                     nc.tensor.matmul_mx(
                         out=acc[:],
                         lhsT=v[a][:, cols].bitcast(FP8X4),
-                        lhsT_scale=v_scale[PACK * a : P, cols],
-                        rhs=w1c[a][:].bitcast(FP8X4),
-                        rhs_scale=w1s[a][:],
+                        lhsT_scale=v_scale[:, S * a + cols.start : S * a + cols.stop],
+                        rhs=w1c[:, H * a : H * (a + 1)].bitcast(FP8X4),
+                        rhs_scale=w1s[:, H * a : H * (a + 1)],
                         start=(a == 0),
                         stop=(a == 1),
                     )
@@ -236,56 +269,70 @@ def tile_list_terrain_weave_kernel(
                     ACT.Copy,
                     scale=gains[:, PACK * b + t : PACK * b + t + 1],
                 )
-            ac.append(held("ac%d" % b, [P, H], U32))
+            ac.append(placed("ac%d" % b, AT_H + 8 + 4 * b, [P, H], U32))
             asc.append(held("asc%d" % b, [P, H], U8))
-            quantize(ac[b], asc[b], interleave(nc.scalar.copy, "a_woven", planes[:]))
+            a_woven = interleave(nc.scalar.copy, "a_woven%d" % b, AT_TAB2 + 16 + 4 * b, planes[:])
+            if b == 1:
+                place(3, h2[3][:], wg2_t[3], list4, 0, BANK)
+            quantize(ac[b], asc[b], a_woven)
 
-        blend_raw1 = load_blend(1)
-        quantize_blend(1, blend_raw1)
+        h2_last = placed("h2_last", AT_W1 + 4, [P, BANK], F32)
+        nc.scalar.activation(h2_last[:], last_acc[:], ACT.Abs)
+        place(3, h2_last[:], wg2_t[3], list4, BANK, BANK)
+
         list3 = load_list("list3", offs3)
-        wg1_t = {0: load_factor("wg1_0", wg1, 0)}
-        wg2_t[3] = load_factor("wg2_3", wg2, 3)
-        place(3, h2[3], wg2_t[3], list4, 1)
+        wg1_low = load_factor(held("wg1_low", [P, 2 * S], F32), wg1, 0, 2)
+        blend_raw = [load_blend(b, 1) for b in (1, 0)]
+        wg1_high = load_factor(held("wg1_high", [P, 2 * S], F32), wg1, 2, 2)
+        wg1_t = [(wg1_low, wg1_high)[u // 2][:, S * (u % 2) : S * (u % 2 + 1)] for u in range(PACK)]
         biases = held("biases", [P, PACK], F32)
         nc.sync.dma_start(biases[:], bias.rearrange("(p t) -> p t", t=PACK))
-        for u in range(1, PACK):
-            wg1_t[u] = load_factor("wg1_%d" % u, wg1, u)
         w3c = held("w3c", [P, N], U32)
         nc.sync.dma_start(w3c[:].bitcast(I32), w3_words[0].rearrange("p c i -> p (c i)").bitcast(I32))
         for q in range(QUADS):
             nc.sync.dma_start(w3s[32 * q : 32 * q + 4, :].bitcast(I32), w3_scales[0, 4 * q : 4 * q + 4, :].bitcast(I32))
 
-        widths = [BANK // 2, BANK // 2, BANK, BANK, BANK]
+        widths = [BANK // 2, BANK // 2, BANK, BANK, BANK // 2, BANK // 2]
+        first_on_vector = [4, 4, 3, 3, 3, 2]
         chunks = [slice(sum(widths[:c]), sum(widths[: c + 1])) for c in range(len(widths))]
-        z_planes = [shared("picked", 5, "z_planes%d" % c, [P, PACK, w], BF16) for c, w in enumerate(widths)]
-        h1 = []
+        z_planes = [
+            placed("z_planes%d" % c, AT_BLEND0 + cols.start * PACK * 2 // 1024, [P, PACK, widths[c]], BF16)
+            for c, cols in enumerate(chunks)
+        ]
+        h1_at = [AT_H, AT_H + 4, AT_WG2_1, AT_WG2_0]
+
+        def blended(u, half):
+            acc = bank("acc_h1")
+            for b in range(2):
+                nc.tensor.matmul_mx(
+                    out=acc[:],
+                    lhsT=ac[b][:, P * u : P * (u + 1)].bitcast(FP8X4),
+                    lhsT_scale=asc[b][:, P * u : P * (u + 1)],
+                    rhs=bc[b, half][:].bitcast(FP8X4),
+                    rhs_scale=bs[b, half][:],
+                    start=(b == 0),
+                    stop=(b == 1),
+                )
+            h = placed("h1_%d%d" % (u, half), h1_at[u] + 2 * half, [P, BANK], F32)
+            nc.scalar.copy(h[:], acc[:])
+            return h
+
         for u in range(PACK):
-            h = shared("h", 5, "h1_%d" % u, [P, S], F32)
-            h1.append(h)
-            for half in range(2):
-                acc = bank("acc_h1")
-                for b in range(2):
-                    nc.tensor.matmul_mx(
-                        out=acc[:],
-                        lhsT=ac[b][:, P * u : P * (u + 1)].bitcast(FP8X4),
-                        lhsT_scale=asc[b][:, P * u : P * (u + 1)],
-                        rhs=bc[b, half][:].bitcast(FP8X4),
-                        rhs_scale=bs[b, half][:],
-                        start=(b == 0),
-                        stop=(b == 1),
-                    )
-                nc.scalar.copy(h[:, BANK * half : BANK * (half + 1)], acc[:])
+            place(u, blended(u, 0)[:], wg1_t[u], list3, 0, BANK)
+            if u < 2:
+                quantize_blend(1 - u, 1, blend_raw[u], (AT_W1 + 6, AT_TAB2 + 20)[u])
+        h1 = [blended(u, 1) for u in range(PACK)]
         for u in range(PACK):
-            place(u, h1[u], wg1_t[u], list3, 2 if u == 0 else 1)
+            place(u, h1[u][:], wg1_t[u], list3, BANK, BANK)
             for c, cols in enumerate(chunks):
                 nc.scalar.activation(z_planes[c][:, u, :], pages[u][:, cols], ACT.Relu, bias=biases[:, u : u + 1])
 
-        staged = [shared("table", 2, "staged%d" % g, [P, 2, T2], F32) for g in range(2)]
+        staged = [placed("staged%d" % g, AT_TAB + 16 * g, [P, 2, T2], F32) for g in range(2)]
         out_rows = out.rearrange("(nb p) t -> p nb t", p=P)
         for c, cols in enumerate(chunks):
             zc = shared("zc", 2, "zc", [P, widths[c]], U32)
             zs = shared("zs", 2, "zs", [P, widths[c]], U8)
-            quantize(zc, zs, interleave(nc.vector.tensor_copy, "z_woven", z_planes[c][:]))
+            quantize(zc, zs, interleave(nc.vector.tensor_copy, "z_woven%d" % c, AT_TAB2 + 16 + cols.start * PACK * 2 // 1024, z_planes[c][:]))
             for nb in range(N // P):
                 acc = bank("acc_out")[:, 0 : widths[c]]
                 nc.tensor.matmul_mx(
@@ -298,7 +345,7 @@ def tile_list_terrain_weave_kernel(
                     stop=True,
                 )
                 dst = staged[nb // 2]
-                if nb == 3:
+                if nb >= first_on_vector[c]:
                     nc.vector.tensor_copy(dst[:, nb % 2, cols], acc)
                 else:
                     nc.scalar.copy(dst[:, nb % 2, cols], acc)

@@ -123,7 +123,7 @@ def tile_list_terrain_weave_kernel(
         sc1 = load_table_scales("sc1", tab_scales)
         w1_raw = placed("w1_raw", AT_W1, [P, 2, PACK, H], F32)
         w1_rows = w1.rearrange("(a p j) c -> a p j c", a=2, j=PACK)
-        spread_scales(nc.gpsimd, v2_scale, v2_scale_picked)
+        spread_scales(nc.sync, v2_scale, v2_scale_picked)
         list4 = load_list("list4", offs4)
         wg2_t = {0: load_factor(placed("wg2_0", AT_WG2_0, [P, S], F32), wg2, 0, 1)}
         v_scale = zeroed("v_scale", [P, 2 * S])
@@ -243,8 +243,8 @@ def tile_list_terrain_weave_kernel(
             nc.vector.tensor_copy(
                 v[a][:].rearrange("p (t q i) -> p q t i", t=PACK, i=8), words[:].indirect(list1[:])
             )
-        wg2_rest = load_factor(held("wg2_rest", [P, 2 * S], F32), wg2, 2, 2)
-        wg2_t[2], wg2_t[3] = wg2_rest[:, 0:S], wg2_rest[:, S : 2 * S]
+        for u in (2, 3):
+            wg2_t[u] = load_factor(held("wg2_%d" % u, [P, S], F32), wg2, u, 1)
         place(2, h2[2][:], wg2_t[2], list4, 0, S)
 
         ac, asc = [], []

@@ -32,6 +32,7 @@ AT_V2 = 104
 AT_WG2_1 = 112
 AT_H = 116
 AT_WG2_0 = 132
+AT_BC = 136
 
 
 def tile_list_terrain_weave_kernel(
@@ -180,7 +181,7 @@ def tile_list_terrain_weave_kernel(
 
         def place(u, h, factor, where, first, width):
             nc.vector.tensor_tensor(
-                pages[u][:].indirect(where[:, first // 16 : (first + width) // 16]), h, factor[:, first : first + width], MULT
+                pages[u][:].indirect(where[:, first // 16 : (first + width) // 16]), h, factor, MULT
             )
 
         h2 = []
@@ -193,7 +194,7 @@ def tile_list_terrain_weave_kernel(
                 else:
                     nc.scalar.activation(h2[u][:, BANK * half : BANK * (half + 1)], acc[:], ACT.Abs)
         for half in range(2):
-            place(0, h2[0][:, BANK * half : BANK * (half + 1)], wg2_t[0], list4, BANK * half, BANK)
+            place(0, h2[0][:, BANK * half : BANK * (half + 1)], wg2_t[0][:, BANK * half : BANK * (half + 1)], list4, BANK * half, BANK)
 
         for a in range(2):
             nc.sync.dma_start(w1_raw[:, a], w1_rows[a])
@@ -210,7 +211,7 @@ def tile_list_terrain_weave_kernel(
         )
         w1c = held("w1c", [P, 2 * H], U32)
         w1s = held("w1s", [P, 2 * H], U8)
-        place(1, h2[1][:], wg2_t[1], list4, 0, S)
+        place(1, h2[1][:], wg2_t[1][:], list4, 0, S)
         quantize(w1c, w1s, w1_woven)
 
         gain_turned = bank("gain_turned")
@@ -229,13 +230,13 @@ def tile_list_terrain_weave_kernel(
 
         bc, bs = {}, {}
 
-        def quantize_blend(b, half, raw, at):
-            bc[b, half] = held("bc%d%d" % (b, half), [P, BANK], U32)
+        def quantize_blend(b, half, raw, at, codes_at):
+            bc[b, half] = placed("bc%d%d" % (b, half), codes_at, [P, BANK], U32)
             bs[b, half] = held("bs%d%d" % (b, half), [P, BANK], U8)
             quantize(bc[b, half], bs[b, half], interleave(nc.scalar.copy, "blend_woven%d%d" % (b, half), at, raw[:]))
 
         for b in range(2):
-            quantize_blend(b, 0, load_blend(b, 0), AT_V2 + 4 * b)
+            quantize_blend(b, 0, load_blend(b, 0), AT_V2 + 4 * b, AT_BC + 2 + 2 * b)
         v = []
         for a in range(2):
             words = load_table_words("tab_%d" % a, tab_words, a, AT_TAB)
@@ -245,7 +246,7 @@ def tile_list_terrain_weave_kernel(
             )
         for u in (2, 3):
             wg2_t[u] = load_factor(held("wg2_%d" % u, [P, S], F32), wg2, u, 1)
-        place(2, h2[2][:], wg2_t[2], list4, 0, S)
+        place(2, h2[2][:], wg2_t[2][:], list4, 0, S)
 
         ac, asc = [], []
         for b in range(2):
@@ -273,18 +274,24 @@ def tile_list_terrain_weave_kernel(
             asc.append(held("asc%d" % b, [P, H], U8))
             a_woven = interleave(nc.scalar.copy, "a_woven%d" % b, AT_TAB2 + 16 + 4 * b, planes[:])
             if b == 1:
-                place(3, h2[3][:], wg2_t[3], list4, 0, BANK)
+                place(3, h2[3][:], wg2_t[3][:, 0:BANK], list4, 0, BANK)
             quantize(ac[b], asc[b], a_woven)
 
         h2_last = placed("h2_last", AT_W1 + 4, [P, BANK], F32)
         nc.scalar.activation(h2_last[:], last_acc[:], ACT.Abs)
-        place(3, h2_last[:], wg2_t[3], list4, BANK, BANK)
+        place(3, h2_last[:], wg2_t[3][:, BANK:S], list4, BANK, BANK)
 
         list3 = load_list("list3", offs3)
-        wg1_low = load_factor(held("wg1_low", [P, 2 * S], F32), wg1, 0, 2)
-        blend_raw = [load_blend(b, 1) for b in (1, 0)]
-        wg1_high = load_factor(held("wg1_high", [P, 2 * S], F32), wg1, 2, 2)
-        wg1_t = [(wg1_low, wg1_high)[u // 2][:, S * (u % 2) : S * (u % 2 + 1)] for u in range(PACK)]
+        def load_factor_half(half):
+            dst = held("wg1_%d" % half, [P, PACK, BANK], F32)
+            rows = wg1.rearrange("(q t) m -> q t m", t=PACK)[:, :, BANK * half : BANK * (half + 1)]
+            for q in (0, 2, 1, 3):
+                nc.sync.dma_start(dst[32 * q : 32 * q + 32], rows)
+            return dst
+
+        wg1_half = [load_factor_half(0)]
+        blend_raw = [load_blend(b, 1) for b in range(2)]
+        wg1_half.append(load_factor_half(1))
         biases = held("biases", [P, PACK], F32)
         nc.sync.dma_start(biases[:], bias.rearrange("(p t) -> p t", t=PACK))
         w3c = held("w3c", [P, N], U32)
@@ -317,13 +324,14 @@ def tile_list_terrain_weave_kernel(
             nc.scalar.copy(h[:], acc[:])
             return h
 
+        h1 = [blended(u, 0) for u in range(PACK)]
         for u in range(PACK):
-            place(u, blended(u, 0)[:], wg1_t[u], list3, 0, BANK)
-            if u < 2:
-                quantize_blend(1 - u, 1, blend_raw[u], (AT_W1 + 6, AT_TAB2 + 20)[u])
+            place(u, h1[u][:], wg1_half[0][:, u, :], list3, 0, BANK)
+            if u in (1, 2):
+                quantize_blend(u - 1, 1, blend_raw[u - 1], AT_BC + 4 * (u - 1), h1_at[u])
         h1 = [blended(u, 1) for u in range(PACK)]
         for u in range(PACK):
-            place(u, h1[u][:], wg1_t[u], list3, BANK, BANK)
+            place(u, h1[u][:], wg1_half[1][:, u, :], list3, BANK, BANK)
             for c, cols in enumerate(chunks):
                 nc.scalar.activation(z_planes[c][:, u, :], pages[u][:, cols], ACT.Relu, bias=biases[:, u : u + 1])
 

@@ -180,9 +180,8 @@ def tile_list_terrain_weave_kernel(
             return acc
 
         def place(u, h, factor, where, first, width):
-            nc.vector.tensor_tensor(
-                pages[u][:].indirect(where[:, first // 16 : (first + width) // 16]), h, factor, MULT
-            )
+            nc.vector.tensor_tensor(h, h, factor, MULT)
+            nc.vector.tensor_copy(pages[u][:].indirect(where[:, first // 16 : (first + width) // 16]), h)
 
         h2 = []
         for u in range(PACK):

@@ -24,15 +24,16 @@ BANK = 512
 QUADS = 4
 
 AT_TAB2 = 0
+AT_A_PLANES = 8
+AT_A_WOVEN = 16
+AT_H1 = 24
 AT_TAB = 32
 AT_W1 = 64
-AT_BLEND0 = 80
-AT_W2 = 96
-AT_V2 = 104
-AT_WG2_1 = 112
-AT_H = 116
-AT_WG2_0 = 132
-AT_BC = 136
+AT_BLEND = 80
+AT_WG2 = 112
+AT_H2 = (128, 132, 140, 136)
+AT_W1_WOVEN = 148
+AT_PAGE = (AT_TAB2, AT_TAB, AT_TAB + 16, AT_H2[2])
 
 
 def tile_list_terrain_weave_kernel(
@@ -44,35 +45,35 @@ def tile_list_terrain_weave_kernel(
         lists = ctx.enter_context(tc.tile_pool(name="lists", bufs=1))
         sb = ctx.enter_context(tc.tile_pool(name="sb", bufs=1))
         reuse = ctx.enter_context(tc.tile_pool(name="reuse", bufs=1))
-        psum = ctx.enter_context(tc.psum_pool(name="psum", bufs=8))
+        psum = ctx.enter_context(tc.psum_pool(name="psum", bufs=1))
 
         def held(name, shape, dtype):
             return sb.tile(shape, dtype, name=name, align_bytes=64)
 
-        def shared(tag, bufs, name, shape, dtype):
-            return sb.tile(shape, dtype, name=name, tag=tag, bufs=bufs, align_bytes=64)
+        def ring(tag, shape, dtype):
+            return sb.tile(shape, dtype, name=tag, tag=tag, bufs=2, align_bytes=64)
 
         def placed(name, kib, shape, dtype):
             return reuse.tile(shape, dtype, name=name, align_bytes=64, offset=kib * 1024)
 
-        def bank(name):
-            return psum.tile([P, BANK], F32, name=name, tag="bank")
+        def bank(name, index):
+            return psum.tile([P, BANK], F32, name=name, tag="bank%d" % index)
 
         def load_list(name, src):
             dst = lists.tile([P, S // 16], U16, name=name)
             nc.sync.dma_start(dst[:], src)
             return dst
 
-        def zeroed(name, shape):
-            dst = shared(name, 1, name, shape, U8)
-            nc.vector.memset(dst[:].bitcast(I32), 0)
+        def zeroed(engine, name, width):
+            dst = held(name, [P, width], U8)
+            engine.memset(dst[:].bitcast(I32), 0)
             return dst
 
-        def load_table_scales(name, src):
-            dst = shared(name, 1, name, [P, T], U8)
+        def load_table_scales(engine, name, src):
+            dst = held(name, [P, T], U8)
             nc.sync.dma_start(dst[0:32, :].bitcast(I32), src.bitcast(I32).rearrange("a q t -> q a t"))
-            nc.vector.memset(dst[32:64, :].bitcast(I32), 0)
-            nc.vector.memset(dst[64:P, :].bitcast(I32), 0)
+            engine.memset(dst[32:64, :].bitcast(I32), 0)
+            engine.memset(dst[64:P, :].bitcast(I32), 0)
             return dst
 
         def spread_scales(queue, dst, src):
@@ -87,61 +88,87 @@ def tile_list_terrain_weave_kernel(
             nc.sync.dma_start(dst[:].bitcast(I32), src[a].rearrange("p t i -> p (t i)").bitcast(I32))
             return dst
 
-        def load_factor(dst, src, u, count):
-            rows = src.rearrange("(q t) m -> q (t m)", t=PACK)[:, S * u : S * (u + count)]
+        def load_wg2(u):
+            dst = placed("wg2_%d" % u, AT_WG2 + 4 * u, [P, S], F32)
+            rows = wg2.rearrange("(q t) m -> q t m", t=PACK)[:, u, :]
             for q in (0, 2, 1, 3):
                 nc.sync.dma_start(dst[32 * q : 32 * q + 32, :], rows)
             return dst
 
-        def interleave(engine_copy, name, at, planes):
-            dst = placed(name, at, [P, planes.shape[2] * PACK], BF16)
-            engine_copy(
-                dst[:].rearrange("p (c i t) -> p c t i", i=4, t=PACK),
+        def load_wg1(half):
+            dst = held("wg1_%d" % half, [P, PACK, BANK], F32)
+            rows = wg1.rearrange("(q t) m -> q t m", t=PACK)[:, :, BANK * half : BANK * (half + 1)]
+            for q in (0, 2, 1, 3):
+                nc.sync.dma_start(dst[32 * q : 32 * q + 32], rows)
+            return dst
+
+        pieces = [slice(0, 256), slice(256, 512), slice(512, 1024)]
+
+        def blend_at(i, b):
+            return AT_BLEND + (2 * pieces[i].start + b * (pieces[i].stop - pieces[i].start)) * PACK * 4 // 1024
+
+        def load_blend(i):
+            raw = []
+            cols = pieces[i]
+            for b in range(2):
+                raw.append(placed("blend_raw%d%d" % (i, b), blend_at(i, b), [P, PACK, cols.stop - cols.start], F32))
+                rows = blend[PASS * b : PASS * (b + 1), cols]
+                rows = rows.rearrange("(q t i) m -> t q i m", t=PACK, i=8)
+                for t in range(PACK):
+                    nc.sync.dma_start(raw[b][:, t, :], rows[t])
+            return raw
+
+        def weave(dst, planes):
+            nc.scalar.copy(
+                dst.rearrange("p (c i t) -> p c t i", i=4, t=PACK),
                 planes.rearrange("p t (c i) -> p c t i", i=4),
             )
-            return dst
 
         def quantize(codes, scales, woven):
             nc.vector.quantize_mx(out=codes[:].bitcast(FP8X4), scales=scales[:], in_=woven[:])
 
-        w2s_raw = zeroed("w2s_raw", [P, 2 * H])
+        w2s_raw = zeroed(nc.vector, "w2s_raw", 2 * H)
         list2 = load_list("list2", offs2)
-        sc2 = load_table_scales("sc2", tab2_scales)
+        sc2 = load_table_scales(nc.vector, "sc2", tab2_scales)
+        list1 = load_list("list1", offs)
+        sc1 = load_table_scales(nc.gpsimd, "sc1", tab_scales)
         tab2_0 = load_table_words("tab2_0", tab2_words, 0, AT_TAB2)
+        w2_raw = held("w2_raw", [P, 2, 2 * H], U8)
+        nc.sync.dma_start(w2_raw[:].bitcast(I32), w2_words.bitcast(I32).rearrange("a p c -> p a c"))
         for q in range(QUADS):
             nc.sync.dma_start(
                 w2s_raw[32 * q : 32 * q + 4, :].bitcast(I32).rearrange("r (a c) -> r a c", a=2),
                 w2_scales[:, 4 * q : 4 * q + 4, :].bitcast(I32).rearrange("a r c -> r a c"),
             )
-        w2_raw = held("w2_raw", [P, 2, 2 * H], U8)
-        nc.sync.dma_start(w2_raw[:].bitcast(I32), w2_words.bitcast(I32).rearrange("a p c -> p a c"))
         tab2_1 = load_table_words("tab2_1", tab2_words, 1, AT_TAB2)
-
-        v2_scale = zeroed("v2_scale", [P, 2 * S])
-        v2_scale_picked = held("v2_scale_picked", [P, S], U8)
-        nc.vector.tensor_copy(v2_scale_picked[:], sc2[:].indirect(list2[:]))
-        list1 = load_list("list1", offs)
-        sc1 = load_table_scales("sc1", tab_scales)
-        w1_raw = placed("w1_raw", AT_W1, [P, 2, PACK, H], F32)
-        w1_rows = w1.rearrange("(a p j) c -> a p j c", a=2, j=PACK)
-        spread_scales(nc.sync, v2_scale, v2_scale_picked)
         list4 = load_list("list4", offs4)
-        wg2_t = {0: load_factor(placed("wg2_0", AT_WG2_0, [P, S], F32), wg2, 0, 1)}
-        v_scale = zeroed("v_scale", [P, 2 * S])
-        w3s = zeroed("w3s", [P, N])
+        v2_scale = zeroed(nc.vector, "v2_scale", 2 * S)
+        v_scale = zeroed(nc.gpsimd, "v_scale", 2 * S)
+        w3s = zeroed(nc.gpsimd, "w3s", N)
         gain_rows = held("gain_rows", [P, P], F32)
-        nc.vector.memset(gain_rows[:], 0.0)
+        nc.gpsimd.memset(gain_rows[:], 0.0)
         ident = held("ident", [P, P], F32)
         make_identity(nc, ident[:])
 
-        v2 = [placed("v2_%d" % a, AT_V2 + 4 * a, [P, S], U32) for a in range(2)]
+        v2_scale_picked = held("v2_scale_picked", [P, S], U8)
+        nc.vector.tensor_copy(v2_scale_picked[:], sc2[:].indirect(list2[:]))
+        spread_scales(nc.sync, v2_scale, v2_scale_picked)
+        v_scale_picked = held("v_scale_picked", [P, S], U8)
+        nc.vector.tensor_copy(v_scale_picked[:], sc1[:].indirect(list1[:]))
+        v_scale_sorted = held("v_scale_sorted", [P, S], U8)
+        nc.vector.tensor_copy(
+            v_scale_sorted[:].bitcast(I32).rearrange("p (t q w) -> p t q w", t=PACK, w=2),
+            v_scale_picked[:].bitcast(I32).rearrange("p (q t w) -> p t q w", t=PACK, w=2),
+        )
+
+        v2 = [held("v2_%d" % a, [P, S], U32) for a in range(2)]
         nc.vector.tensor_copy(v2[0][:], tab2_0[:].indirect(list2[:]))
-        w2c = placed("w2c", AT_W2, [P, 2, 2 * H], U8)
+        w2c = held("w2c", [P, 2, 2 * H], U8)
         nc.vector.tensor_copy(
             w2c[:].bitcast(U16).rearrange("p a (u m) -> p a u m", u=PACK),
             w2_raw[:].bitcast(U16).rearrange("p a (m u) -> p a u m", u=PACK),
         )
-        w2s = placed("w2s", AT_W2 + 2, [P, 2 * H], U8)
+        w2s = held("w2s", [P, 2 * H], U8)
         nc.vector.tensor_copy(
             w2s[:].rearrange("p (a u m) -> p a u m", a=2, u=PACK),
             w2s_raw[:].rearrange("p (a m u) -> p a u m", a=2, u=PACK),
@@ -151,108 +178,85 @@ def tile_list_terrain_weave_kernel(
                 v2[1][:, BANK * half : BANK * (half + 1)], tab2_1[:].indirect(list2[:, 32 * half : 32 * (half + 1)])
             )
 
-        v_scale_picked = held("v_scale_picked", [P, S], U8)
-        nc.vector.tensor_copy(v_scale_picked[:], sc1[:].indirect(list1[:]))
-        v_scale_sorted = held("v_scale_sorted", [P, S], U8)
-        nc.vector.tensor_copy(
-            v_scale_sorted[:].bitcast(I32).rearrange("p (t q w) -> p t q w", t=PACK, w=2),
-            v_scale_picked[:].bitcast(I32).rearrange("p (q t w) -> p t q w", t=PACK, w=2),
-        )
+        pages = [placed("page%d" % u, AT_PAGE[u], [P, T2], F32) for u in range(PACK)]
 
-        spread_scales(nc.gpsimd, v_scale, v_scale_sorted)
+        def place(u, h, factor, where, cols):
+            nc.vector.tensor_tensor(pages[u][:].indirect(where[:, cols.start // 16 : cols.stop // 16]), h, factor, MULT)
 
-        page_at = [AT_TAB2, AT_TAB2 + 8, AT_W2, AT_V2]
-        pages = [placed("page%d" % u, page_at[u], [P, T2], F32) for u in range(PACK)]
-
-        def plain_product(u, half):
-            cols = slice(BANK * half, BANK * (half + 1))
-            acc = bank("acc_h2")
-            for a in range(2):
-                nc.tensor.matmul_mx(
-                    out=acc[:],
-                    lhsT=w2c[:, a, 256 * u : 256 * (u + 1)].bitcast(FP4X4),
-                    lhsT_scale=w2s[:, H * a + P * u : H * a + P * (u + 1)],
-                    rhs=v2[a][:, cols].bitcast(FP8X4),
-                    rhs_scale=v2_scale[:, S * a + cols.start : S * a + cols.stop],
-                    start=(a == 0),
-                    stop=(a == 1),
-                )
-            return acc
-
-        def place(u, h, factor, where, first, width):
-            nc.vector.tensor_tensor(h, h, factor, MULT)
-            nc.vector.tensor_copy(pages[u][:].indirect(where[:, first // 16 : (first + width) // 16]), h)
-
-        h2 = []
+        HELD_BACK = 256
+        kept = slice(0, S - HELD_BACK)
+        late = slice(S - HELD_BACK, S)
+        h2 = [placed("h2_%d" % u, AT_H2[u], [P, S], F32) for u in range(PACK)]
         for u in range(PACK):
-            h2.append(placed("h2_%d" % u, AT_H + 4 * u, [P, S if u < PACK - 1 else BANK], F32))
             for half in range(2):
-                acc = plain_product(u, half)
+                cols = slice(BANK * half, BANK * (half + 1))
+                acc = bank("acc_h2", 2 * u + half)
+                for a in range(2):
+                    nc.tensor.matmul_mx(
+                        out=acc[:],
+                        lhsT=w2c[:, a, 256 * u : 256 * (u + 1)].bitcast(FP4X4),
+                        lhsT_scale=w2s[:, H * a + P * u : H * a + P * (u + 1)],
+                        rhs=v2[a][:, cols].bitcast(FP8X4),
+                        rhs_scale=v2_scale[:, S * a + cols.start : S * a + cols.stop],
+                        start=(a == 0),
+                        stop=(a == 1),
+                    )
                 if (u, half) == (PACK - 1, 1):
                     last_acc = acc
+                    nc.scalar.activation(h2[u][:, BANK : kept.stop], acc[:, 0 : kept.stop - BANK], ACT.Abs)
                 else:
-                    nc.scalar.activation(h2[u][:, BANK * half : BANK * (half + 1)], acc[:], ACT.Abs)
-        for half in range(2):
-            place(0, h2[0][:, BANK * half : BANK * (half + 1)], wg2_t[0][:, BANK * half : BANK * (half + 1)], list4, BANK * half, BANK)
+                    nc.scalar.activation(h2[u][:, cols], acc[:], ACT.Abs)
 
+        wg2_t = [load_wg2(0)]
+        for half in range(2):
+            cols = slice(BANK * half, BANK * (half + 1))
+            place(0, h2[0][:, cols], wg2_t[0][:, cols], list4, cols)
+
+        def gather_mountain(a):
+            words = load_table_words("tab_%d" % a, tab_words, a, AT_TAB)
+            picked = placed("v_%d" % a, (AT_H2[0], AT_W1_WOVEN)[a], [P, S], U32)
+            nc.vector.tensor_copy(
+                picked[:].rearrange("p (t q i) -> p q t i", t=PACK, i=8), words[:].indirect(list1[:])
+            )
+            return picked
+
+        v = [gather_mountain(0)]
+        wg2_t.append(load_wg2(1))
+        place(1, h2[1][:], wg2_t[1][:], list4, slice(0, S))
+
+        w1_raw = placed("w1_raw", AT_W1, [P, 2, PACK, H], F32)
+        w1_rows = w1.rearrange("(a p j) c -> a p j c", a=2, j=PACK)
+        w1_woven = placed("w1_woven", AT_W1_WOVEN, [P, 2 * PACK * H], BF16)
         for a in range(2):
             nc.sync.dma_start(w1_raw[:, a], w1_rows[a])
-        wg2_t[1] = load_factor(placed("wg2_1", AT_WG2_1, [P, S], F32), wg2, 1, 1)
+            weave(w1_woven[:, PACK * H * a : PACK * H * (a + 1)], w1_raw[:, a])
+        spread_scales(nc.sync, v_scale, v_scale_sorted)
+        w1c = placed("w1c", AT_H2[1], [P, 2 * H], U32)
+        w1s = held("w1s", [P, 2 * H], U8)
+        quantize(w1c, w1s, w1_woven)
+
         for b in range(2):
             nc.sync.dma_start(
                 gain_rows[PACK * b : PACK * (b + 1), :].rearrange("t (q i) -> t q i", i=8),
                 gain[PASS * b : PASS * (b + 1)].rearrange("(q t i) -> t q i", t=PACK, i=8),
             )
-        w1_woven = placed("w1_woven", AT_W2, [P, 2 * H * PACK], BF16)
-        nc.scalar.copy(
-            w1_woven[:].rearrange("p (a c i t) -> p a c t i", a=2, i=4, t=PACK),
-            w1_raw[:].rearrange("p a t (c i) -> p a c t i", i=4),
-        )
-        w1c = held("w1c", [P, 2 * H], U32)
-        w1s = held("w1s", [P, 2 * H], U8)
-        place(1, h2[1][:], wg2_t[1][:], list4, 0, S)
-        quantize(w1c, w1s, w1_woven)
-
-        gain_turned = bank("gain_turned")
+        gain_turned = bank("gain_turned", 0)
         nc.tensor.transpose(gain_turned[:, 0:P], gain_rows[:], ident[:])
         gains = held("gains", [P, 2 * PACK], F32)
         nc.scalar.copy(gains[:], gain_turned[:, 0 : 2 * PACK])
 
-        def load_blend(b, half):
-            name = "blend_raw%d%d" % (b, half)
-            raw = held(name, [P, PACK, BANK], F32) if half else placed(name, AT_BLEND0 + 8 * b, [P, PACK, BANK], F32)
-            rows = blend[PASS * b : PASS * (b + 1), BANK * half : BANK * (half + 1)]
-            rows = rows.rearrange("(q t i) m -> t q i m", t=PACK, i=8)
-            for t in range(PACK):
-                nc.sync.dma_start(raw[:, t, :], rows[t])
-            return raw
-
-        bc, bs = {}, {}
-
-        def quantize_blend(b, half, raw, at, codes_at):
-            bc[b, half] = placed("bc%d%d" % (b, half), codes_at, [P, BANK], U32)
-            bs[b, half] = held("bs%d%d" % (b, half), [P, BANK], U8)
-            quantize(bc[b, half], bs[b, half], interleave(nc.scalar.copy, "blend_woven%d%d" % (b, half), at, raw[:]))
-
-        for b in range(2):
-            quantize_blend(b, 0, load_blend(b, 0), AT_V2 + 4 * b, AT_BC + 2 + 2 * b)
-        v = []
-        for a in range(2):
-            words = load_table_words("tab_%d" % a, tab_words, a, AT_TAB)
-            v.append(placed("v_%d" % a, (AT_WG2_1, AT_H + 4)[a], [P, S], U32))
-            nc.vector.tensor_copy(
-                v[a][:].rearrange("p (t q i) -> p q t i", t=PACK, i=8), words[:].indirect(list1[:])
-            )
+        v.append(gather_mountain(1))
         for u in (2, 3):
-            wg2_t[u] = load_factor(held("wg2_%d" % u, [P, S], F32), wg2, u, 1)
-        place(2, h2[2][:], wg2_t[2][:], list4, 0, S)
+            wg2_t.append(load_wg2(u))
+        place(2, h2[2][:], wg2_t[2][:], list4, slice(0, S))
+        place(3, h2[3][:, kept], wg2_t[3][:, kept], list4, kept)
 
-        ac, asc = [], []
+        a_planes = placed("a_planes", AT_A_PLANES, [P, 2, PACK, H], BF16)
+        a_woven = placed("a_woven", AT_A_WOVEN, [P, 2 * PACK * H], BF16)
         for b in range(2):
-            planes = placed("a_planes%d" % b, AT_W1 + 4 * b, [P, PACK, H], BF16)
             for t in range(PACK):
                 cols = slice(2 * P * t + P * b, 2 * P * t + P * (b + 1))
-                acc = bank("acc_a")
+                acc = bank("acc_a", 1 + (PACK * b + t) % 6)
                 for a in range(2):
                     nc.tensor.matmul_mx(
                         out=acc[:],
@@ -264,33 +268,22 @@ def tile_list_terrain_weave_kernel(
                         stop=(a == 1),
                     )
                 nc.scalar.activation(
-                    planes[:, t, :].rearrange("p (u m) -> p u m", u=PACK),
+                    a_planes[:, b, t, :].rearrange("p (u m) -> p u m", u=PACK),
                     acc[:].rearrange("p (m u) -> p u m", u=PACK),
                     ACT.Copy,
                     scale=gains[:, PACK * b + t : PACK * b + t + 1],
                 )
-            ac.append(placed("ac%d" % b, AT_H + 8 + 4 * b, [P, H], U32))
-            asc.append(held("asc%d" % b, [P, H], U8))
-            a_woven = interleave(nc.scalar.copy, "a_woven%d" % b, AT_TAB2 + 16 + 4 * b, planes[:])
-            if b == 1:
-                place(3, h2[3][:], wg2_t[3][:, 0:BANK], list4, 0, BANK)
-            quantize(ac[b], asc[b], a_woven)
-
-        h2_last = placed("h2_last", AT_W1 + 4, [P, BANK], F32)
-        nc.scalar.activation(h2_last[:], last_acc[:], ACT.Abs)
-        place(3, h2_last[:], wg2_t[3][:, BANK:S], list4, BANK, BANK)
+        for b in range(2):
+            weave(a_woven[:, PACK * H * b : PACK * H * (b + 1)], a_planes[:, b])
+        ac = placed("ac", AT_H2[3], [P, 2 * H], U32)
+        asc = held("asc", [P, 2 * H], U8)
+        quantize(ac, asc, a_woven)
 
         list3 = load_list("list3", offs3)
-        def load_factor_half(half):
-            dst = held("wg1_%d" % half, [P, PACK, BANK], F32)
-            rows = wg1.rearrange("(q t) m -> q t m", t=PACK)[:, :, BANK * half : BANK * (half + 1)]
-            for q in (0, 2, 1, 3):
-                nc.sync.dma_start(dst[32 * q : 32 * q + 32], rows)
-            return dst
-
-        wg1_half = [load_factor_half(0)]
-        blend_raw = [load_blend(b, 1) for b in range(2)]
-        wg1_half.append(load_factor_half(1))
+        blend_raw = [load_blend(0), load_blend(1)]
+        wg1_t = [load_wg1(0)]
+        blend_raw.append(load_blend(2))
+        wg1_t.append(load_wg1(1))
         biases = held("biases", [P, PACK], F32)
         nc.sync.dma_start(biases[:], bias.rearrange("(p t) -> p t", t=PACK))
         w3c = held("w3c", [P, N], U32)
@@ -298,50 +291,87 @@ def tile_list_terrain_weave_kernel(
         for q in range(QUADS):
             nc.sync.dma_start(w3s[32 * q : 32 * q + 4, :].bitcast(I32), w3_scales[0, 4 * q : 4 * q + 4, :].bitcast(I32))
 
-        widths = [BANK // 2, BANK // 2, BANK, BANK, BANK // 2, BANK // 2]
-        first_on_vector = [4, 4, 3, 3, 3, 2]
-        chunks = [slice(sum(widths[:c]), sum(widths[: c + 1])) for c in range(len(widths))]
-        z_planes = [
-            placed("z_planes%d" % c, AT_BLEND0 + cols.start * PACK * 2 // 1024, [P, PACK, widths[c]], BF16)
-            for c, cols in enumerate(chunks)
-        ]
-        h1_at = [AT_H, AT_H + 4, AT_WG2_1, AT_WG2_0]
+        woven_at = [AT_A_PLANES, AT_A_WOVEN, AT_A_WOVEN]
+        bc, bs = [], []
 
-        def blended(u, half):
-            acc = bank("acc_h1")
+        def quantize_blend(i):
+            cols = pieces[i]
+            width = cols.stop - cols.start
+            woven = placed("blend_woven%d" % i, woven_at[i], [P, 2 * PACK * width], BF16)
+            for b in range(2):
+                weave(woven[:, PACK * width * b : PACK * width * (b + 1)], blend_raw[i][b][:])
+            if i == 0:
+                bc.append(placed("bc0", AT_A_WOVEN, [P, 2 * width], U32))
+            elif i == 1:
+                bc.append(held("bc1", [P, 2 * width], U32))
+            else:
+                bc.append(placed("bc2", AT_BLEND, [P, 2 * width], U32))
+            if i == 0:
+                bs.append(held("bs0", [P, 2 * width], U8))
+            else:
+                bs.append(placed("bs%d" % i, AT_H1 + 4 * (i - 1) + 2, [P, 2 * width], U8))
+            quantize(bc[i], bs[i], woven)
+
+        def blended_sum(i, u):
+            width = pieces[i].stop - pieces[i].start
+            acc = bank("acc_h1", PACK * (i % 2) + u)[:, 0:width]
             for b in range(2):
                 nc.tensor.matmul_mx(
-                    out=acc[:],
-                    lhsT=ac[b][:, P * u : P * (u + 1)].bitcast(FP8X4),
-                    lhsT_scale=asc[b][:, P * u : P * (u + 1)],
-                    rhs=bc[b, half][:].bitcast(FP8X4),
-                    rhs_scale=bs[b, half][:],
+                    out=acc,
+                    lhsT=ac[:, H * b + P * u : H * b + P * (u + 1)].bitcast(FP8X4),
+                    lhsT_scale=asc[:, H * b + P * u : H * b + P * (u + 1)],
+                    rhs=bc[i][:, width * b : width * (b + 1)].bitcast(FP8X4),
+                    rhs_scale=bs[i][:, width * b : width * (b + 1)],
                     start=(b == 0),
                     stop=(b == 1),
                 )
-            h = placed("h1_%d%d" % (u, half), h1_at[u] + 2 * half, [P, BANK], F32)
-            nc.scalar.copy(h[:], acc[:])
-            return h
+            return acc
 
-        h1 = [blended(u, 0) for u in range(PACK)]
-        for u in range(PACK):
-            place(u, h1[u][:], wg1_half[0][:, u, :], list3, 0, BANK)
-            if u in (1, 2):
-                quantize_blend(u - 1, 1, blend_raw[u - 1], AT_BC + 4 * (u - 1), h1_at[u])
-        h1 = [blended(u, 1) for u in range(PACK)]
-        for u in range(PACK):
-            place(u, h1[u][:], wg1_half[1][:, u, :], list3, BANK, BANK)
-            for c, cols in enumerate(chunks):
-                nc.scalar.activation(z_planes[c][:, u, :], pages[u][:, cols], ACT.Relu, bias=biases[:, u : u + 1])
+        def place_blended(i, u, acc, at):
+            cols = pieces[i]
+            h = placed("h1_%d%d" % (i, u), at, [P, cols.stop - cols.start], F32)
+            nc.scalar.copy(h[:], acc)
+            first = cols.start % BANK
+            place(u, h[:], wg1_t[cols.start // BANK][:, u, first : first + cols.stop - cols.start], list3, cols)
 
-        staged = [placed("staged%d" % g, AT_TAB + 16 * g, [P, 2, T2], F32) for g in range(2)]
+        quantize_blend(0)
+        h2_late = placed("h2_late", blend_at(0, 1), [P, HELD_BACK], F32)
+        nc.scalar.activation(h2_late[:], last_acc[:, BANK - HELD_BACK : BANK], ACT.Abs)
+        place(3, h2_late[:], wg2_t[3][:, late], list4, late)
+
+        z_pairs = placed("z_pairs", AT_BLEND, [P, 2 * T2 * 2], BF16)
+
+        def relu(u, cols):
+            dst = z_pairs[:].rearrange("p (h t e) -> p h t e", h=2, e=2)[:, u // 2, cols, u % 2]
+            nc.scalar.activation(dst, pages[u][:, cols], ACT.Relu, bias=biases[:, u : u + 1])
+
+        for i in range(len(pieces)):
+            sums = [blended_sum(i, u) for u in range(PACK)]
+            for u in range(PACK):
+                at = AT_H1 + 4 * (i % 2) + 2 * u
+                if i + 1 < len(pieces) and u >= 2:
+                    at = blend_at(i + 1, 1) + u - 2
+                if i + 1 < len(pieces) and u == 2:
+                    quantize_blend(i + 1)
+                place_blended(i, u, sums[u], at)
+        for u in range(PACK - 1):
+            relu(u, slice(0, T2))
+
+        widths = [BANK // 2, BANK // 2, BANK, BANK, BANK // 2, BANK // 2]
+        first_on_vector = [3, 3, 2, 2, 2, 2]
+        chunks = [slice(sum(widths[:c]), sum(widths[: c + 1])) for c in range(len(widths))]
+        staged = [placed("staged%d" % g, (AT_W1, AT_BLEND + 16)[g], [P, 2, T2], F32) for g in range(2)]
         out_rows = out.rearrange("(nb p) t -> p nb t", p=P)
+        pair_words = z_pairs[:].bitcast(F32).rearrange("p (h t) -> p t h", h=2)
         for c, cols in enumerate(chunks):
-            zc = shared("zc", 2, "zc", [P, widths[c]], U32)
-            zs = shared("zs", 2, "zs", [P, widths[c]], U8)
-            quantize(zc, zs, interleave(nc.vector.tensor_copy, "z_woven%d" % c, AT_TAB2 + 16 + cols.start * PACK * 2 // 1024, z_planes[c][:]))
+            relu(PACK - 1, cols)
+            z_woven = placed("z_woven%d" % c, AT_WG2 + cols.start * PACK * 2 // 1024, [P, PACK * widths[c]], BF16)
+            nc.vector.tensor_copy(z_woven[:].bitcast(F32).rearrange("p (t h) -> p t h", h=2), pair_words[:, cols, :])
+            zc = ring("zc", [P, widths[c]], U32)
+            zs = ring("zs", [P, widths[c]], U8)
+            quantize(zc, zs, z_woven)
             for nb in range(N // P):
-                acc = bank("acc_out")[:, 0 : widths[c]]
+                acc = bank("acc_out", PACK * (c % 2) + nb)[:, 0 : widths[c]]
                 nc.tensor.matmul_mx(
                     out=acc,
                     lhsT=w3c[:, P * nb : P * (nb + 1)].bitcast(FP8X4),

@@ -88,12 +88,23 @@ def tile_list_terrain_weave_kernel(
             nc.sync.dma_start(dst[:].bitcast(I32), src[a].rearrange("p t i -> p (t i)").bitcast(I32))
             return dst
 
-        def load_wg2(u):
-            dst = placed("wg2_%d" % u, AT_WG2 + 4 * u, [P, S], F32)
-            rows = wg2.rearrange("(q t) m -> q t m", t=PACK)[:, u, :]
-            for q in (0, 2, 1, 3):
-                nc.sync.dma_start(dst[32 * q : 32 * q + 32, :], rows)
-            return dst
+        def turn_wg2(half):
+            turned = bank("wg2_turned", 6 + half)
+            for c in range(PACK):
+                first = BANK * half + P * c
+                nc.tensor.transpose(turned[:, P * c : P * (c + 1)], wg2_rows[:, first : first + P], ident[:])
+            return turned
+
+        def deal_wg2(turned, u, half):
+            repeated = ring("wg2_repeated", [P, PACK, QUADS, 32], F32)
+            src = turned[:].rearrange("p (c q u) -> p c u q", c=PACK, u=PACK)[:, :, u, :]
+            nc.scalar.copy(repeated[:], src.unsqueeze(2).to_broadcast([P, PACK, QUADS, 32]))
+            back = bank("wg2_back", 4 + half)
+            for c in range(PACK):
+                nc.tensor.transpose(
+                    back[:, P * c : P * (c + 1)], repeated[:, c].rearrange("p g q -> p (g q)"), ident[:]
+                )
+            nc.scalar.copy(wg2_t[u][:, BANK * half : BANK * (half + 1)], back[:])
 
         def load_wg1(half):
             dst = held("wg1_%d" % half, [P, PACK, BANK], F32)
@@ -142,24 +153,27 @@ def tile_list_terrain_weave_kernel(
             )
         tab2_1 = load_table_words("tab2_1", tab2_words, 1, AT_TAB2)
         list4 = load_list("list4", offs4)
-        v2_scale = zeroed(nc.vector, "v2_scale", 2 * S)
+        ident = held("ident", [P, P], F32)
+        make_identity(nc, ident[:])
+        v2_scale = zeroed(nc.gpsimd, "v2_scale", 2 * S)
         v_scale = zeroed(nc.gpsimd, "v_scale", 2 * S)
         w3s = zeroed(nc.gpsimd, "w3s", N)
         gain_rows = held("gain_rows", [P, P], F32)
         nc.gpsimd.memset(gain_rows[:], 0.0)
-        ident = held("ident", [P, P], F32)
-        make_identity(nc, ident[:])
 
         v2_scale_picked = held("v2_scale_picked", [P, S], U8)
         nc.vector.tensor_copy(v2_scale_picked[:], sc2[:].indirect(list2[:]))
         spread_scales(nc.sync, v2_scale, v2_scale_picked)
-        v_scale_picked = held("v_scale_picked", [P, S], U8)
-        nc.vector.tensor_copy(v_scale_picked[:], sc1[:].indirect(list1[:]))
         v_scale_sorted = held("v_scale_sorted", [P, S], U8)
-        nc.vector.tensor_copy(
-            v_scale_sorted[:].bitcast(I32).rearrange("p (t q w) -> p t q w", t=PACK, w=2),
-            v_scale_picked[:].bitcast(I32).rearrange("p (q t w) -> p t q w", t=PACK, w=2),
-        )
+
+        def gather_mountain_scales(picked):
+            nc.vector.tensor_copy(picked[:], sc1[:].indirect(list1[:]))
+            nc.vector.tensor_copy(
+                v_scale_sorted[:].bitcast(I32).rearrange("p (t q w) -> p t q w", t=PACK, w=2),
+                picked[:].bitcast(I32).rearrange("p (q t w) -> p t q w", t=PACK, w=2),
+            )
+
+        gather_mountain_scales(held("v_scale_picked", [P, S], U8))
 
         v2 = [held("v2_%d" % a, [P, S], U32) for a in range(2)]
         nc.vector.tensor_copy(v2[0][:], tab2_0[:].indirect(list2[:]))
@@ -186,11 +200,17 @@ def tile_list_terrain_weave_kernel(
         HELD_BACK = 256
         kept = slice(0, S - HELD_BACK)
         late = slice(S - HELD_BACK, S)
+        wg2_t = [placed("wg2_%d" % u, AT_WG2 + 4 * u, [P, S], F32) for u in range(PACK)]
+        for q in (0, 2, 1, 3):
+            nc.sync.dma_start(wg2_t[0][32 * q : 32 * q + 32, :], wg2.rearrange("(q t) m -> q t m", t=PACK)[:, 0, :])
+        wg2_rows = held("wg2_rows", [P, S], F32)
+        nc.sync.dma_start(wg2_rows[:], wg2)
+        h2_banks = (0, 1, 2, 3, 0, 1, 2, 3)
         h2 = [placed("h2_%d" % u, AT_H2[u], [P, S], F32) for u in range(PACK)]
         for u in range(PACK):
             for half in range(2):
                 cols = slice(BANK * half, BANK * (half + 1))
-                acc = bank("acc_h2", 2 * u + half)
+                acc = bank("acc_h2", h2_banks[2 * u + half])
                 for a in range(2):
                     nc.tensor.matmul_mx(
                         out=acc[:],
@@ -206,8 +226,12 @@ def tile_list_terrain_weave_kernel(
                     nc.scalar.activation(h2[u][:, BANK : kept.stop], acc[:, 0 : kept.stop - BANK], ACT.Abs)
                 else:
                     nc.scalar.activation(h2[u][:, cols], acc[:], ACT.Abs)
+            if u == 0:
+                turned = [turn_wg2(half) for half in range(2)]
+            else:
+                for half in range(2):
+                    deal_wg2(turned[half], u, half)
 
-        wg2_t = [load_wg2(0)]
         for half in range(2):
             cols = slice(BANK * half, BANK * (half + 1))
             place(0, h2[0][:, cols], wg2_t[0][:, cols], list4, cols)
@@ -215,13 +239,15 @@ def tile_list_terrain_weave_kernel(
         def gather_mountain(a):
             words = load_table_words("tab_%d" % a, tab_words, a, AT_TAB)
             picked = placed("v_%d" % a, (AT_H2[0], AT_W1_WOVEN)[a], [P, S], U32)
-            nc.vector.tensor_copy(
-                picked[:].rearrange("p (t q i) -> p q t i", t=PACK, i=8), words[:].indirect(list1[:])
-            )
+            dst = picked[:].rearrange("p (t q i) -> p q t i", t=PACK, i=8)
+            if a == 0:
+                nc.vector.tensor_copy(dst, words[:].indirect(list1[:]))
+            else:
+                for b in range(2):
+                    nc.vector.tensor_copy(dst[:, 16 * b : 16 * (b + 1)], words[:].indirect(list1[:, 32 * b : 32 * (b + 1)]))
             return picked
 
         v = [gather_mountain(0)]
-        wg2_t.append(load_wg2(1))
         place(1, h2[1][:], wg2_t[1][:], list4, slice(0, S))
 
         w1_raw = placed("w1_raw", AT_W1, [P, 2, PACK, H], F32)
@@ -240,14 +266,12 @@ def tile_list_terrain_weave_kernel(
                 gain_rows[PACK * b : PACK * (b + 1), :].rearrange("t (q i) -> t q i", i=8),
                 gain[PASS * b : PASS * (b + 1)].rearrange("(q t i) -> t q i", t=PACK, i=8),
             )
-        gain_turned = bank("gain_turned", 0)
+        gain_turned = bank("gain_turned", 6)
         nc.tensor.transpose(gain_turned[:, 0:P], gain_rows[:], ident[:])
         gains = held("gains", [P, 2 * PACK], F32)
         nc.scalar.copy(gains[:], gain_turned[:, 0 : 2 * PACK])
 
         v.append(gather_mountain(1))
-        for u in (2, 3):
-            wg2_t.append(load_wg2(u))
         place(2, h2[2][:], wg2_t[2][:], list4, slice(0, S))
         place(3, h2[3][:, kept], wg2_t[3][:, kept], list4, kept)
 
@@ -256,7 +280,7 @@ def tile_list_terrain_weave_kernel(
         for b in range(2):
             for t in range(PACK):
                 cols = slice(2 * P * t + P * b, 2 * P * t + P * (b + 1))
-                acc = bank("acc_a", 1 + (PACK * b + t) % 6)
+                acc = bank("acc_a", (0, 1, 2, 4, 5, 6, 7, 0)[PACK * b + t])
                 for a in range(2):
                     nc.tensor.matmul_mx(
                         out=acc[:],
@@ -291,7 +315,7 @@ def tile_list_terrain_weave_kernel(
         for q in range(QUADS):
             nc.sync.dma_start(w3s[32 * q : 32 * q + 4, :].bitcast(I32), w3_scales[0, 4 * q : 4 * q + 4, :].bitcast(I32))
 
-        woven_at = [AT_A_PLANES, AT_A_WOVEN, AT_A_WOVEN]
+        woven_at = [AT_TAB + 8, AT_WG2 + 8, AT_WG2 + 8]
         bc, bs = [], []
 
         def quantize_blend(i):
@@ -301,7 +325,7 @@ def tile_list_terrain_weave_kernel(
             for b in range(2):
                 weave(woven[:, PACK * width * b : PACK * width * (b + 1)], blend_raw[i][b][:])
             if i == 0:
-                bc.append(placed("bc0", AT_A_WOVEN, [P, 2 * width], U32))
+                bc.append(placed("bc0", AT_WG2 + 8, [P, 2 * width], U32))
             elif i == 1:
                 bc.append(held("bc1", [P, 2 * width], U32))
             else:
@@ -314,7 +338,7 @@ def tile_list_terrain_weave_kernel(
 
         def blended_sum(i, u):
             width = pieces[i].stop - pieces[i].start
-            acc = bank("acc_h1", PACK * (i % 2) + u)[:, 0:width]
+            acc = bank("acc_h1", PACK * ((i + 1) % 2) + u)[:, 0:width]
             for b in range(2):
                 nc.tensor.matmul_mx(
                     out=acc,
@@ -335,7 +359,7 @@ def tile_list_terrain_weave_kernel(
             place(u, h[:], wg1_t[cols.start // BANK][:, u, first : first + cols.stop - cols.start], list3, cols)
 
         quantize_blend(0)
-        h2_late = placed("h2_late", blend_at(0, 1), [P, HELD_BACK], F32)
+        h2_late = placed("h2_late", AT_A_PLANES, [P, HELD_BACK], F32)
         nc.scalar.activation(h2_late[:], last_acc[:, BANK - HELD_BACK : BANK], ACT.Abs)
         place(3, h2_late[:], wg2_t[3][:, late], list4, late)
 

@@ -116,7 +116,7 @@ def tile_list_terrain_weave_kernel(
         pieces = [slice(0, 256), slice(256, 512), slice(512, 1024)]
 
         def blend_at(i, b):
-            return AT_BLEND + (2 * pieces[i].start + b * (pieces[i].stop - pieces[i].start)) * PACK * 4 // 1024
+            return AT_BLEND + (0, 24, 8)[i] + b * (pieces[i].stop - pieces[i].start) * PACK * 4 // 1024
 
         def load_blend(i):
             raw = []
@@ -304,9 +304,9 @@ def tile_list_terrain_weave_kernel(
         quantize(ac, asc, a_woven)
 
         list3 = load_list("list3", offs3)
-        blend_raw = [load_blend(0), load_blend(1)]
+        blend_raw = [load_blend(0)]
         wg1_t = [load_wg1(0)]
-        blend_raw.append(load_blend(2))
+        blend_raw.extend([load_blend(1), load_blend(2)])
         wg1_t.append(load_wg1(1))
         biases = held("biases", [P, PACK], F32)
         nc.sync.dma_start(biases[:], bias.rearrange("(p t) -> p t", t=PACK))
@@ -315,7 +315,8 @@ def tile_list_terrain_weave_kernel(
         for q in range(QUADS):
             nc.sync.dma_start(w3s[32 * q : 32 * q + 4, :].bitcast(I32), w3_scales[0, 4 * q : 4 * q + 4, :].bitcast(I32))
 
-        woven_at = [AT_TAB + 8, AT_WG2 + 8, AT_WG2 + 8]
+        woven_at = [AT_TAB + 8, AT_WG2 + 8, AT_WG2 - 1]
+        h1_banks = ((4, 5, 6, 7), (0, 1, 2, 3), (4, 5, 6, 7))
         bc, bs = [], []
 
         def quantize_blend(i):
@@ -338,7 +339,7 @@ def tile_list_terrain_weave_kernel(
 
         def blended_sum(i, u):
             width = pieces[i].stop - pieces[i].start
-            acc = bank("acc_h1", PACK * ((i + 1) % 2) + u)[:, 0:width]
+            acc = bank("acc_h1", h1_banks[i][u])[:, 0:width]
             for b in range(2):
                 nc.tensor.matmul_mx(
                     out=acc,
@@ -351,10 +352,11 @@ def tile_list_terrain_weave_kernel(
                 )
             return acc
 
-        def place_blended(i, u, acc, at):
-            cols = pieces[i]
-            h = placed("h1_%d%d" % (i, u), at, [P, cols.stop - cols.start], F32)
-            nc.scalar.copy(h[:], acc)
+        def place_blended(name, u, at, parts):
+            cols = slice(pieces[parts[0]].start, pieces[parts[-1]].stop)
+            h = placed(name, at, [P, cols.stop - cols.start], F32)
+            for i in parts:
+                nc.scalar.copy(h[:, pieces[i].start - cols.start : pieces[i].stop - cols.start], sums[i, u])
             first = cols.start % BANK
             place(u, h[:], wg1_t[cols.start // BANK][:, u, first : first + cols.stop - cols.start], list3, cols)
 
@@ -369,46 +371,64 @@ def tile_list_terrain_weave_kernel(
             dst = z_pairs[:].rearrange("p (h t e) -> p h t e", h=2, e=2)[:, u // 2, cols, u % 2]
             nc.scalar.activation(dst, pages[u][:, cols], ACT.Relu, bias=biases[:, u : u + 1])
 
+        sums = {}
+        last = len(pieces) - 1
         for i in range(len(pieces)):
-            sums = [blended_sum(i, u) for u in range(PACK)]
+            for u in range(PACK):
+                sums[i, u] = blended_sum(i, u)
             for u in range(PACK):
                 at = AT_H1 + 4 * (i % 2) + 2 * u
-                if i + 1 < len(pieces) and u >= 2:
+                if i < last and u >= 2:
                     at = blend_at(i + 1, 1) + u - 2
-                if i + 1 < len(pieces) and u == 2:
+                if i < last and u == 2:
                     quantize_blend(i + 1)
-                place_blended(i, u, sums[u], at)
+                place_blended("h1_%d%d" % (i, u), u, at, [i])
         for u in range(PACK - 1):
             relu(u, slice(0, T2))
 
-        widths = [BANK // 2, BANK // 2, BANK, BANK, BANK // 2, BANK // 2]
-        first_on_vector = [3, 3, 2, 2, 2, 2]
+        widths = [128, 128, 256, 512, 512, 512]
+        on_vector = [(0,), (), (), (1, 3), (1, 3), (1, 3)]
         chunks = [slice(sum(widths[:c]), sum(widths[: c + 1])) for c in range(len(widths))]
-        staged = [placed("staged%d" % g, (AT_W1, AT_BLEND + 16)[g], [P, 2, T2], F32) for g in range(2)]
         out_rows = out.rearrange("(nb p) t -> p nb t", p=P)
         pair_words = z_pairs[:].bitcast(F32).rearrange("p (h t) -> p t h", h=2)
-        for c, cols in enumerate(chunks):
-            relu(PACK - 1, cols)
-            z_woven = placed("z_woven%d" % c, AT_WG2 + cols.start * PACK * 2 // 1024, [P, PACK * widths[c]], BF16)
-            nc.vector.tensor_copy(z_woven[:].bitcast(F32).rearrange("p (t h) -> p t h", h=2), pair_words[:, cols, :])
-            zc = ring("zc", [P, widths[c]], U32)
-            zs = ring("zs", [P, widths[c]], U8)
-            quantize(zc, zs, z_woven)
-            for nb in range(N // P):
-                acc = bank("acc_out", PACK * (c % 2) + nb)[:, 0 : widths[c]]
-                nc.tensor.matmul_mx(
-                    out=acc,
-                    lhsT=w3c[:, P * nb : P * (nb + 1)].bitcast(FP8X4),
-                    lhsT_scale=w3s[:, P * nb : P * (nb + 1)],
-                    rhs=zc[:].bitcast(FP8X4),
-                    rhs_scale=zs[:],
-                    start=True,
-                    stop=True,
-                )
-                dst = staged[nb // 2]
-                if nb >= first_on_vector[c]:
-                    nc.vector.tensor_copy(dst[:, nb % 2, cols], acc)
-                else:
-                    nc.scalar.copy(dst[:, nb % 2, cols], acc)
-                if nb % 2 == 1:
-                    nc.sync.dma_start(out_rows[:, nb - 1 : nb + 1, cols], dst[:, :, cols])
+        z_woven, zc, zs = {}, {}, {}
+
+        def weave_z(c):
+            relu(PACK - 1, chunks[c])
+            z_woven[c] = placed("z_woven%d" % c, AT_W1 + chunks[c].start * PACK * 2 // 1024, [P, PACK * widths[c]], BF16)
+            nc.vector.tensor_copy(
+                z_woven[c][:].bitcast(F32).rearrange("p (t h) -> p t h", h=2), pair_words[:, chunks[c], :]
+            )
+
+        def quantize_z(c):
+            zc[c] = held("zc%d" % c, [P, widths[c]], U32)
+            zs[c] = held("zs%d" % c, [P, widths[c]], U8)
+            quantize(zc[c], zs[c], z_woven[c])
+
+        def features(c):
+            cols, width = chunks[c], widths[c]
+            staged = placed("staged%d" % c, AT_BLEND + 16 + cols.start * PACK * 4 // 1024, [P, PACK, width], F32)
+            together = BANK // width
+            for g in range(PACK // together):
+                acc = bank("acc_out", (cols.start * PACK // BANK + g) % 8)
+                blocks = slice(together * g, together * (g + 1))
+                for nb in range(blocks.start, blocks.stop):
+                    nc.tensor.matmul_mx(
+                        out=acc[:, width * (nb - blocks.start) : width * (nb - blocks.start + 1)],
+                        lhsT=w3c[:, P * nb : P * (nb + 1)].bitcast(FP8X4),
+                        lhsT_scale=w3s[:, P * nb : P * (nb + 1)],
+                        rhs=zc[c][:].bitcast(FP8X4),
+                        rhs_scale=zs[c][:],
+                        start=True,
+                        stop=True,
+                    )
+                copy = nc.vector.tensor_copy if g in on_vector[c] else nc.scalar.copy
+                copy(staged[:, blocks, :].rearrange("p b t -> p (b t)"), acc[:])
+                nc.sync.dma_start(out_rows[:, blocks, cols], staged[:, blocks, :])
+
+        for c in range(len(chunks) + 1):
+            if c < len(chunks):
+                weave_z(c)
+                quantize_z(c)
+            if c > 0:
+                features(c - 1)

@@ -194,8 +194,13 @@ def tile_list_terrain_weave_kernel(
 
         pages = [placed("page%d" % u, AT_PAGE[u], [P, T2], F32) for u in range(PACK)]
 
-        def place(u, h, factor, where, cols):
-            nc.vector.tensor_tensor(pages[u][:].indirect(where[:, cols.start // 16 : cols.stop // 16]), h, factor, MULT)
+        def place(u, h, factor, where, cols, apart=False):
+            window = pages[u][:].indirect(where[:, cols.start // 16 : cols.stop // 16])
+            if apart:
+                nc.gpsimd.tensor_tensor(h, h, factor, MULT)
+                nc.vector.tensor_copy(window, h)
+            else:
+                nc.vector.tensor_tensor(window, h, factor, MULT)
 
         HELD_BACK = 256
         kept = slice(0, S - HELD_BACK)
@@ -248,7 +253,7 @@ def tile_list_terrain_weave_kernel(
             return picked
 
         v = [gather_mountain(0)]
-        place(1, h2[1][:], wg2_t[1][:], list4, slice(0, S))
+        place(1, h2[1][:], wg2_t[1][:], list4, slice(0, S), apart=True)
 
         w1_raw = placed("w1_raw", AT_W1, [P, 2, PACK, H], F32)
         w1_rows = w1.rearrange("(a p j) c -> a p j c", a=2, j=PACK)
@@ -272,8 +277,8 @@ def tile_list_terrain_weave_kernel(
         nc.scalar.copy(gains[:], gain_turned[:, 0 : 2 * PACK])
 
         v.append(gather_mountain(1))
-        place(2, h2[2][:], wg2_t[2][:], list4, slice(0, S))
-        place(3, h2[3][:, kept], wg2_t[3][:, kept], list4, kept)
+        place(2, h2[2][:], wg2_t[2][:], list4, slice(0, S), apart=True)
+        place(3, h2[3][:, kept], wg2_t[3][:, kept], list4, kept, apart=True)
 
         a_planes = placed("a_planes", AT_A_PLANES, [P, 2, PACK, H], BF16)
         a_woven = placed("a_woven", AT_A_WOVEN, [P, 2 * PACK * H], BF16)
@@ -358,7 +363,7 @@ def tile_list_terrain_weave_kernel(
             for i in parts:
                 nc.scalar.copy(h[:, pieces[i].start - cols.start : pieces[i].stop - cols.start], sums[i, u])
             first = cols.start % BANK
-            place(u, h[:], wg1_t[cols.start // BANK][:, u, first : first + cols.stop - cols.start], list3, cols)
+            place(u, h[:], wg1_t[cols.start // BANK][:, u, first : first + cols.stop - cols.start], list3, cols, apart=cols.stop == S and u > 0)
 
         quantize_blend(0)
         h2_late = placed("h2_late", AT_A_PLANES, [P, HELD_BACK], F32)

@@ -363,7 +363,7 @@ def tile_list_terrain_weave_kernel(
             for i in parts:
                 nc.scalar.copy(h[:, pieces[i].start - cols.start : pieces[i].stop - cols.start], sums[i, u])
             first = cols.start % BANK
-            place(u, h[:], wg1_t[cols.start // BANK][:, u, first : first + cols.stop - cols.start], list3, cols, apart=cols.stop == S and u > 0)
+            place(u, h[:], wg1_t[cols.start // BANK][:, u, first : first + cols.stop - cols.start], list3, cols)
 
         quantize_blend(0)
         h2_late = placed("h2_late", AT_A_PLANES, [P, HELD_BACK], F32)

@@ -25,7 +25,7 @@ QUADS = 4
 
 AT_TAB2 = 0
 AT_A_PLANES = 8
-AT_A_WOVEN = 16
+AT_A_WOVEN = 32
 AT_H1 = 24
 AT_TAB = 32
 AT_W1 = 64
@@ -33,7 +33,7 @@ AT_BLEND = 80
 AT_WG2 = 112
 AT_H2 = (128, 132, 140, 136)
 AT_W1_WOVEN = 148
-AT_PAGE = (AT_TAB2, AT_TAB, AT_TAB + 16, AT_H2[2])
+AT_PAGE = (AT_TAB2, AT_TAB2 + 16, AT_TAB + 16, AT_H2[2])
 
 
 def tile_list_terrain_weave_kernel(
@@ -194,56 +194,51 @@ def tile_list_terrain_weave_kernel(
 
         pages = [placed("page%d" % u, AT_PAGE[u], [P, T2], F32) for u in range(PACK)]
 
-        def place(u, h, factor, where, cols, apart=False):
-            window = pages[u][:].indirect(where[:, cols.start // 16 : cols.stop // 16])
-            if apart:
-                nc.gpsimd.tensor_tensor(h, h, factor, MULT)
-                nc.vector.tensor_copy(window, h)
-            else:
-                nc.vector.tensor_tensor(window, h, factor, MULT)
+        def place(u, h, factor, where, cols):
+            nc.vector.tensor_tensor(pages[u][:].indirect(where[:, cols.start // 16 : cols.stop // 16]), h, factor, MULT)
 
         HELD_BACK = 256
         kept = slice(0, S - HELD_BACK)
         late = slice(S - HELD_BACK, S)
         wg2_t = [placed("wg2_%d" % u, AT_WG2 + 4 * u, [P, S], F32) for u in range(PACK)]
-        for q in (0, 2, 1, 3):
-            nc.sync.dma_start(wg2_t[0][32 * q : 32 * q + 32, :], wg2.rearrange("(q t) m -> q t m", t=PACK)[:, 0, :])
-        wg2_rows = held("wg2_rows", [P, S], F32)
-        nc.sync.dma_start(wg2_rows[:], wg2)
-        h2_banks = (0, 1, 2, 3, 0, 1, 2, 3)
+        for u in range(2):
+            for q in (0, 2, 1, 3):
+                nc.sync.dma_start(wg2_t[u][32 * q : 32 * q + 32, :], wg2.rearrange("(q t) m -> q t m", t=PACK)[:, u, :])
         h2 = [placed("h2_%d" % u, AT_H2[u], [P, S], F32) for u in range(PACK)]
-        for u in range(PACK):
-            for half in range(2):
-                cols = slice(BANK * half, BANK * (half + 1))
-                acc = bank("acc_h2", h2_banks[2 * u + half])
+
+        def plain_sum(u, cols, width, at_bank):
+            acc = bank("acc_h2", at_bank)
+            for first in range(cols.start, cols.stop, width):
                 for a in range(2):
                     nc.tensor.matmul_mx(
-                        out=acc[:],
+                        out=acc[:, first - cols.start : first - cols.start + width],
                         lhsT=w2c[:, a, 256 * u : 256 * (u + 1)].bitcast(FP4X4),
                         lhsT_scale=w2s[:, H * a + P * u : H * a + P * (u + 1)],
-                        rhs=v2[a][:, cols].bitcast(FP8X4),
-                        rhs_scale=v2_scale[:, S * a + cols.start : S * a + cols.stop],
+                        rhs=v2[a][:, first : first + width].bitcast(FP8X4),
+                        rhs_scale=v2_scale[:, S * a + first : S * a + first + width],
                         start=(a == 0),
                         stop=(a == 1),
                     )
-                if (u, half) == (PACK - 1, 1):
-                    last_acc = acc
-                    nc.scalar.activation(h2[u][:, BANK : kept.stop], acc[:, 0 : kept.stop - BANK], ACT.Abs)
-                else:
-                    nc.scalar.activation(h2[u][:, cols], acc[:], ACT.Abs)
-            if u == 0:
-                turned = [turn_wg2(half) for half in range(2)]
-            else:
-                for half in range(2):
-                    deal_wg2(turned[half], u, half)
+            return acc
 
-        for half in range(2):
-            cols = slice(BANK * half, BANK * (half + 1))
+        FIRST = 256
+        for u in range(PACK):
+            parts = [(slice(0, BANK), BANK, 2 * u % PACK), (slice(BANK, S), BANK, (2 * u + 1) % PACK)]
+            if u == 0:
+                parts[0:1] = [(slice(0, FIRST), P, 0), (slice(FIRST, BANK), P, 3)]
+            for cols, width, at_bank in parts:
+                acc = plain_sum(u, cols, width, at_bank)
+                if (u, cols.stop) == (PACK - 1, S):
+                    last_acc = acc
+                    cols = slice(BANK, kept.stop)
+                nc.scalar.activation(h2[u][:, cols], acc[:, 0 : cols.stop - cols.start], ACT.Abs)
+
+        for cols in (slice(0, FIRST), slice(FIRST, BANK), slice(BANK, S)):
             place(0, h2[0][:, cols], wg2_t[0][:, cols], list4, cols)
 
         def gather_mountain(a):
             words = load_table_words("tab_%d" % a, tab_words, a, AT_TAB)
-            picked = placed("v_%d" % a, (AT_H2[0], AT_W1_WOVEN)[a], [P, S], U32)
+            picked = placed("v_%d" % a, (AT_H2[1], AT_W1_WOVEN)[a], [P, S], U32)
             dst = picked[:].rearrange("p (t q i) -> p q t i", t=PACK, i=8)
             if a == 0:
                 nc.vector.tensor_copy(dst, words[:].indirect(list1[:]))
@@ -252,8 +247,7 @@ def tile_list_terrain_weave_kernel(
                     nc.vector.tensor_copy(dst[:, 16 * b : 16 * (b + 1)], words[:].indirect(list1[:, 32 * b : 32 * (b + 1)]))
             return picked
 
-        v = [gather_mountain(0)]
-        place(1, h2[1][:], wg2_t[1][:], list4, slice(0, S), apart=True)
+        place(1, h2[1][:], wg2_t[1][:], list4, slice(0, S))
 
         w1_raw = placed("w1_raw", AT_W1, [P, 2, PACK, H], F32)
         w1_rows = w1.rearrange("(a p j) c -> a p j c", a=2, j=PACK)
@@ -261,11 +255,19 @@ def tile_list_terrain_weave_kernel(
         for a in range(2):
             nc.sync.dma_start(w1_raw[:, a], w1_rows[a])
             weave(w1_woven[:, PACK * H * a : PACK * H * (a + 1)], w1_raw[:, a])
-        spread_scales(nc.sync, v_scale, v_scale_sorted)
-        w1c = placed("w1c", AT_H2[1], [P, 2 * H], U32)
+        v = [gather_mountain(0)]
+        w1c = placed("w1c", AT_TAB + 12, [P, 2 * H], U32)
         w1s = held("w1s", [P, 2 * H], U8)
         quantize(w1c, w1s, w1_woven)
 
+        wg2_rows = held("wg2_rows", [P, S], F32)
+        nc.sync.dma_start(wg2_rows[:], wg2)
+        turned = [turn_wg2(half) for half in range(2)]
+        for u in (2, 3):
+            for half in range(2):
+                deal_wg2(turned[half], u, half)
+        v.append(gather_mountain(1))
+        spread_scales(nc.sync, v_scale, v_scale_sorted)
         for b in range(2):
             nc.sync.dma_start(
                 gain_rows[PACK * b : PACK * (b + 1), :].rearrange("t (q i) -> t q i", i=8),
@@ -276,9 +278,8 @@ def tile_list_terrain_weave_kernel(
         gains = held("gains", [P, 2 * PACK], F32)
         nc.scalar.copy(gains[:], gain_turned[:, 0 : 2 * PACK])
 
-        v.append(gather_mountain(1))
-        place(2, h2[2][:], wg2_t[2][:], list4, slice(0, S), apart=True)
-        place(3, h2[3][:, kept], wg2_t[3][:, kept], list4, kept, apart=True)
+        place(2, h2[2][:], wg2_t[2][:], list4, slice(0, S))
+        place(3, h2[3][:, kept], wg2_t[3][:, kept], list4, kept)
 
         a_planes = placed("a_planes", AT_A_PLANES, [P, 2, PACK, H], BF16)
         a_woven = placed("a_woven", AT_A_WOVEN, [P, 2 * PACK * H], BF16)
@@ -431,9 +432,12 @@ def tile_list_terrain_weave_kernel(
                 copy(staged[:, blocks, :].rearrange("p b t -> p (b t)"), acc[:])
                 nc.sync.dma_start(out_rows[:, blocks, cols], staged[:, blocks, :])
 
-        for c in range(len(chunks) + 1):
-            if c < len(chunks):
-                weave_z(c)
-                quantize_z(c)
-            if c > 0:
-                features(c - 1)
+        weave_z(0)
+        quantize_z(0)
+        weave_z(1)
+        for c in range(1, len(chunks)):
+            if c + 1 < len(chunks):
+                weave_z(c + 1)
+            quantize_z(c)
+            features(c - 1)
+        features(len(chunks) - 1)

@@ -183,7 +183,7 @@ def tile_list_terrain_weave_kernel(
             w2_raw[:].bitcast(U16).rearrange("p a (m u) -> p a u m", u=PACK),
         )
         w2s = held("w2s", [P, 2 * H], U8)
-        nc.vector.tensor_copy(
+        nc.gpsimd.tensor_copy(
             w2s[:].rearrange("p (a u m) -> p a u m", a=2, u=PACK),
             w2s_raw[:].rearrange("p (a m u) -> p a u m", a=2, u=PACK),
         )

@@ -16,24 +16,29 @@ FP8X4 = mybir.dt.float8_e4m3fn_x4
 FP4X4 = mybir.dt.float4_e2m1fn_x4
 ACT = mybir.ActivationFunctionType
 MULT = mybir.AluOpType.mult
+ADD = mybir.AluOpType.add
+MAX = mybir.AluOpType.max
 
 P = 128
 PACK = 4
 PASS = P * PACK
 BANK = 512
 QUADS = 4
+ROWS = 96
 
 AT_TAB2 = 0
-AT_A_PLANES = 8
-AT_A_WOVEN = 32
-AT_H1 = 24
 AT_TAB = 32
+AT_A_PLANES = 84
+AT_A_WOVEN = 40
+AT_H1 = 48
 AT_W1 = 64
 AT_BLEND = 80
 AT_WG2 = 112
-AT_H2 = (128, 132, 140, 136)
-AT_W1_WOVEN = 148
-AT_PAGE = (AT_TAB2, AT_TAB2 + 16, AT_TAB + 16, AT_H2[2])
+AT_H2 = 128
+AT_V = 144
+AT_W1_WOVEN = 152
+AT_BC = (160, 164, 152)
+AT_WG1 = 168
 
 
 def tile_list_terrain_weave_kernel(
@@ -50,11 +55,8 @@ def tile_list_terrain_weave_kernel(
         def held(name, shape, dtype):
             return sb.tile(shape, dtype, name=name, align_bytes=64)
 
-        def ring(tag, shape, dtype):
-            return sb.tile(shape, dtype, name=tag, tag=tag, bufs=2, align_bytes=64)
-
         def placed(name, kib, shape, dtype):
-            return reuse.tile(shape, dtype, name=name, align_bytes=64, offset=kib * 1024)
+            return reuse.tile(shape, dtype, name=name, align_bytes=64, offset=int(kib * 1024))
 
         def bank(name, index):
             return psum.tile([P, BANK], F32, name=name, tag="bank%d" % index)
@@ -70,17 +72,16 @@ def tile_list_terrain_weave_kernel(
             return dst
 
         def load_table_scales(engine, name, src):
-            dst = held(name, [P, T], U8)
-            nc.sync.dma_start(dst[0:32, :].bitcast(I32), src.bitcast(I32).rearrange("a q t -> q a t"))
-            engine.memset(dst[32:64, :].bitcast(I32), 0)
-            engine.memset(dst[64:P, :].bitcast(I32), 0)
+            dst = held(name, [P, src.shape[2]], U8)
+            nc.sync.dma_start(dst[ROWS:P, :].bitcast(I32), src.bitcast(I32).rearrange("a q t -> q a t"))
+            engine.memset(dst[0:ROWS, :].bitcast(I32), 0)
             return dst
 
         def spread_scales(queue, dst, src):
             for q in range(QUADS):
                 queue.dma_start(
                     dst[32 * q : 32 * q + 4, :].bitcast(I32).rearrange("r (a c) -> r a c", a=2),
-                    src[8 * q : 8 * q + 8, :].bitcast(I32),
+                    src[ROWS + 8 * q : ROWS + 8 * q + 8, :].bitcast(I32),
                 )
 
         def load_table_words(name, src, a, at):
@@ -88,35 +89,25 @@ def tile_list_terrain_weave_kernel(
             nc.sync.dma_start(dst[:].bitcast(I32), src[a].rearrange("p t i -> p (t i)").bitcast(I32))
             return dst
 
-        def turn_wg2(half):
-            turned = bank("wg2_turned", 6 + half)
-            for c in range(PACK):
-                first = BANK * half + P * c
-                nc.tensor.transpose(turned[:, P * c : P * (c + 1)], wg2_rows[:, first : first + P], ident[:])
-            return turned
+        wg2_t = [placed("wg2_%d" % u, AT_WG2 + 4 * u, [P, S], F32) for u in range(PACK)]
 
-        def deal_wg2(turned, u, half):
-            repeated = ring("wg2_repeated", [P, PACK, QUADS, 32], F32)
-            src = turned[:].rearrange("p (c q u) -> p c u q", c=PACK, u=PACK)[:, :, u, :]
-            nc.scalar.copy(repeated[:], src.unsqueeze(2).to_broadcast([P, PACK, QUADS, 32]))
-            back = bank("wg2_back", 4 + half)
-            for c in range(PACK):
-                nc.tensor.transpose(
-                    back[:, P * c : P * (c + 1)], repeated[:, c].rearrange("p g q -> p (g q)"), ident[:]
-                )
-            nc.scalar.copy(wg2_t[u][:, BANK * half : BANK * (half + 1)], back[:])
+        def load_wg2(u, quads):
+            rows = wg2.rearrange("(q t) m -> q t m", t=PACK)[:, u, :]
+            for q in quads:
+                nc.sync.dma_start(wg2_t[u][32 * q : 32 * q + 32, :], rows)
+
+        wg1_t = placed("wg1", AT_WG1, [P, PACK, S], F32)
 
         def load_wg1(half):
-            dst = held("wg1_%d" % half, [P, PACK, BANK], F32)
-            rows = wg1.rearrange("(q t) m -> q t m", t=PACK)[:, :, BANK * half : BANK * (half + 1)]
+            cols = slice(BANK * half, BANK * (half + 1))
+            rows = wg1.rearrange("(q t) m -> q t m", t=PACK)[:, :, cols]
             for q in (0, 2, 1, 3):
-                nc.sync.dma_start(dst[32 * q : 32 * q + 32], rows)
-            return dst
+                nc.sync.dma_start(wg1_t[32 * q : 32 * q + 32, :, cols], rows)
 
         pieces = [slice(0, 256), slice(256, 512), slice(512, 1024)]
 
         def blend_at(i, b):
-            return AT_BLEND + (0, 24, 8)[i] + b * (pieces[i].stop - pieces[i].start) * PACK * 4 // 1024
+            return AT_BLEND + ((4, 8), (0, 12), (16, 24))[i][b]
 
         def load_blend(i):
             raw = []
@@ -138,24 +129,20 @@ def tile_list_terrain_weave_kernel(
         def quantize(codes, scales, woven):
             nc.vector.quantize_mx(out=codes[:].bitcast(FP8X4), scales=scales[:], in_=woven[:])
 
-        w2s_raw = zeroed(nc.vector, "w2s_raw", 2 * H)
         list2 = load_list("list2", offs2)
         sc2 = load_table_scales(nc.vector, "sc2", tab2_scales)
+        w2s_raw = load_table_scales(nc.vector, "w2s_raw", w2_scales)
         list1 = load_list("list1", offs)
         sc1 = load_table_scales(nc.gpsimd, "sc1", tab_scales)
         tab2_0 = load_table_words("tab2_0", tab2_words, 0, AT_TAB2)
         w2_raw = held("w2_raw", [P, 2, 2 * H], U8)
         nc.sync.dma_start(w2_raw[:].bitcast(I32), w2_words.bitcast(I32).rearrange("a p c -> p a c"))
-        for q in range(QUADS):
-            nc.sync.dma_start(
-                w2s_raw[32 * q : 32 * q + 4, :].bitcast(I32).rearrange("r (a c) -> r a c", a=2),
-                w2_scales[:, 4 * q : 4 * q + 4, :].bitcast(I32).rearrange("a r c -> r a c"),
-            )
-        tab2_1 = load_table_words("tab2_1", tab2_words, 1, AT_TAB2)
         list4 = load_list("list4", offs4)
+        load_wg2(0, (0,))
+        tab2_1 = load_table_words("tab2_1", tab2_words, 1, AT_TAB2)
         ident = held("ident", [P, P], F32)
         make_identity(nc, ident[:])
-        v2_scale = zeroed(nc.gpsimd, "v2_scale", 2 * S)
+        plain_scale = zeroed(nc.gpsimd, "plain_scale", 2 * (S + H))
         v_scale = zeroed(nc.gpsimd, "v_scale", 2 * S)
         w3s = zeroed(nc.gpsimd, "w3s", N)
         gain_rows = held("gain_rows", [P, P], F32)
@@ -163,7 +150,13 @@ def tile_list_terrain_weave_kernel(
 
         v2_scale_picked = held("v2_scale_picked", [P, S], U8)
         nc.vector.tensor_copy(v2_scale_picked[:], sc2[:].indirect(list2[:]))
-        spread_scales(nc.sync, v2_scale, v2_scale_picked)
+        plain_rows = held("plain_rows", [P, S + H], U8)
+        nc.vector.tensor_copy(plain_rows[:, 0:S].bitcast(I32), v2_scale_picked[:].bitcast(I32))
+        nc.gpsimd.tensor_copy(
+            plain_rows[:, S:].rearrange("p (u m) -> p u m", u=PACK),
+            w2s_raw[:].rearrange("p (m u) -> p u m", u=PACK),
+        )
+        spread_scales(nc.sync, plain_scale, plain_rows)
         v_scale_sorted = held("v_scale_sorted", [P, S], U8)
 
         def gather_mountain_scales(picked):
@@ -175,24 +168,19 @@ def tile_list_terrain_weave_kernel(
 
         gather_mountain_scales(held("v_scale_picked", [P, S], U8))
 
-        v2 = [held("v2_%d" % a, [P, S], U32) for a in range(2)]
+        v2 = [placed("v2_%d" % a, AT_V + 4 * a, [P, S], U32) for a in range(2)]
         nc.vector.tensor_copy(v2[0][:], tab2_0[:].indirect(list2[:]))
         w2c = held("w2c", [P, 2, 2 * H], U8)
         nc.vector.tensor_copy(
             w2c[:].bitcast(U16).rearrange("p a (u m) -> p a u m", u=PACK),
             w2_raw[:].bitcast(U16).rearrange("p a (m u) -> p a u m", u=PACK),
         )
-        w2s = held("w2s", [P, 2 * H], U8)
-        nc.gpsimd.tensor_copy(
-            w2s[:].rearrange("p (a u m) -> p a u m", a=2, u=PACK),
-            w2s_raw[:].rearrange("p (a m u) -> p a u m", a=2, u=PACK),
-        )
         for half in range(2):
             nc.vector.tensor_copy(
                 v2[1][:, BANK * half : BANK * (half + 1)], tab2_1[:].indirect(list2[:, 32 * half : 32 * (half + 1)])
             )
 
-        pages = [placed("page%d" % u, AT_PAGE[u], [P, T2], F32) for u in range(PACK)]
+        pages = [placed("page%d" % u, AT_TAB2 + 8 * u, [P, T2], F32) for u in range(PACK)]
 
         def place(u, h, factor, where, cols):
             nc.vector.tensor_tensor(pages[u][:].indirect(where[:, cols.start // 16 : cols.stop // 16]), h, factor, MULT)
@@ -200,11 +188,9 @@ def tile_list_terrain_weave_kernel(
         HELD_BACK = 256
         kept = slice(0, S - HELD_BACK)
         late = slice(S - HELD_BACK, S)
-        wg2_t = [placed("wg2_%d" % u, AT_WG2 + 4 * u, [P, S], F32) for u in range(PACK)]
-        for u in range(2):
-            for q in (0, 2, 1, 3):
-                nc.sync.dma_start(wg2_t[u][32 * q : 32 * q + 32, :], wg2.rearrange("(q t) m -> q t m", t=PACK)[:, u, :])
-        h2 = [placed("h2_%d" % u, AT_H2[u], [P, S], F32) for u in range(PACK)]
+        load_wg2(0, (2, 1, 3))
+        load_wg2(1, (0, 2, 1, 3))
+        h2 = [placed("h2_%d" % u, AT_H2 + 4 * u, [P, S], F32) for u in range(PACK)]
 
         def plain_sum(u, cols, width, at_bank):
             acc = bank("acc_h2", at_bank)
@@ -213,116 +199,70 @@ def tile_list_terrain_weave_kernel(
                     nc.tensor.matmul_mx(
                         out=acc[:, first - cols.start : first - cols.start + width],
                         lhsT=w2c[:, a, 256 * u : 256 * (u + 1)].bitcast(FP4X4),
-                        lhsT_scale=w2s[:, H * a + P * u : H * a + P * (u + 1)],
+                        lhsT_scale=plain_scale[:, (S + H) * a + S + P * u : (S + H) * a + S + P * (u + 1)],
                         rhs=v2[a][:, first : first + width].bitcast(FP8X4),
-                        rhs_scale=v2_scale[:, S * a + first : S * a + first + width],
+                        rhs_scale=plain_scale[:, (S + H) * a + first : (S + H) * a + first + width],
                         start=(a == 0),
                         stop=(a == 1),
                     )
             return acc
 
         FIRST = 256
-        for u in range(PACK):
-            parts = [(slice(0, BANK), BANK, 2 * u % PACK), (slice(BANK, S), BANK, (2 * u + 1) % PACK)]
-            if u == 0:
-                parts[0:1] = [(slice(0, FIRST), P, 0), (slice(FIRST, BANK), P, 3)]
-            for cols, width, at_bank in parts:
-                acc = plain_sum(u, cols, width, at_bank)
-                if (u, cols.stop) == (PACK - 1, S):
-                    last_acc = acc
-                    cols = slice(BANK, kept.stop)
-                nc.scalar.activation(h2[u][:, cols], acc[:, 0 : cols.stop - cols.start], ACT.Abs)
+        low, high = slice(0, BANK), slice(BANK, S)
+        sums_h2 = [(0, slice(0, FIRST), P), (0, slice(FIRST, BANK), P), (0, high, BANK), (1, low, BANK), (1, high, BANK)]
+        sums_h2.extend([(u, cols, BANK) for u in (2, 3) for cols in (low, high)])
+        for n, (u, cols, width) in enumerate(sums_h2):
+            acc = plain_sum(u, cols, width, (0, 1, 2, 4, 5, 6, 7, 0, 3)[n])
+            if (u, cols.stop) == (PACK - 1, S):
+                last_acc = acc
+                cols = slice(BANK, kept.stop)
+            nc.scalar.activation(h2[u][:, cols], acc[:, 0 : cols.stop - cols.start], ACT.Abs)
 
-        for cols in (slice(0, FIRST), slice(FIRST, BANK), slice(BANK, S)):
-            place(0, h2[0][:, cols], wg2_t[0][:, cols], list4, cols)
+        for u, cols in ((0, slice(0, FIRST)), (0, slice(FIRST, BANK)), (0, high), (1, slice(0, S))):
+            place(u, h2[u][:, cols], wg2_t[u][:, cols], list4, cols)
 
         def gather_mountain(a):
             words = load_table_words("tab_%d" % a, tab_words, a, AT_TAB)
-            picked = placed("v_%d" % a, (AT_H2[1], AT_W1_WOVEN)[a], [P, S], U32)
-            dst = picked[:].rearrange("p (t q i) -> p q t i", t=PACK, i=8)
             if a == 0:
+                picked = placed("v_0", AT_V, [P, S], U32)
+                dst = picked[:].rearrange("p (t q i) -> p q t i", t=PACK, i=8)
                 nc.vector.tensor_copy(dst, words[:].indirect(list1[:]))
-            else:
-                for b in range(2):
-                    nc.vector.tensor_copy(dst[:, 16 * b : 16 * (b + 1)], words[:].indirect(list1[:, 32 * b : 32 * (b + 1)]))
-            return picked
+                return [[picked[:, 2 * P * t + P * b : 2 * P * t + P * (b + 1)] for t in range(PACK)] for b in range(2)]
+            halves = []
+            for b in range(2):
+                picked = placed("v_1%d" % b, AT_V + 4 + 2 * b, [P, PASS], U32)
+                dst = picked[:].rearrange("p (t q i) -> p q t i", t=PACK, i=8)
+                nc.vector.tensor_copy(dst, words[:].indirect(list1[:, 32 * b : 32 * (b + 1)]))
+                halves.append([picked[:, P * t : P * (t + 1)] for t in range(PACK)])
+            return halves
 
-        place(1, h2[1][:], wg2_t[1][:], list4, slice(0, S))
-
-        w1_raw = placed("w1_raw", AT_W1, [P, 2, PACK, H], F32)
-        w1_rows = w1.rearrange("(a p j) c -> a p j c", a=2, j=PACK)
-        w1_woven = placed("w1_woven", AT_W1_WOVEN, [P, 2 * PACK * H], BF16)
-        for a in range(2):
-            nc.sync.dma_start(w1_raw[:, a], w1_rows[a])
-            weave(w1_woven[:, PACK * H * a : PACK * H * (a + 1)], w1_raw[:, a])
-        v = [gather_mountain(0)]
-        w1c = placed("w1c", AT_TAB + 12, [P, 2 * H], U32)
-        w1s = held("w1s", [P, 2 * H], U8)
-        quantize(w1c, w1s, w1_woven)
-
-        wg2_rows = held("wg2_rows", [P, S], F32)
-        nc.sync.dma_start(wg2_rows[:], wg2)
-        turned = [turn_wg2(half) for half in range(2)]
-        for u in (2, 3):
-            for half in range(2):
-                deal_wg2(turned[half], u, half)
-        v.append(gather_mountain(1))
-        spread_scales(nc.sync, v_scale, v_scale_sorted)
         for b in range(2):
             nc.sync.dma_start(
                 gain_rows[PACK * b : PACK * (b + 1), :].rearrange("t (q i) -> t q i", i=8),
                 gain[PASS * b : PASS * (b + 1)].rearrange("(q t i) -> t q i", t=PACK, i=8),
             )
-        gain_turned = bank("gain_turned", 6)
+        gain_turned = bank("gain_turned", 1)
         nc.tensor.transpose(gain_turned[:, 0:P], gain_rows[:], ident[:])
         gains = held("gains", [P, 2 * PACK], F32)
         nc.scalar.copy(gains[:], gain_turned[:, 0 : 2 * PACK])
 
-        place(2, h2[2][:], wg2_t[2][:], list4, slice(0, S))
-        place(3, h2[3][:, kept], wg2_t[3][:, kept], list4, kept)
+        w1_raw = [placed("w1_raw%d" % a, AT_W1 + 8 * a, [P, PACK, H], F32) for a in range(2)]
+        w1_rows = w1.rearrange("(a p j) c -> a p j c", a=2, j=PACK)
+        w1_woven = placed("w1_woven", AT_W1_WOVEN, [P, 2 * PACK * H], BF16)
+        for a in range(2):
+            nc.sync.dma_start(w1_raw[a][:], w1_rows[a])
+            weave(w1_woven[:, PACK * H * a : PACK * H * (a + 1)], w1_raw[a][:])
+        v = [gather_mountain(0)]
+        w1c = held("w1c", [P, 2 * H], U32)
+        w1s = held("w1s", [P, 2 * H], U8)
+        quantize(w1c, w1s, w1_woven)
 
-        a_planes = placed("a_planes", AT_A_PLANES, [P, 2, PACK, H], BF16)
-        a_woven = placed("a_woven", AT_A_WOVEN, [P, 2 * PACK * H], BF16)
-        for b in range(2):
-            for t in range(PACK):
-                cols = slice(2 * P * t + P * b, 2 * P * t + P * (b + 1))
-                acc = bank("acc_a", (0, 1, 2, 4, 5, 6, 7, 0)[PACK * b + t])
-                for a in range(2):
-                    nc.tensor.matmul_mx(
-                        out=acc[:],
-                        lhsT=v[a][:, cols].bitcast(FP8X4),
-                        lhsT_scale=v_scale[:, S * a + cols.start : S * a + cols.stop],
-                        rhs=w1c[:, H * a : H * (a + 1)].bitcast(FP8X4),
-                        rhs_scale=w1s[:, H * a : H * (a + 1)],
-                        start=(a == 0),
-                        stop=(a == 1),
-                    )
-                nc.scalar.activation(
-                    a_planes[:, b, t, :].rearrange("p (u m) -> p u m", u=PACK),
-                    acc[:].rearrange("p (m u) -> p u m", u=PACK),
-                    ACT.Copy,
-                    scale=gains[:, PACK * b + t : PACK * b + t + 1],
-                )
-        for b in range(2):
-            weave(a_woven[:, PACK * H * b : PACK * H * (b + 1)], a_planes[:, b])
-        ac = placed("ac", AT_H2[3], [P, 2 * H], U32)
-        asc = held("asc", [P, 2 * H], U8)
-        quantize(ac, asc, a_woven)
+        spread_scales(nc.sync, v_scale, v_scale_sorted)
+        load_wg2(3, (0, 2))
+        v.append(gather_mountain(1))
 
-        list3 = load_list("list3", offs3)
         blend_raw = [load_blend(0)]
-        wg1_t = [load_wg1(0)]
-        blend_raw.extend([load_blend(1), load_blend(2)])
-        wg1_t.append(load_wg1(1))
-        biases = held("biases", [P, PACK], F32)
-        nc.sync.dma_start(biases[:], bias.rearrange("(p t) -> p t", t=PACK))
-        w3c = held("w3c", [P, N], U32)
-        nc.sync.dma_start(w3c[:].bitcast(I32), w3_words[0].rearrange("p c i -> p (c i)").bitcast(I32))
-        for q in range(QUADS):
-            nc.sync.dma_start(w3s[32 * q : 32 * q + 4, :].bitcast(I32), w3_scales[0, 4 * q : 4 * q + 4, :].bitcast(I32))
-
-        woven_at = [AT_TAB + 8, AT_WG2 + 8, AT_WG2 - 1]
-        h1_banks = ((4, 5, 6, 7), (0, 1, 2, 3), (4, 5, 6, 7))
+        woven_at = [AT_WG1 + 16, AT_A_PLANES + 4, AT_BC[0]]
         bc, bs = [], []
 
         def quantize_blend(i):
@@ -331,24 +271,77 @@ def tile_list_terrain_weave_kernel(
             woven = placed("blend_woven%d" % i, woven_at[i], [P, 2 * PACK * width], BF16)
             for b in range(2):
                 weave(woven[:, PACK * width * b : PACK * width * (b + 1)], blend_raw[i][b][:])
-            if i == 0:
-                bc.append(placed("bc0", AT_WG2 + 8, [P, 2 * width], U32))
-            elif i == 1:
-                bc.append(held("bc1", [P, 2 * width], U32))
-            else:
-                bc.append(placed("bc2", AT_BLEND, [P, 2 * width], U32))
-            if i == 0:
-                bs.append(held("bs0", [P, 2 * width], U8))
-            else:
-                bs.append(placed("bs%d" % i, AT_H1 + 4 * (i - 1) + 2, [P, 2 * width], U8))
+            bc.append(placed("bc%d" % i, AT_BC[i], [P, 2 * width], U32))
+            bs.append(held("bs%d" % i, [P, 2 * width], U8))
             quantize(bc[i], bs[i], woven)
 
+        quantize_blend(0)
+        load_wg2(2, (0, 2, 1, 3))
+        load_wg2(3, (1, 3))
+        place(2, h2[2][:], wg2_t[2][:], list4, slice(0, S))
+        place(3, h2[3][:, kept], wg2_t[3][:, kept], list4, kept)
+
+        a_planes = placed("a_planes", AT_A_PLANES, [P, 2, PACK, H], BF16)
+        a_woven = placed("a_woven", AT_A_WOVEN, [P, 2 * PACK * H], BF16)
+        a_banks = (0, 1, 2, 4, 5, 6, 7, 0)
+        acc_a = {}
+
+        def project(b, t, a):
+            cols = slice(2 * P * t + P * b, 2 * P * t + P * (b + 1))
+            if a == 0:
+                acc_a[b, t] = bank("acc_a", a_banks[PACK * b + t])
+            nc.tensor.matmul_mx(
+                out=acc_a[b, t][:],
+                lhsT=v[a][b][t].bitcast(FP8X4),
+                lhsT_scale=v_scale[:, S * a + cols.start : S * a + cols.stop],
+                rhs=w1c[:, H * a : H * (a + 1)].bitcast(FP8X4),
+                rhs_scale=w1s[:, H * a : H * (a + 1)],
+                start=(a == 0),
+                stop=(a == 1),
+            )
+
+        slots = [(b, t) for b in range(2) for t in range(PACK)]
+        for t in range(2):
+            project(0, t, 0)
+        for b, t in slots:
+            if (b, t) > (0, 1):
+                project(b, t, 0)
+            project(b, t, 1)
+            nc.scalar.activation(
+                a_planes[:, b, t, :].rearrange("p (u m) -> p u m", u=PACK),
+                acc_a[b, t][:].rearrange("p (m u) -> p u m", u=PACK),
+                ACT.Copy,
+                scale=gains[:, PACK * b + t : PACK * b + t + 1],
+            )
+            if t == PACK - 1:
+                weave(a_woven[:, PACK * H * b : PACK * H * (b + 1)], a_planes[:, b])
+        ac = held("ac", [P, 2 * H], U32)
+        asc = held("asc", [P, 2 * H], U8)
+        quantize(ac, asc, a_woven)
+
+        list3 = load_list("list3", offs3)
+        blend_raw.append(load_blend(1))
+        load_wg1(0)
+        blend_raw.append(load_blend(2))
+        load_wg1(1)
+        biases = held("biases", [P, PACK], F32)
+        nc.sync.dma_start(biases[:], bias.rearrange("(p t) -> p t", t=PACK))
+        w3c = held("w3c", [P, N], U32)
+        nc.sync.dma_start(w3c[:].bitcast(I32), w3_words[0].rearrange("p c i -> p (c i)").bitcast(I32))
+        for q in range(QUADS):
+            nc.sync.dma_start(w3s[32 * q : 32 * q + 4, :].bitcast(I32), w3_scales[0, 4 * q : 4 * q + 4, :].bitcast(I32))
+
+        acc_h1 = {}
+
         def blended_sum(i, u):
-            width = pieces[i].stop - pieces[i].start
-            acc = bank("acc_h1", h1_banks[i][u])[:, 0:width]
+            cols = pieces[i]
+            width = cols.stop - cols.start
+            half = cols.start // BANK
+            if (half, u) not in acc_h1:
+                acc_h1[half, u] = bank("acc_h1", PACK * (1 - half) + u)
             for b in range(2):
                 nc.tensor.matmul_mx(
-                    out=acc,
+                    out=acc_h1[half, u][:, cols.start % BANK : cols.start % BANK + width],
                     lhsT=ac[:, H * b + P * u : H * b + P * (u + 1)].bitcast(FP8X4),
                     lhsT_scale=asc[:, H * b + P * u : H * b + P * (u + 1)],
                     rhs=bc[i][:, width * b : width * (b + 1)].bitcast(FP8X4),
@@ -356,64 +349,73 @@ def tile_list_terrain_weave_kernel(
                     start=(b == 0),
                     stop=(b == 1),
                 )
-            return acc
 
-        def place_blended(name, u, at, parts):
-            cols = slice(pieces[parts[0]].start, pieces[parts[-1]].stop)
-            h = placed(name, at, [P, cols.stop - cols.start], F32)
-            for i in parts:
-                nc.scalar.copy(h[:, pieces[i].start - cols.start : pieces[i].stop - cols.start], sums[i, u])
-            first = cols.start % BANK
-            place(u, h[:], wg1_t[cols.start // BANK][:, u, first : first + cols.stop - cols.start], list3, cols)
+        def place_blended(u, first, stop, at):
+            h = placed("h1_%d_%d" % (u, first), at, [P, stop - first], F32)
+            for half in range(first // BANK, (stop - 1) // BANK + 1):
+                lo, hi = max(first, BANK * half), min(stop, BANK * (half + 1))
+                nc.scalar.copy(h[:, lo - first : hi - first], acc_h1[half, u][:, lo - BANK * half : hi - BANK * half])
+            place(u, h[:], wg1_t[:, u, first:stop], list3, slice(first, stop))
 
-        quantize_blend(0)
         h2_late = placed("h2_late", AT_A_PLANES, [P, HELD_BACK], F32)
         nc.scalar.activation(h2_late[:], last_acc[:, BANK - HELD_BACK : BANK], ACT.Abs)
         place(3, h2_late[:], wg2_t[3][:, late], list4, late)
 
-        z_pairs = placed("z_pairs", AT_BLEND, [P, 2 * T2 * 2], BF16)
+        z_pairs = placed("z_pairs", AT_WG2, [P, 2 * T2 * 2], BF16)
+
+        def z_slot(u, cols):
+            return z_pairs[:].rearrange("p (h t e) -> p h t e", h=2, e=2)[:, u // 2, cols, u % 2]
 
         def relu(u, cols):
-            dst = z_pairs[:].rearrange("p (h t e) -> p h t e", h=2, e=2)[:, u // 2, cols, u % 2]
-            nc.scalar.activation(dst, pages[u][:, cols], ACT.Relu, bias=biases[:, u : u + 1])
+            nc.scalar.activation(z_slot(u, cols), pages[u][:, cols], ACT.Relu, bias=biases[:, u : u + 1])
 
-        sums = {}
-        last = len(pieces) - 1
-        for i in range(len(pieces)):
-            for u in range(PACK):
-                sums[i, u] = blended_sum(i, u)
-            for u in range(PACK):
-                at = AT_H1 + 4 * (i % 2) + 2 * u
-                if i < last and u >= 2:
-                    at = blend_at(i + 1, 1) + u - 2
-                if i < last and u == 2:
-                    quantize_blend(i + 1)
-                place_blended("h1_%d%d" % (i, u), u, at, [i])
+        for u in range(PACK):
+            blended_sum(0, u)
+        quantize_blend(1)
+        place_blended(0, 0, 256, AT_H1)
+        for u in (1, 2, 0, 3):
+            blended_sum(1, u)
+        for u in (1, 2):
+            place_blended(u, 0, BANK, AT_H1 + 2 * u)
+        quantize_blend(2)
+        for u in range(PACK):
+            blended_sum(2, u)
+        place_blended(0, 256, BANK, blend_at(2, 1))
+        place_blended(3, 0, 256, blend_at(2, 1) + 1)
         for u in range(PACK - 1):
+            place_blended(u, BANK, S, AT_H1 + 6 + 2 * u)
+        place_blended(3, 256, S, AT_H1 + 12)
+        for u in range(2):
             relu(u, slice(0, T2))
+        relu(2, slice(0, T2))
+        last_bias = placed("last_bias", AT_TAB2 + 16, [P, 1], F32)
+        nc.scalar.copy(last_bias[:], biases[:, 3:4])
 
         widths = [128, 128, 256, 512, 512, 512]
-        on_vector = [(0,), (), (), (1, 3), (1, 3), (1, 3)]
+        on_vector = [(), (), (), (), (3,), (1, 3)]
         chunks = [slice(sum(widths[:c]), sum(widths[: c + 1])) for c in range(len(widths))]
         out_rows = out.rearrange("(nb p) t -> p nb t", p=P)
         pair_words = z_pairs[:].bitcast(F32).rearrange("p (h t) -> p t h", h=2)
         z_woven, zc, zs = {}, {}, {}
 
+        def last_relu(c):
+            cols = chunks[c]
+            nc.vector.tensor_scalar(z_slot(3, cols), pages[3][:, cols], last_bias[:], 0.0, ADD, MAX)
+
         def weave_z(c):
-            relu(PACK - 1, chunks[c])
             z_woven[c] = placed("z_woven%d" % c, AT_W1 + chunks[c].start * PACK * 2 // 1024, [P, PACK * widths[c]], BF16)
             nc.vector.tensor_copy(
                 z_woven[c][:].bitcast(F32).rearrange("p (t h) -> p t h", h=2), pair_words[:, chunks[c], :]
             )
 
         def quantize_z(c):
-            zc[c] = held("zc%d" % c, [P, widths[c]], U32)
+            zc[c] = placed("zc%d" % c, AT_H2 + chunks[c].start * 4 / 1024, [P, widths[c]], U32)
             zs[c] = held("zs%d" % c, [P, widths[c]], U8)
             quantize(zc[c], zs[c], z_woven[c])
 
         def features(c):
             cols, width = chunks[c], widths[c]
-            staged = placed("staged%d" % c, AT_BLEND + 16 + cols.start * PACK * 4 // 1024, [P, PACK, width], F32)
+            staged = placed("staged%d" % c, AT_BLEND + cols.start * PACK * 4 // 1024, [P, PACK, width], F32)
             together = BANK // width
             for g in range(PACK // together):
                 acc = bank("acc_out", (cols.start * PACK // BANK + g) % 8)
@@ -432,12 +434,17 @@ def tile_list_terrain_weave_kernel(
                 copy(staged[:, blocks, :].rearrange("p b t -> p (b t)"), acc[:])
                 nc.sync.dma_start(out_rows[:, blocks, cols], staged[:, blocks, :])
 
+        on_scalar = 4
+        last_relu(0)
+        last_relu(1)
+        rest = slice(chunks[on_scalar].start, T2)
+        nc.scalar.activation(z_slot(3, rest), pages[3][:, rest], ACT.Relu, bias=last_bias[:])
         weave_z(0)
-        quantize_z(0)
         weave_z(1)
-        for c in range(1, len(chunks)):
-            if c + 1 < len(chunks):
-                weave_z(c + 1)
+        for c in range(len(chunks)):
             quantize_z(c)
-            features(c - 1)
-        features(len(chunks) - 1)
+            if 0 < c < len(chunks) - 1:
+                weave_z(c + 1)
+            if c + 2 < on_scalar:
+                last_relu(c + 2)
+            features(c)

@@ -28,17 +28,18 @@ ROWS = 96
 
 AT_TAB2 = 0
 AT_TAB = 32
-AT_A_PLANES = 84
-AT_A_WOVEN = 40
-AT_H1 = 48
+AT_A_PLANES = 32
+AT_A_WOVEN = 16
+AT_H1 = 64
 AT_W1 = 64
 AT_BLEND = 80
 AT_WG2 = 112
 AT_H2 = 128
 AT_V = 144
 AT_W1_WOVEN = 152
-AT_BC = (160, 164, 152)
+AT_BC = (50, 160, 152)
 AT_WG1 = 168
+AT_PAGE = (0, 8, 56, 42)
 
 
 def tile_list_terrain_weave_kernel(
@@ -54,6 +55,9 @@ def tile_list_terrain_weave_kernel(
 
         def held(name, shape, dtype):
             return sb.tile(shape, dtype, name=name, align_bytes=64)
+
+        def ring(tag, shape, dtype):
+            return sb.tile(shape, dtype, name=tag, tag=tag, bufs=2, align_bytes=64)
 
         def placed(name, kib, shape, dtype):
             return reuse.tile(shape, dtype, name=name, align_bytes=64, offset=int(kib * 1024))
@@ -96,6 +100,24 @@ def tile_list_terrain_weave_kernel(
             for q in quads:
                 nc.sync.dma_start(wg2_t[u][32 * q : 32 * q + 32, :], rows)
 
+        def turn_wg2(half):
+            turned = bank("wg2_turned", 6 + half)
+            for c in range(PACK):
+                first = BANK * half + P * c
+                nc.tensor.transpose(turned[:, P * c : P * (c + 1)], wg2_rows[:, first : first + P], ident[:])
+            return turned
+
+        def deal_wg2(turned, u, half):
+            repeated = ring("wg2_repeated", [P, PACK, QUADS, 32], F32)
+            src = turned[:].rearrange("p (c q u) -> p c u q", c=PACK, u=PACK)[:, :, u, :]
+            nc.scalar.copy(repeated[:], src.unsqueeze(2).to_broadcast([P, PACK, QUADS, 32]))
+            back = bank("wg2_back", (4, 3)[half] if u == 1 else half)
+            for c in range(PACK):
+                nc.tensor.transpose(
+                    back[:, P * c : P * (c + 1)], repeated[:, c].rearrange("p g q -> p (g q)"), ident[:]
+                )
+            nc.scalar.copy(wg2_t[u][:, BANK * half : BANK * (half + 1)], back[:])
+
         wg1_t = placed("wg1", AT_WG1, [P, PACK, S], F32)
 
         def load_wg1(half):
@@ -129,20 +151,24 @@ def tile_list_terrain_weave_kernel(
         def quantize(codes, scales, woven):
             nc.vector.quantize_mx(out=codes[:].bitcast(FP8X4), scales=scales[:], in_=woven[:])
 
+        w2s_raw = zeroed(nc.vector, "w2s_raw", 2 * H)
         list2 = load_list("list2", offs2)
         sc2 = load_table_scales(nc.vector, "sc2", tab2_scales)
-        w2s_raw = load_table_scales(nc.vector, "w2s_raw", w2_scales)
         list1 = load_list("list1", offs)
         sc1 = load_table_scales(nc.gpsimd, "sc1", tab_scales)
         tab2_0 = load_table_words("tab2_0", tab2_words, 0, AT_TAB2)
         w2_raw = held("w2_raw", [P, 2, 2 * H], U8)
         nc.sync.dma_start(w2_raw[:].bitcast(I32), w2_words.bitcast(I32).rearrange("a p c -> p a c"))
-        list4 = load_list("list4", offs4)
-        load_wg2(0, (0,))
+        for q in range(QUADS):
+            nc.sync.dma_start(
+                w2s_raw[32 * q : 32 * q + 4, :].bitcast(I32).rearrange("r (a c) -> r a c", a=2),
+                w2_scales[:, 4 * q : 4 * q + 4, :].bitcast(I32).rearrange("a r c -> r a c"),
+            )
         tab2_1 = load_table_words("tab2_1", tab2_words, 1, AT_TAB2)
+        list4 = load_list("list4", offs4)
         ident = held("ident", [P, P], F32)
         make_identity(nc, ident[:])
-        plain_scale = zeroed(nc.gpsimd, "plain_scale", 2 * (S + H))
+        v2_scale = zeroed(nc.gpsimd, "v2_scale", 2 * S)
         v_scale = zeroed(nc.gpsimd, "v_scale", 2 * S)
         w3s = zeroed(nc.gpsimd, "w3s", N)
         gain_rows = held("gain_rows", [P, P], F32)
@@ -150,13 +176,7 @@ def tile_list_terrain_weave_kernel(
 
         v2_scale_picked = held("v2_scale_picked", [P, S], U8)
         nc.vector.tensor_copy(v2_scale_picked[:], sc2[:].indirect(list2[:]))
-        plain_rows = held("plain_rows", [P, S + H], U8)
-        nc.vector.tensor_copy(plain_rows[:, 0:S].bitcast(I32), v2_scale_picked[:].bitcast(I32))
-        nc.gpsimd.tensor_copy(
-            plain_rows[:, S:].rearrange("p (u m) -> p u m", u=PACK),
-            w2s_raw[:].rearrange("p (m u) -> p u m", u=PACK),
-        )
-        spread_scales(nc.sync, plain_scale, plain_rows)
+        spread_scales(nc.sync, v2_scale, v2_scale_picked)
         v_scale_sorted = held("v_scale_sorted", [P, S], U8)
 
         def gather_mountain_scales(picked):
@@ -175,12 +195,17 @@ def tile_list_terrain_weave_kernel(
             w2c[:].bitcast(U16).rearrange("p a (u m) -> p a u m", u=PACK),
             w2_raw[:].bitcast(U16).rearrange("p a (m u) -> p a u m", u=PACK),
         )
+        w2s = held("w2s", [P, 2 * H], U8)
+        nc.gpsimd.tensor_copy(
+            w2s[:].rearrange("p (a u m) -> p a u m", a=2, u=PACK),
+            w2s_raw[:].rearrange("p (a m u) -> p a u m", a=2, u=PACK),
+        )
         for half in range(2):
             nc.vector.tensor_copy(
                 v2[1][:, BANK * half : BANK * (half + 1)], tab2_1[:].indirect(list2[:, 32 * half : 32 * (half + 1)])
             )
 
-        pages = [placed("page%d" % u, AT_TAB2 + 8 * u, [P, T2], F32) for u in range(PACK)]
+        pages = [placed("page%d" % u, AT_PAGE[u], [P, T2], F32) for u in range(PACK)]
 
         def place(u, h, factor, where, cols):
             nc.vector.tensor_tensor(pages[u][:].indirect(where[:, cols.start // 16 : cols.stop // 16]), h, factor, MULT)
@@ -188,8 +213,7 @@ def tile_list_terrain_weave_kernel(
         HELD_BACK = 256
         kept = slice(0, S - HELD_BACK)
         late = slice(S - HELD_BACK, S)
-        load_wg2(0, (2, 1, 3))
-        load_wg2(1, (0, 2, 1, 3))
+        load_wg2(0, (0, 2, 1, 3))
         h2 = [placed("h2_%d" % u, AT_H2 + 4 * u, [P, S], F32) for u in range(PACK)]
 
         def plain_sum(u, cols, width, at_bank):
@@ -199,9 +223,9 @@ def tile_list_terrain_weave_kernel(
                     nc.tensor.matmul_mx(
                         out=acc[:, first - cols.start : first - cols.start + width],
                         lhsT=w2c[:, a, 256 * u : 256 * (u + 1)].bitcast(FP4X4),
-                        lhsT_scale=plain_scale[:, (S + H) * a + S + P * u : (S + H) * a + S + P * (u + 1)],
+                        lhsT_scale=w2s[:, H * a + P * u : H * a + P * (u + 1)],
                         rhs=v2[a][:, first : first + width].bitcast(FP8X4),
-                        rhs_scale=plain_scale[:, (S + H) * a + first : (S + H) * a + first + width],
+                        rhs_scale=v2_scale[:, S * a + first : S * a + first + width],
                         start=(a == 0),
                         stop=(a == 1),
                     )
@@ -211,15 +235,22 @@ def tile_list_terrain_weave_kernel(
         low, high = slice(0, BANK), slice(BANK, S)
         sums_h2 = [(0, slice(0, FIRST), P), (0, slice(FIRST, BANK), P), (0, high, BANK), (1, low, BANK), (1, high, BANK)]
         sums_h2.extend([(u, cols, BANK) for u in (2, 3) for cols in (low, high)])
+        wg2_rows = held("wg2_rows", [P, S], F32)
+        nc.sync.dma_start(wg2_rows[:], wg2)
         for n, (u, cols, width) in enumerate(sums_h2):
-            acc = plain_sum(u, cols, width, (0, 1, 2, 4, 5, 6, 7, 0, 3)[n])
+            if n == 5:
+                turned = [turn_wg2(half) for half in range(2)]
+                for half in range(2):
+                    deal_wg2(turned[half], 1, half)
+            acc = plain_sum(u, cols, width, (0, 1, 2, 4, 5, 4, 4, 4, 3)[n])
             if (u, cols.stop) == (PACK - 1, S):
                 last_acc = acc
                 cols = slice(BANK, kept.stop)
             nc.scalar.activation(h2[u][:, cols], acc[:, 0 : cols.stop - cols.start], ACT.Abs)
 
-        for u, cols in ((0, slice(0, FIRST)), (0, slice(FIRST, BANK)), (0, high), (1, slice(0, S))):
-            place(u, h2[u][:, cols], wg2_t[u][:, cols], list4, cols)
+        for cols in (slice(0, FIRST), slice(FIRST, BANK), high):
+            place(0, h2[0][:, cols], wg2_t[0][:, cols], list4, cols)
+        place(1, h2[1][:], wg2_t[1][:], list4, slice(0, S))
 
         def gather_mountain(a):
             words = load_table_words("tab_%d" % a, tab_words, a, AT_TAB)
@@ -246,6 +277,10 @@ def tile_list_terrain_weave_kernel(
         gains = held("gains", [P, 2 * PACK], F32)
         nc.scalar.copy(gains[:], gain_turned[:, 0 : 2 * PACK])
 
+        for u in (2, 3):
+            for half in range(2):
+                deal_wg2(turned[half], u, half)
+
         w1_raw = [placed("w1_raw%d" % a, AT_W1 + 8 * a, [P, PACK, H], F32) for a in range(2)]
         w1_rows = w1.rearrange("(a p j) c -> a p j c", a=2, j=PACK)
         w1_woven = placed("w1_woven", AT_W1_WOVEN, [P, 2 * PACK * H], BF16)
@@ -258,11 +293,10 @@ def tile_list_terrain_weave_kernel(
         quantize(w1c, w1s, w1_woven)
 
         spread_scales(nc.sync, v_scale, v_scale_sorted)
-        load_wg2(3, (0, 2))
+        blend_raw = [load_blend(0)]
         v.append(gather_mountain(1))
 
-        blend_raw = [load_blend(0)]
-        woven_at = [AT_WG1 + 16, AT_A_PLANES + 4, AT_BC[0]]
+        woven_at = [AT_WG1 + 16, AT_A_PLANES + 4, AT_BC[1]]
         bc, bs = [], []
 
         def quantize_blend(i):
@@ -276,8 +310,6 @@ def tile_list_terrain_weave_kernel(
             quantize(bc[i], bs[i], woven)
 
         quantize_blend(0)
-        load_wg2(2, (0, 2, 1, 3))
-        load_wg2(3, (1, 3))
         place(2, h2[2][:], wg2_t[2][:], list4, slice(0, S))
         place(3, h2[3][:, kept], wg2_t[3][:, kept], list4, kept)
 
@@ -315,7 +347,7 @@ def tile_list_terrain_weave_kernel(
             )
             if t == PACK - 1:
                 weave(a_woven[:, PACK * H * b : PACK * H * (b + 1)], a_planes[:, b])
-        ac = held("ac", [P, 2 * H], U32)
+        ac = placed("ac", AT_H2 + 12, [P, 2 * H], U32)
         asc = held("asc", [P, 2 * H], U8)
         quantize(ac, asc, a_woven)
 
@@ -388,7 +420,7 @@ def tile_list_terrain_weave_kernel(
         for u in range(2):
             relu(u, slice(0, T2))
         relu(2, slice(0, T2))
-        last_bias = placed("last_bias", AT_TAB2 + 16, [P, 1], F32)
+        last_bias = placed("last_bias", AT_PAGE[2], [P, 1], F32)
         nc.scalar.copy(last_bias[:], biases[:, 3:4])
 
         widths = [128, 128, 256, 512, 512, 512]

@@ -37,9 +37,9 @@ AT_WG2 = 112
 AT_H2 = 128
 AT_V = 144
 AT_W1_WOVEN = 152
-AT_BC = (50, 160, 152)
+AT_BC = (160, 164, 152)
 AT_WG1 = 168
-AT_PAGE = (0, 8, 56, 42)
+AT_PAGE = (0, 8, 56, 48)
 
 
 def tile_list_terrain_weave_kernel(
@@ -103,8 +103,7 @@ def tile_list_terrain_weave_kernel(
         def turn_wg2(half):
             turned = bank("wg2_turned", 6 + half)
             for c in range(PACK):
-                first = BANK * half + P * c
-                nc.tensor.transpose(turned[:, P * c : P * (c + 1)], wg2_rows[:, first : first + P], ident[:])
+                nc.tensor.transpose(turned[:, P * c : P * (c + 1)], wg2_rows[half][:, P * c : P * (c + 1)], ident[:])
             return turned
 
         def deal_wg2(turned, u, half):
@@ -235,12 +234,14 @@ def tile_list_terrain_weave_kernel(
         low, high = slice(0, BANK), slice(BANK, S)
         sums_h2 = [(0, slice(0, FIRST), P), (0, slice(FIRST, BANK), P), (0, high, BANK), (1, low, BANK), (1, high, BANK)]
         sums_h2.extend([(u, cols, BANK) for u in (2, 3) for cols in (low, high)])
-        wg2_rows = held("wg2_rows", [P, S], F32)
-        nc.sync.dma_start(wg2_rows[:], wg2)
+        wg2_rows = [held("wg2_rows%d" % half, [P, BANK], F32) for half in range(2)]
+        for half in range(2):
+            nc.sync.dma_start(wg2_rows[half][:], wg2[:, BANK * half : BANK * (half + 1)])
         for n, (u, cols, width) in enumerate(sums_h2):
             if n == 5:
-                turned = [turn_wg2(half) for half in range(2)]
+                turned = []
                 for half in range(2):
+                    turned.append(turn_wg2(half))
                     deal_wg2(turned[half], 1, half)
             acc = plain_sum(u, cols, width, (0, 1, 2, 4, 5, 4, 4, 4, 3)[n])
             if (u, cols.stop) == (PACK - 1, S):
@@ -250,7 +251,8 @@ def tile_list_terrain_weave_kernel(
 
         for cols in (slice(0, FIRST), slice(FIRST, BANK), high):
             place(0, h2[0][:, cols], wg2_t[0][:, cols], list4, cols)
-        place(1, h2[1][:], wg2_t[1][:], list4, slice(0, S))
+        for cols in (low, high):
+            place(1, h2[1][:, cols], wg2_t[1][:, cols], list4, cols)
 
         def gather_mountain(a):
             words = load_table_words("tab_%d" % a, tab_words, a, AT_TAB)
@@ -293,10 +295,10 @@ def tile_list_terrain_weave_kernel(
         quantize(w1c, w1s, w1_woven)
 
         spread_scales(nc.sync, v_scale, v_scale_sorted)
-        blend_raw = [load_blend(0)]
         v.append(gather_mountain(1))
+        blend_raw = [load_blend(0)]
 
-        woven_at = [AT_WG1 + 16, AT_A_PLANES + 4, AT_BC[1]]
+        woven_at = [AT_WG1 + 16, AT_A_PLANES + 4, blend_at(1, 0)]
         bc, bs = [], []
 
         def quantize_blend(i):
@@ -306,12 +308,16 @@ def tile_list_terrain_weave_kernel(
             for b in range(2):
                 weave(woven[:, PACK * width * b : PACK * width * (b + 1)], blend_raw[i][b][:])
             bc.append(placed("bc%d" % i, AT_BC[i], [P, 2 * width], U32))
-            bs.append(held("bs%d" % i, [P, 2 * width], U8))
+            if i == 0:
+                bs.append(held("bs0", [P, 2 * width], U8))
+            else:
+                bs.append(placed("bs%d" % i, AT_H1 + 4 * (i - 1), [P, 2 * width], U8))
             quantize(bc[i], bs[i], woven)
 
-        quantize_blend(0)
         place(2, h2[2][:], wg2_t[2][:], list4, slice(0, S))
         place(3, h2[3][:, kept], wg2_t[3][:, kept], list4, kept)
+
+        quantize_blend(0)
 
         a_planes = placed("a_planes", AT_A_PLANES, [P, 2, PACK, H], BF16)
         a_woven = placed("a_woven", AT_A_WOVEN, [P, 2 * PACK * H], BF16)
@@ -347,7 +353,7 @@ def tile_list_terrain_weave_kernel(
             )
             if t == PACK - 1:
                 weave(a_woven[:, PACK * H * b : PACK * H * (b + 1)], a_planes[:, b])
-        ac = placed("ac", AT_H2 + 12, [P, 2 * H], U32)
+        ac = held("ac", [P, 2 * H], U32)
         asc = held("asc", [P, 2 * H], U8)
         quantize(ac, asc, a_woven)
 
@@ -366,14 +372,11 @@ def tile_list_terrain_weave_kernel(
         acc_h1 = {}
 
         def blended_sum(i, u):
-            cols = pieces[i]
-            width = cols.stop - cols.start
-            half = cols.start // BANK
-            if (half, u) not in acc_h1:
-                acc_h1[half, u] = bank("acc_h1", PACK * (1 - half) + u)
+            width = pieces[i].stop - pieces[i].start
+            acc_h1[i, u] = bank("acc_h1", PACK * ((i + 1) % 2) + u)[:, 0:width]
             for b in range(2):
                 nc.tensor.matmul_mx(
-                    out=acc_h1[half, u][:, cols.start % BANK : cols.start % BANK + width],
+                    out=acc_h1[i, u],
                     lhsT=ac[:, H * b + P * u : H * b + P * (u + 1)].bitcast(FP8X4),
                     lhsT_scale=asc[:, H * b + P * u : H * b + P * (u + 1)],
                     rhs=bc[i][:, width * b : width * (b + 1)].bitcast(FP8X4),
@@ -382,12 +385,11 @@ def tile_list_terrain_weave_kernel(
                     stop=(b == 1),
                 )
 
-        def place_blended(u, first, stop, at):
-            h = placed("h1_%d_%d" % (u, first), at, [P, stop - first], F32)
-            for half in range(first // BANK, (stop - 1) // BANK + 1):
-                lo, hi = max(first, BANK * half), min(stop, BANK * (half + 1))
-                nc.scalar.copy(h[:, lo - first : hi - first], acc_h1[half, u][:, lo - BANK * half : hi - BANK * half])
-            place(u, h[:], wg1_t[:, u, first:stop], list3, slice(first, stop))
+        def place_blended(i, u, at):
+            cols = pieces[i]
+            h = placed("h1_%d%d" % (i, u), at, [P, cols.stop - cols.start], F32)
+            nc.scalar.copy(h[:], acc_h1[i, u])
+            place(u, h[:], wg1_t[:, u, cols], list3, cols)
 
         h2_late = placed("h2_late", AT_A_PLANES, [P, HELD_BACK], F32)
         nc.scalar.activation(h2_late[:], last_acc[:, BANK - HELD_BACK : BANK], ACT.Abs)
@@ -401,27 +403,23 @@ def tile_list_terrain_weave_kernel(
         def relu(u, cols):
             nc.scalar.activation(z_slot(u, cols), pages[u][:, cols], ACT.Relu, bias=biases[:, u : u + 1])
 
-        for u in range(PACK):
-            blended_sum(0, u)
-        quantize_blend(1)
-        place_blended(0, 0, 256, AT_H1)
-        for u in (1, 2, 0, 3):
-            blended_sum(1, u)
-        for u in (1, 2):
-            place_blended(u, 0, BANK, AT_H1 + 2 * u)
-        quantize_blend(2)
-        for u in range(PACK):
-            blended_sum(2, u)
-        place_blended(0, 256, BANK, blend_at(2, 1))
-        place_blended(3, 0, 256, blend_at(2, 1) + 1)
-        for u in range(PACK - 1):
-            place_blended(u, BANK, S, AT_H1 + 6 + 2 * u)
-        place_blended(3, 256, S, AT_H1 + 12)
+        for i, cols in enumerate(pieces):
+            for u in range(PACK):
+                blended_sum(i, u)
+            for u in range(PACK):
+                at = AT_H1 + 4 * i + (cols.stop - cols.start) // 256 * u
+                if u >= 2 and i + 1 < len(pieces):
+                    at = blend_at(i + 1, 1) + u - 2
+                place_blended(i, u, at)
+                if u == 0 and i + 1 < len(pieces):
+                    quantize_blend(i + 1)
         for u in range(2):
             relu(u, slice(0, T2))
-        relu(2, slice(0, T2))
-        last_bias = placed("last_bias", AT_PAGE[2], [P, 1], F32)
-        nc.scalar.copy(last_bias[:], biases[:, 3:4])
+        last_bias = []
+        for half in range(2):
+            relu(2, slice(S * half, S * (half + 1)))
+            last_bias.append(placed("last_bias%d" % half, AT_PAGE[1 + half], [P, 1], F32))
+            nc.scalar.copy(last_bias[half][:], biases[:, 3:4])
 
         widths = [128, 128, 256, 512, 512, 512]
         on_vector = [(), (), (), (), (3,), (1, 3)]
@@ -432,7 +430,7 @@ def tile_list_terrain_weave_kernel(
 
         def last_relu(c):
             cols = chunks[c]
-            nc.vector.tensor_scalar(z_slot(3, cols), pages[3][:, cols], last_bias[:], 0.0, ADD, MAX)
+            nc.vector.tensor_scalar(z_slot(3, cols), pages[3][:, cols], last_bias[cols.start // S][:], 0.0, ADD, MAX)
 
         def weave_z(c):
             z_woven[c] = placed("z_woven%d" % c, AT_W1 + chunks[c].start * PACK * 2 // 1024, [P, PACK * widths[c]], BF16)
@@ -466,17 +464,14 @@ def tile_list_terrain_weave_kernel(
                 copy(staged[:, blocks, :].rearrange("p b t -> p (b t)"), acc[:])
                 nc.sync.dma_start(out_rows[:, blocks, cols], staged[:, blocks, :])
 
-        on_scalar = 4
         last_relu(0)
         last_relu(1)
-        rest = slice(chunks[on_scalar].start, T2)
-        nc.scalar.activation(z_slot(3, rest), pages[3][:, rest], ACT.Relu, bias=last_bias[:])
         weave_z(0)
         weave_z(1)
         for c in range(len(chunks)):
             quantize_z(c)
             if 0 < c < len(chunks) - 1:
                 weave_z(c + 1)
-            if c + 2 < on_scalar:
+            if c + 2 < len(chunks):
                 last_relu(c + 2)
             features(c)

@@ -28,7 +28,7 @@ ROWS = 96
 
 AT_TAB2 = 0
 AT_TAB = 32
-AT_A_PLANES = 32
+AT_A_PLANES = 84
 AT_A_WOVEN = 16
 AT_H1 = 64
 AT_W1 = 64
@@ -95,11 +95,6 @@ def tile_list_terrain_weave_kernel(
 
         wg2_t = [placed("wg2_%d" % u, AT_WG2 + 4 * u, [P, S], F32) for u in range(PACK)]
 
-        def load_wg2(u, quads):
-            rows = wg2.rearrange("(q t) m -> q t m", t=PACK)[:, u, :]
-            for q in quads:
-                nc.sync.dma_start(wg2_t[u][32 * q : 32 * q + 32, :], rows)
-
         def turn_wg2(half):
             turned = bank("wg2_turned", 6 + half)
             for c in range(PACK):
@@ -110,7 +105,7 @@ def tile_list_terrain_weave_kernel(
             repeated = ring("wg2_repeated", [P, PACK, QUADS, 32], F32)
             src = turned[:].rearrange("p (c q u) -> p c u q", c=PACK, u=PACK)[:, :, u, :]
             nc.scalar.copy(repeated[:], src.unsqueeze(2).to_broadcast([P, PACK, QUADS, 32]))
-            back = bank("wg2_back", (4, 3)[half] if u == 1 else half)
+            back = bank("wg2_back", ((4, 5, 4, 5), (3, 4, 1, 2))[half][u])
             for c in range(PACK):
                 nc.tensor.transpose(
                     back[:, P * c : P * (c + 1)], repeated[:, c].rearrange("p g q -> p (g q)"), ident[:]
@@ -163,6 +158,8 @@ def tile_list_terrain_weave_kernel(
                 w2s_raw[32 * q : 32 * q + 4, :].bitcast(I32).rearrange("r (a c) -> r a c", a=2),
                 w2_scales[:, 4 * q : 4 * q + 4, :].bitcast(I32).rearrange("a r c -> r a c"),
             )
+        wg2_rows = [held("wg2_rows%d" % half, [P, BANK], F32) for half in range(2)]
+        nc.sync.dma_start(wg2_rows[0][:], wg2[:, 0:BANK])
         tab2_1 = load_table_words("tab2_1", tab2_words, 1, AT_TAB2)
         list4 = load_list("list4", offs4)
         ident = held("ident", [P, P], F32)
@@ -209,10 +206,13 @@ def tile_list_terrain_weave_kernel(
         def place(u, h, factor, where, cols):
             nc.vector.tensor_tensor(pages[u][:].indirect(where[:, cols.start // 16 : cols.stop // 16]), h, factor, MULT)
 
+        turned = [turn_wg2(0)]
+        for u in range(PACK):
+            deal_wg2(turned[0], u, 0)
+
         HELD_BACK = 256
         kept = slice(0, S - HELD_BACK)
         late = slice(S - HELD_BACK, S)
-        load_wg2(0, (0, 2, 1, 3))
         h2 = [placed("h2_%d" % u, AT_H2 + 4 * u, [P, S], F32) for u in range(PACK)]
 
         def plain_sum(u, cols, width, at_bank):
@@ -232,27 +232,22 @@ def tile_list_terrain_weave_kernel(
 
         FIRST = 256
         low, high = slice(0, BANK), slice(BANK, S)
-        sums_h2 = [(0, slice(0, FIRST), P), (0, slice(FIRST, BANK), P), (0, high, BANK), (1, low, BANK), (1, high, BANK)]
+        sums_h2 = [(0, slice(0, FIRST), P), (1, low, BANK), (0, slice(FIRST, BANK), P), (1, high, BANK), (0, high, BANK)]
         sums_h2.extend([(u, cols, BANK) for u in (2, 3) for cols in (low, high)])
-        wg2_rows = [held("wg2_rows%d" % half, [P, BANK], F32) for half in range(2)]
-        for half in range(2):
-            nc.sync.dma_start(wg2_rows[half][:], wg2[:, BANK * half : BANK * (half + 1)])
+        nc.sync.dma_start(wg2_rows[1][:], wg2[:, BANK:S])
         for n, (u, cols, width) in enumerate(sums_h2):
             if n == 5:
-                turned = []
-                for half in range(2):
-                    turned.append(turn_wg2(half))
-                    deal_wg2(turned[half], 1, half)
-            acc = plain_sum(u, cols, width, (0, 1, 2, 4, 5, 4, 4, 4, 3)[n])
+                turned.append(turn_wg2(1))
+                for page in (1, 0):
+                    deal_wg2(turned[1], page, 1)
+            acc = plain_sum(u, cols, width, (0, 1, 2, 6, 0, 4, 4, 4, 3)[n])
             if (u, cols.stop) == (PACK - 1, S):
                 last_acc = acc
                 cols = slice(BANK, kept.stop)
             nc.scalar.activation(h2[u][:, cols], acc[:, 0 : cols.stop - cols.start], ACT.Abs)
 
-        for cols in (slice(0, FIRST), slice(FIRST, BANK), high):
-            place(0, h2[0][:, cols], wg2_t[0][:, cols], list4, cols)
-        for cols in (low, high):
-            place(1, h2[1][:, cols], wg2_t[1][:, cols], list4, cols)
+        for u, cols, width in sums_h2[0:5]:
+            place(u, h2[u][:, cols], wg2_t[u][:, cols], list4, cols)
 
         def gather_mountain(a):
             words = load_table_words("tab_%d" % a, tab_words, a, AT_TAB)
@@ -269,19 +264,8 @@ def tile_list_terrain_weave_kernel(
                 halves.append([picked[:, P * t : P * (t + 1)] for t in range(PACK)])
             return halves
 
-        for b in range(2):
-            nc.sync.dma_start(
-                gain_rows[PACK * b : PACK * (b + 1), :].rearrange("t (q i) -> t q i", i=8),
-                gain[PASS * b : PASS * (b + 1)].rearrange("(q t i) -> t q i", t=PACK, i=8),
-            )
-        gain_turned = bank("gain_turned", 1)
-        nc.tensor.transpose(gain_turned[:, 0:P], gain_rows[:], ident[:])
-        gains = held("gains", [P, 2 * PACK], F32)
-        nc.scalar.copy(gains[:], gain_turned[:, 0 : 2 * PACK])
-
         for u in (2, 3):
-            for half in range(2):
-                deal_wg2(turned[half], u, half)
+            deal_wg2(turned[1], u, 1)
 
         w1_raw = [placed("w1_raw%d" % a, AT_W1 + 8 * a, [P, PACK, H], F32) for a in range(2)]
         w1_rows = w1.rearrange("(a p j) c -> a p j c", a=2, j=PACK)
@@ -289,6 +273,16 @@ def tile_list_terrain_weave_kernel(
         for a in range(2):
             nc.sync.dma_start(w1_raw[a][:], w1_rows[a])
             weave(w1_woven[:, PACK * H * a : PACK * H * (a + 1)], w1_raw[a][:])
+        for b in range(2):
+            nc.sync.dma_start(
+                gain_rows[PACK * b : PACK * (b + 1), :].rearrange("t (q i) -> t q i", i=8),
+                gain[PASS * b : PASS * (b + 1)].rearrange("(q t i) -> t q i", t=PACK, i=8),
+            )
+        gain_turned = bank("gain_turned", 5)
+        nc.tensor.transpose(gain_turned[:, 0:P], gain_rows[:], ident[:])
+        gains = held("gains", [P, 2 * PACK], F32)
+        nc.scalar.copy(gains[:], gain_turned[:, 0 : 2 * PACK])
+
         v = [gather_mountain(0)]
         w1c = held("w1c", [P, 2 * H], U32)
         w1s = held("w1s", [P, 2 * H], U8)

@@ -24,7 +24,6 @@ PACK = 4
 PASS = P * PACK
 BANK = 512
 QUADS = 4
-ROWS = 96
 
 AT_TAB2 = 0
 AT_TAB = 32
@@ -75,17 +74,18 @@ def tile_list_terrain_weave_kernel(
             engine.memset(dst[:].bitcast(I32), 0)
             return dst
 
-        def load_table_scales(engine, name, src):
+        def load_table_scales(engine, name, src, first):
             dst = held(name, [P, src.shape[2]], U8)
-            nc.sync.dma_start(dst[ROWS:P, :].bitcast(I32), src.bitcast(I32).rearrange("a q t -> q a t"))
-            engine.memset(dst[0:ROWS, :].bitcast(I32), 0)
+            nc.sync.dma_start(dst[first : first + 32, :].bitcast(I32), src.bitcast(I32).rearrange("a q t -> q a t"))
+            for rest in {0: (slice(32, 64), slice(64, P)), 96: (slice(0, 96),)}[first]:
+                engine.memset(dst[rest, :].bitcast(I32), 0)
             return dst
 
-        def spread_scales(queue, dst, src):
+        def spread_scales(queue, dst, src, first):
             for q in range(QUADS):
                 queue.dma_start(
                     dst[32 * q : 32 * q + 4, :].bitcast(I32).rearrange("r (a c) -> r a c", a=2),
-                    src[ROWS + 8 * q : ROWS + 8 * q + 8, :].bitcast(I32),
+                    src[first + 8 * q : first + 8 * q + 8, :].bitcast(I32),
                 )
 
         def load_table_words(name, src, a, at):
@@ -145,34 +145,35 @@ def tile_list_terrain_weave_kernel(
         def quantize(codes, scales, woven):
             nc.vector.quantize_mx(out=codes[:].bitcast(FP8X4), scales=scales[:], in_=woven[:])
 
-        w2s_raw = zeroed(nc.vector, "w2s_raw", 2 * H)
+        w2s_raw = load_table_scales(nc.vector, "w2s_raw", w2_scales, 96)
         list2 = load_list("list2", offs2)
-        sc2 = load_table_scales(nc.vector, "sc2", tab2_scales)
+        sc2 = load_table_scales(nc.vector, "sc2", tab2_scales, 96)
         list1 = load_list("list1", offs)
-        sc1 = load_table_scales(nc.gpsimd, "sc1", tab_scales)
+        sc1 = load_table_scales(nc.gpsimd, "sc1", tab_scales, 0)
+        wg2_rows = [held("wg2_rows%d" % half, [P, BANK], F32) for half in range(2)]
+        nc.sync.dma_start(wg2_rows[0][:], wg2[:, 0:BANK])
         tab2_0 = load_table_words("tab2_0", tab2_words, 0, AT_TAB2)
         w2_raw = held("w2_raw", [P, 2, 2 * H], U8)
         nc.sync.dma_start(w2_raw[:].bitcast(I32), w2_words.bitcast(I32).rearrange("a p c -> p a c"))
-        for q in range(QUADS):
-            nc.sync.dma_start(
-                w2s_raw[32 * q : 32 * q + 4, :].bitcast(I32).rearrange("r (a c) -> r a c", a=2),
-                w2_scales[:, 4 * q : 4 * q + 4, :].bitcast(I32).rearrange("a r c -> r a c"),
-            )
-        wg2_rows = [held("wg2_rows%d" % half, [P, BANK], F32) for half in range(2)]
-        nc.sync.dma_start(wg2_rows[0][:], wg2[:, 0:BANK])
         tab2_1 = load_table_words("tab2_1", tab2_words, 1, AT_TAB2)
         list4 = load_list("list4", offs4)
         ident = held("ident", [P, P], F32)
         make_identity(nc, ident[:])
-        v2_scale = zeroed(nc.gpsimd, "v2_scale", 2 * S)
+        plain_scale = zeroed(nc.gpsimd, "plain_scale", 2 * (S + H))
         v_scale = zeroed(nc.gpsimd, "v_scale", 2 * S)
         w3s = zeroed(nc.gpsimd, "w3s", N)
         gain_rows = held("gain_rows", [P, P], F32)
         nc.gpsimd.memset(gain_rows[:], 0.0)
 
+        plain_rows = held("plain_rows", [P, S + H], U8)
+        nc.vector.tensor_copy(
+            plain_rows[:, S:].rearrange("p (u m) -> p u m", u=PACK),
+            w2s_raw[:].rearrange("p (m u) -> p u m", u=PACK),
+        )
         v2_scale_picked = held("v2_scale_picked", [P, S], U8)
         nc.vector.tensor_copy(v2_scale_picked[:], sc2[:].indirect(list2[:]))
-        spread_scales(nc.sync, v2_scale, v2_scale_picked)
+        nc.vector.tensor_copy(plain_rows[:, 0:S].bitcast(I32), v2_scale_picked[:].bitcast(I32))
+        spread_scales(nc.sync, plain_scale, plain_rows, 96)
         v_scale_sorted = held("v_scale_sorted", [P, S], U8)
 
         def gather_mountain_scales(picked):
@@ -190,11 +191,6 @@ def tile_list_terrain_weave_kernel(
         nc.vector.tensor_copy(
             w2c[:].bitcast(U16).rearrange("p a (u m) -> p a u m", u=PACK),
             w2_raw[:].bitcast(U16).rearrange("p a (m u) -> p a u m", u=PACK),
-        )
-        w2s = held("w2s", [P, 2 * H], U8)
-        nc.gpsimd.tensor_copy(
-            w2s[:].rearrange("p (a u m) -> p a u m", a=2, u=PACK),
-            w2s_raw[:].rearrange("p (a m u) -> p a u m", a=2, u=PACK),
         )
         for half in range(2):
             nc.vector.tensor_copy(
@@ -217,16 +213,17 @@ def tile_list_terrain_weave_kernel(
 
         def plain_sum(u, cols, width, at_bank):
             acc = bank("acc_h2", at_bank)
-            for first in range(cols.start, cols.stop, width):
-                for a in range(2):
+            firsts = range(cols.start, cols.stop, width)
+            for a in range(2):
+                for first in firsts:
                     nc.tensor.matmul_mx(
                         out=acc[:, first - cols.start : first - cols.start + width],
                         lhsT=w2c[:, a, 256 * u : 256 * (u + 1)].bitcast(FP4X4),
-                        lhsT_scale=w2s[:, H * a + P * u : H * a + P * (u + 1)],
+                        lhsT_scale=plain_scale[:, (S + H) * a + S + P * u : (S + H) * a + S + P * (u + 1)],
                         rhs=v2[a][:, first : first + width].bitcast(FP8X4),
-                        rhs_scale=v2_scale[:, S * a + first : S * a + first + width],
-                        start=(a == 0),
-                        stop=(a == 1),
+                        rhs_scale=plain_scale[:, (S + H) * a + first : (S + H) * a + first + width],
+                        start=(a == 0 and first == firsts[0]),
+                        stop=(a == 1 and first == firsts[-1]),
                     )
             return acc
 
@@ -236,10 +233,18 @@ def tile_list_terrain_weave_kernel(
         sums_h2.extend([(u, cols, BANK) for u in (2, 3) for cols in (low, high)])
         nc.sync.dma_start(wg2_rows[1][:], wg2[:, BANK:S])
         for n, (u, cols, width) in enumerate(sums_h2):
-            if n == 5:
+            if n == 2:
                 turned.append(turn_wg2(1))
-                for page in (1, 0):
-                    deal_wg2(turned[1], page, 1)
+                deal_wg2(turned[1], 1, 1)
+            if n == 4:
+                deal_wg2(turned[1], 0, 1)
+            if n == 5:
+                w1_raw = [placed("w1_raw%d" % a, AT_W1 + 8 * a, [P, PACK, H], F32) for a in range(2)]
+                w1_rows = w1.rearrange("(a p j) c -> a p j c", a=2, j=PACK)
+                w1_woven = placed("w1_woven", AT_W1_WOVEN, [P, 2 * PACK * H], BF16)
+                for a in range(2):
+                    nc.sync.dma_start(w1_raw[a][:], w1_rows[a])
+                    weave(w1_woven[:, PACK * H * a : PACK * H * (a + 1)], w1_raw[a][:])
             acc = plain_sum(u, cols, width, (0, 1, 2, 6, 0, 4, 4, 4, 3)[n])
             if (u, cols.stop) == (PACK - 1, S):
                 last_acc = acc
@@ -267,12 +272,6 @@ def tile_list_terrain_weave_kernel(
         for u in (2, 3):
             deal_wg2(turned[1], u, 1)
 
-        w1_raw = [placed("w1_raw%d" % a, AT_W1 + 8 * a, [P, PACK, H], F32) for a in range(2)]
-        w1_rows = w1.rearrange("(a p j) c -> a p j c", a=2, j=PACK)
-        w1_woven = placed("w1_woven", AT_W1_WOVEN, [P, 2 * PACK * H], BF16)
-        for a in range(2):
-            nc.sync.dma_start(w1_raw[a][:], w1_rows[a])
-            weave(w1_woven[:, PACK * H * a : PACK * H * (a + 1)], w1_raw[a][:])
         for b in range(2):
             nc.sync.dma_start(
                 gain_rows[PACK * b : PACK * (b + 1), :].rearrange("t (q i) -> t q i", i=8),
@@ -288,7 +287,7 @@ def tile_list_terrain_weave_kernel(
         w1s = held("w1s", [P, 2 * H], U8)
         quantize(w1c, w1s, w1_woven)
 
-        spread_scales(nc.sync, v_scale, v_scale_sorted)
+        spread_scales(nc.sync, v_scale, v_scale_sorted, 0)
         v.append(gather_mountain(1))
         blend_raw = [load_blend(0)]
 

@@ -24,21 +24,20 @@ PACK = 4
 PASS = P * PACK
 BANK = 512
 QUADS = 4
+UNIT = 256
 
 AT_TAB2 = 0
 AT_TAB = 32
-AT_A_PLANES = 84
-AT_A_WOVEN = 16
-AT_H1 = 64
 AT_W1 = 64
 AT_BLEND = 80
+AT_A_PLANES = 84
 AT_WG2 = 112
 AT_H2 = 128
 AT_V = 144
 AT_W1_WOVEN = 152
 AT_BC = (160, 164, 152)
 AT_WG1 = 168
-AT_PAGE = (0, 8, 56, 48)
+AT_BLEND_WOVEN = 184
 
 
 def tile_list_terrain_weave_kernel(
@@ -74,16 +73,16 @@ def tile_list_terrain_weave_kernel(
             engine.memset(dst[:].bitcast(I32), 0)
             return dst
 
-        def load_table_scales(engine, name, src, first):
+        def load_scale_rows(engine, name, src, first):
             dst = held(name, [P, src.shape[2]], U8)
             nc.sync.dma_start(dst[first : first + 32, :].bitcast(I32), src.bitcast(I32).rearrange("a q t -> q a t"))
             for rest in {0: (slice(32, 64), slice(64, P)), 96: (slice(0, 96),)}[first]:
                 engine.memset(dst[rest, :].bitcast(I32), 0)
             return dst
 
-        def spread_scales(queue, dst, src, first):
+        def spread_scales(dst, src, first):
             for q in range(QUADS):
-                queue.dma_start(
+                nc.sync.dma_start(
                     dst[32 * q : 32 * q + 4, :].bitcast(I32).rearrange("r (a c) -> r a c", a=2),
                     src[first + 8 * q : first + 8 * q + 8, :].bitcast(I32),
                 )
@@ -93,48 +92,8 @@ def tile_list_terrain_weave_kernel(
             nc.sync.dma_start(dst[:].bitcast(I32), src[a].rearrange("p t i -> p (t i)").bitcast(I32))
             return dst
 
-        wg2_t = [placed("wg2_%d" % u, AT_WG2 + 4 * u, [P, S], F32) for u in range(PACK)]
-
-        def turn_wg2(half):
-            turned = bank("wg2_turned", 6 + half)
-            for c in range(PACK):
-                nc.tensor.transpose(turned[:, P * c : P * (c + 1)], wg2_rows[half][:, P * c : P * (c + 1)], ident[:])
-            return turned
-
-        def deal_wg2(turned, u, half):
-            repeated = ring("wg2_repeated", [P, PACK, QUADS, 32], F32)
-            src = turned[:].rearrange("p (c q u) -> p c u q", c=PACK, u=PACK)[:, :, u, :]
-            nc.scalar.copy(repeated[:], src.unsqueeze(2).to_broadcast([P, PACK, QUADS, 32]))
-            back = bank("wg2_back", ((4, 5, 4, 5), (3, 4, 1, 2))[half][u])
-            for c in range(PACK):
-                nc.tensor.transpose(
-                    back[:, P * c : P * (c + 1)], repeated[:, c].rearrange("p g q -> p (g q)"), ident[:]
-                )
-            nc.scalar.copy(wg2_t[u][:, BANK * half : BANK * (half + 1)], back[:])
-
-        wg1_t = placed("wg1", AT_WG1, [P, PACK, S], F32)
-
-        def load_wg1(half):
-            cols = slice(BANK * half, BANK * (half + 1))
-            rows = wg1.rearrange("(q t) m -> q t m", t=PACK)[:, :, cols]
-            for q in (0, 2, 1, 3):
-                nc.sync.dma_start(wg1_t[32 * q : 32 * q + 32, :, cols], rows)
-
-        pieces = [slice(0, 256), slice(256, 512), slice(512, 1024)]
-
-        def blend_at(i, b):
-            return AT_BLEND + ((4, 8), (0, 12), (16, 24))[i][b]
-
-        def load_blend(i):
-            raw = []
-            cols = pieces[i]
-            for b in range(2):
-                raw.append(placed("blend_raw%d%d" % (i, b), blend_at(i, b), [P, PACK, cols.stop - cols.start], F32))
-                rows = blend[PASS * b : PASS * (b + 1), cols]
-                rows = rows.rearrange("(q t i) m -> t q i m", t=PACK, i=8)
-                for t in range(PACK):
-                    nc.sync.dma_start(raw[b][:, t, :], rows[t])
-            return raw
+        def entries(lst, cols):
+            return lst[:, cols.start // 16 : cols.stop // 16]
 
         def weave(dst, planes):
             nc.scalar.copy(
@@ -143,15 +102,17 @@ def tile_list_terrain_weave_kernel(
             )
 
         def quantize(codes, scales, woven):
-            nc.vector.quantize_mx(out=codes[:].bitcast(FP8X4), scales=scales[:], in_=woven[:])
+            nc.vector.quantize_mx(out=codes.bitcast(FP8X4), scales=scales, in_=woven)
 
-        w2s_raw = load_table_scales(nc.vector, "w2s_raw", w2_scales, 96)
+        low, high = slice(0, BANK), slice(BANK, S)
+
+        w2s_raw = load_scale_rows(nc.vector, "w2s_raw", w2_scales, 96)
         list2 = load_list("list2", offs2)
-        sc2 = load_table_scales(nc.vector, "sc2", tab2_scales, 96)
+        sc2 = load_scale_rows(nc.vector, "sc2", tab2_scales, 96)
         list1 = load_list("list1", offs)
-        sc1 = load_table_scales(nc.gpsimd, "sc1", tab_scales, 0)
+        sc1 = load_scale_rows(nc.gpsimd, "sc1", tab_scales, 0)
         wg2_rows = [held("wg2_rows%d" % half, [P, BANK], F32) for half in range(2)]
-        nc.sync.dma_start(wg2_rows[0][:], wg2[:, 0:BANK])
+        nc.sync.dma_start(wg2_rows[0][:], wg2[:, low])
         tab2_0 = load_table_words("tab2_0", tab2_words, 0, AT_TAB2)
         w2_raw = held("w2_raw", [P, 2, 2 * H], U8)
         nc.sync.dma_start(w2_raw[:].bitcast(I32), w2_words.bitcast(I32).rearrange("a p c -> p a c"))
@@ -173,17 +134,15 @@ def tile_list_terrain_weave_kernel(
         v2_scale_picked = held("v2_scale_picked", [P, S], U8)
         nc.vector.tensor_copy(v2_scale_picked[:], sc2[:].indirect(list2[:]))
         nc.vector.tensor_copy(plain_rows[:, 0:S].bitcast(I32), v2_scale_picked[:].bitcast(I32))
-        spread_scales(nc.sync, plain_scale, plain_rows, 96)
-        v_scale_sorted = held("v_scale_sorted", [P, S], U8)
+        spread_scales(plain_scale, plain_rows, 96)
 
-        def gather_mountain_scales(picked):
-            nc.vector.tensor_copy(picked[:], sc1[:].indirect(list1[:]))
-            nc.vector.tensor_copy(
-                v_scale_sorted[:].bitcast(I32).rearrange("p (t q w) -> p t q w", t=PACK, w=2),
-                picked[:].bitcast(I32).rearrange("p (q t w) -> p t q w", t=PACK, w=2),
-            )
-
-        gather_mountain_scales(held("v_scale_picked", [P, S], U8))
+        v_scale_picked = held("v_scale_picked", [P, S], U8)
+        nc.vector.tensor_copy(v_scale_picked[:], sc1[:].indirect(list1[:]))
+        v_scale_sorted = placed("v_scale_sorted", AT_H2 + 6, [P, S], U8)
+        nc.vector.tensor_copy(
+            v_scale_sorted[:].bitcast(I32).rearrange("p (t q w) -> p t q w", t=PACK, w=2),
+            v_scale_picked[:].bitcast(I32).rearrange("p (q t w) -> p t q w", t=PACK, w=2),
+        )
 
         v2 = [placed("v2_%d" % a, AT_V + 4 * a, [P, S], U32) for a in range(2)]
         nc.vector.tensor_copy(v2[0][:], tab2_0[:].indirect(list2[:]))
@@ -192,85 +151,90 @@ def tile_list_terrain_weave_kernel(
             w2c[:].bitcast(U16).rearrange("p a (u m) -> p a u m", u=PACK),
             w2_raw[:].bitcast(U16).rearrange("p a (m u) -> p a u m", u=PACK),
         )
-        for half in range(2):
-            nc.vector.tensor_copy(
-                v2[1][:, BANK * half : BANK * (half + 1)], tab2_1[:].indirect(list2[:, 32 * half : 32 * (half + 1)])
-            )
+        for cols in (slice(0, UNIT), slice(UNIT, S)):
+            nc.vector.tensor_copy(v2[1][:, cols], tab2_1[:].indirect(entries(list2, cols)))
 
-        pages = [placed("page%d" % u, AT_PAGE[u], [P, T2], F32) for u in range(PACK)]
+        pages = [placed("page%d" % u, AT_TAB2 + 8 * u, [P, T2], F32) for u in range(PACK)]
 
-        def place(u, h, factor, where, cols):
-            nc.vector.tensor_tensor(pages[u][:].indirect(where[:, cols.start // 16 : cols.stop // 16]), h, factor, MULT)
+        def place(u, h, factor, lst, cols):
+            nc.vector.tensor_tensor(pages[u][:].indirect(entries(lst, cols)), h, factor, MULT)
 
-        turned = [turn_wg2(0)]
+        wg2_t = [placed("wg2_%d" % u, AT_WG2 + 4 * u, [P, S], F32) for u in range(PACK)]
+
+        def turn_wg2(half):
+            turned = bank("wg2_turned", 6 + half)
+            for c in range(PACK):
+                nc.tensor.transpose(turned[:, P * c : P * (c + 1)], wg2_rows[half][:, P * c : P * (c + 1)], ident[:])
+            return turned
+
+        def deal_wg2(turned, u, cols):
+            repeated = ring("wg2_repeated", [P, PACK, QUADS, 32], F32)
+            src = turned[:].rearrange("p (c q u) -> p c u q", c=PACK, u=PACK)[:, :, u, :]
+            nc.scalar.copy(repeated[:], src.unsqueeze(2).to_broadcast([P, PACK, QUADS, 32]))
+            back = bank("wg2_back", 4 + u % 2)
+            for c in range(PACK):
+                nc.tensor.transpose(
+                    back[:, P * c : P * (c + 1)], repeated[:, c].rearrange("p g q -> p (g q)"), ident[:]
+                )
+            nc.scalar.copy(wg2_t[u][:, cols], back[:])
+
+        turned = turn_wg2(0)
         for u in range(PACK):
-            deal_wg2(turned[0], u, 0)
+            deal_wg2(turned, u, low)
 
-        HELD_BACK = 256
-        kept = slice(0, S - HELD_BACK)
-        late = slice(S - HELD_BACK, S)
-        h2 = [placed("h2_%d" % u, AT_H2 + 4 * u, [P, S], F32) for u in range(PACK)]
-
-        def plain_sum(u, cols, width, at_bank):
-            acc = bank("acc_h2", at_bank)
-            firsts = range(cols.start, cols.stop, width)
+        def plain_sum(acc, u, cols):
             for a in range(2):
-                for first in firsts:
-                    nc.tensor.matmul_mx(
-                        out=acc[:, first - cols.start : first - cols.start + width],
-                        lhsT=w2c[:, a, 256 * u : 256 * (u + 1)].bitcast(FP4X4),
-                        lhsT_scale=plain_scale[:, (S + H) * a + S + P * u : (S + H) * a + S + P * (u + 1)],
-                        rhs=v2[a][:, first : first + width].bitcast(FP8X4),
-                        rhs_scale=plain_scale[:, (S + H) * a + first : (S + H) * a + first + width],
-                        start=(a == 0 and first == firsts[0]),
-                        stop=(a == 1 and first == firsts[-1]),
-                    )
-            return acc
+                nc.tensor.matmul_mx(
+                    out=acc,
+                    lhsT=w2c[:, a, 256 * u : 256 * (u + 1)].bitcast(FP4X4),
+                    lhsT_scale=plain_scale[:, (S + H) * a + S + P * u : (S + H) * a + S + P * (u + 1)],
+                    rhs=v2[a][:, cols].bitcast(FP8X4),
+                    rhs_scale=plain_scale[:, (S + H) * a + cols.start : (S + H) * a + cols.stop],
+                    start=(a == 0),
+                    stop=(a == 1),
+                )
 
-        FIRST = 256
-        low, high = slice(0, BANK), slice(BANK, S)
-        sums_h2 = [(0, slice(0, FIRST), P), (1, low, BANK), (0, slice(FIRST, BANK), P), (1, high, BANK), (0, high, BANK)]
-        sums_h2.extend([(u, cols, BANK) for u in (2, 3) for cols in (low, high)])
-        nc.sync.dma_start(wg2_rows[1][:], wg2[:, BANK:S])
-        for n, (u, cols, width) in enumerate(sums_h2):
-            if n == 2:
-                turned.append(turn_wg2(1))
-                deal_wg2(turned[1], 1, 1)
-            if n == 4:
-                deal_wg2(turned[1], 0, 1)
-            if n == 5:
-                w1_raw = [placed("w1_raw%d" % a, AT_W1 + 8 * a, [P, PACK, H], F32) for a in range(2)]
-                w1_rows = w1.rearrange("(a p j) c -> a p j c", a=2, j=PACK)
-                w1_woven = placed("w1_woven", AT_W1_WOVEN, [P, 2 * PACK * H], BF16)
-                for a in range(2):
-                    nc.sync.dma_start(w1_raw[a][:], w1_rows[a])
-                    weave(w1_woven[:, PACK * H * a : PACK * H * (a + 1)], w1_raw[a][:])
-            acc = plain_sum(u, cols, width, (0, 1, 2, 6, 0, 4, 4, 4, 3)[n])
-            if (u, cols.stop) == (PACK - 1, S):
-                last_acc = acc
-                cols = slice(BANK, kept.stop)
-            nc.scalar.activation(h2[u][:, cols], acc[:, 0 : cols.stop - cols.start], ACT.Abs)
+        first, second = slice(0, UNIT), slice(UNIT, BANK)
+        for u in range(2):
+            acc = bank("acc_h2", u)
+            plain_sum(acc[:, 0:UNIT], u, first)
+            h = placed("h2_first%d" % u, AT_H2 + u, [P, UNIT], F32)
+            nc.scalar.activation(h[:], acc[:, 0:UNIT], ACT.Abs)
+            place(u, h[:], wg2_t[u][:, first], list4, first)
+        acc = bank("acc_h2", 2)
+        plain_sum(acc[:], 2, low)
+        h = placed("h2_low2", AT_H2 + 2, [P, BANK], F32)
+        nc.scalar.activation(h[:], acc[:], ACT.Abs)
+        place(2, h[:], wg2_t[2][:, low], list4, low)
+        acc = bank("acc_h2", 6)
+        for u in range(2):
+            plain_sum(acc[:, UNIT * u : UNIT * (u + 1)], u, second)
+        h = placed("h2_second", AT_H2 + 4, [P, BANK], F32)
+        nc.scalar.activation(h[:], acc[:], ACT.Abs)
+        for u in range(2):
+            place(u, h[:, UNIT * u : UNIT * (u + 1)], wg2_t[u][:, second], list4, second)
 
-        for u, cols, width in sums_h2[0:5]:
-            place(u, h2[u][:, cols], wg2_t[u][:, cols], list4, cols)
+        nc.sync.dma_start(wg2_rows[1][:], wg2[:, high])
+        w1_raw = [placed("w1_raw%d" % a, AT_W1 + 8 * a, [P, PACK, H], F32) for a in range(2)]
+        w1_rows = w1.rearrange("(a p j) c -> a p j c", a=2, j=PACK)
+        w1_woven = placed("w1_woven", AT_W1_WOVEN, [P, 2 * PACK * H], BF16)
+        for a in range(2):
+            nc.sync.dma_start(w1_raw[a][:], w1_rows[a])
+            weave(w1_woven[:, PACK * H * a : PACK * H * (a + 1)], w1_raw[a][:])
 
-        def gather_mountain(a):
-            words = load_table_words("tab_%d" % a, tab_words, a, AT_TAB)
-            if a == 0:
-                picked = placed("v_0", AT_V, [P, S], U32)
-                dst = picked[:].rearrange("p (t q i) -> p q t i", t=PACK, i=8)
-                nc.vector.tensor_copy(dst, words[:].indirect(list1[:]))
-                return [[picked[:, 2 * P * t + P * b : 2 * P * t + P * (b + 1)] for t in range(PACK)] for b in range(2)]
-            halves = []
-            for b in range(2):
-                picked = placed("v_1%d" % b, AT_V + 4 + 2 * b, [P, PASS], U32)
-                dst = picked[:].rearrange("p (t q i) -> p q t i", t=PACK, i=8)
-                nc.vector.tensor_copy(dst, words[:].indirect(list1[:, 32 * b : 32 * (b + 1)]))
-                halves.append([picked[:, P * t : P * (t + 1)] for t in range(PACK)])
-            return halves
+        waiting = [(3, low), (0, high), (1, high), (2, high)]
+        acc_waiting = []
+        for n, (u, cols) in enumerate(waiting):
+            acc_waiting.append(bank("acc_h2", n))
+            plain_sum(acc_waiting[n][:], u, cols)
+        acc = bank("acc_h2", 6)
+        plain_sum(acc[:], 3, high)
+        h2_last = placed("h2_last", AT_H2 + 13, [P, BANK], F32)
+        nc.scalar.activation(h2_last[:], acc[:], ACT.Abs)
 
-        for u in (2, 3):
-            deal_wg2(turned[1], u, 1)
+        turned = turn_wg2(1)
+        for u in range(PACK):
+            deal_wg2(turned, u, high)
 
         for b in range(2):
             nc.sync.dma_start(
@@ -282,39 +246,69 @@ def tile_list_terrain_weave_kernel(
         gains = held("gains", [P, 2 * PACK], F32)
         nc.scalar.copy(gains[:], gain_turned[:, 0 : 2 * PACK])
 
-        v = [gather_mountain(0)]
+        tab_0 = load_table_words("tab_0", tab_words, 0, AT_TAB)
+        v_0 = placed("v_0", AT_V, [P, S], U32)
+        nc.vector.tensor_copy(v_0[:].rearrange("p (t q i) -> p q t i", t=PACK, i=8), tab_0[:].indirect(list1[:]))
+        v = [[[v_0[:, 2 * P * t + P * b : 2 * P * t + P * (b + 1)] for t in range(PACK)] for b in range(2)], []]
         w1c = held("w1c", [P, 2 * H], U32)
         w1s = held("w1s", [P, 2 * H], U8)
-        quantize(w1c, w1s, w1_woven)
+        quantize(w1c[:], w1s[:], w1_woven[:])
+        tab_1 = load_table_words("tab_1", tab_words, 1, AT_TAB)
+        for b, cols in enumerate((low, high)):
+            v_1 = placed("v_1%d" % b, AT_V + 4 + 2 * b, [P, PASS], U32)
+            nc.vector.tensor_copy(
+                v_1[:].rearrange("p (t q i) -> p q t i", t=PACK, i=8), tab_1[:].indirect(entries(list1, cols))
+            )
+            v[1].append([v_1[:, P * t : P * (t + 1)] for t in range(PACK)])
+        spread_scales(v_scale, v_scale_sorted, 0)
 
-        spread_scales(nc.sync, v_scale, v_scale_sorted, 0)
-        v.append(gather_mountain(1))
+        z_pairs = placed("z_pairs", AT_TAB + 16, [P, 2 * T2 * 2], BF16)
+        nc.gpsimd.memset(z_pairs[:, 2 * T2 :].bitcast(I32), 0)
+
+        h2_waiting = placed("h2_waiting", AT_H2 + 6, [P, 3 * BANK + UNIT], F32)
+        kept, late = slice(BANK, S - UNIT), slice(S - UNIT, S)
+        for n, (u, cols) in enumerate(waiting):
+            if u == 2:
+                cols = kept
+            width = cols.stop - cols.start
+            h = h2_waiting[:, BANK * n : BANK * n + width]
+            nc.scalar.activation(h, acc_waiting[n][:, 0:width], ACT.Abs)
+            place(u, h, wg2_t[u][:, cols], list4, cols)
+
+        pieces = [slice(0, UNIT), slice(UNIT, BANK), high]
+
+        def blend_at(i, b):
+            return AT_BLEND + ((4, 8), (0, 12), (16, 24))[i][b]
+
+        def load_blend(i):
+            raw = []
+            cols = pieces[i]
+            for b in range(2):
+                raw.append(placed("blend_raw%d%d" % (i, b), blend_at(i, b), [P, PACK, cols.stop - cols.start], F32))
+                rows = blend[PASS * b : PASS * (b + 1), cols]
+                rows = rows.rearrange("(q t i) m -> t q i m", t=PACK, i=8)
+                for t in range(PACK):
+                    nc.sync.dma_start(raw[b][:, t, :], rows[t])
+            return raw
+
         blend_raw = [load_blend(0)]
-
-        woven_at = [AT_WG1 + 16, AT_A_PLANES + 4, blend_at(1, 0)]
+        woven_at = [AT_BLEND_WOVEN, AT_A_PLANES + 4, blend_at(1, 0)]
         bc, bs = [], []
 
         def quantize_blend(i):
-            cols = pieces[i]
-            width = cols.stop - cols.start
+            width = pieces[i].stop - pieces[i].start
             woven = placed("blend_woven%d" % i, woven_at[i], [P, 2 * PACK * width], BF16)
             for b in range(2):
                 weave(woven[:, PACK * width * b : PACK * width * (b + 1)], blend_raw[i][b][:])
             bc.append(placed("bc%d" % i, AT_BC[i], [P, 2 * width], U32))
-            if i == 0:
-                bs.append(held("bs0", [P, 2 * width], U8))
-            else:
-                bs.append(placed("bs%d" % i, AT_H1 + 4 * (i - 1), [P, 2 * width], U8))
-            quantize(bc[i], bs[i], woven)
-
-        place(2, h2[2][:], wg2_t[2][:], list4, slice(0, S))
-        place(3, h2[3][:, kept], wg2_t[3][:, kept], list4, kept)
+            bs.append(held("bs%d" % i, [P, 2 * width], U8))
+            quantize(bc[i][:], bs[i][:], woven[:])
 
         quantize_blend(0)
 
         a_planes = placed("a_planes", AT_A_PLANES, [P, 2, PACK, H], BF16)
-        a_woven = placed("a_woven", AT_A_WOVEN, [P, 2 * PACK * H], BF16)
-        a_banks = (0, 1, 2, 4, 5, 6, 7, 0)
+        a_woven = placed("a_woven", AT_TAB, [P, 2 * PACK * H], BF16)
+        a_banks = (4, 5, 6, 7, 0, 1, 2, 4)
         acc_a = {}
 
         def project(b, t, a):
@@ -331,30 +325,33 @@ def tile_list_terrain_weave_kernel(
                 stop=(a == 1),
             )
 
-        slots = [(b, t) for b in range(2) for t in range(PACK)]
-        for t in range(2):
-            project(0, t, 0)
-        for b, t in slots:
-            if (b, t) > (0, 1):
+        for b in range(2):
+            for t in range(PACK):
                 project(b, t, 0)
-            project(b, t, 1)
-            nc.scalar.activation(
-                a_planes[:, b, t, :].rearrange("p (u m) -> p u m", u=PACK),
-                acc_a[b, t][:].rearrange("p (m u) -> p u m", u=PACK),
-                ACT.Copy,
-                scale=gains[:, PACK * b + t : PACK * b + t + 1],
-            )
-            if t == PACK - 1:
-                weave(a_woven[:, PACK * H * b : PACK * H * (b + 1)], a_planes[:, b])
+                project(b, t, 1)
+                nc.scalar.activation(
+                    a_planes[:, b, t, :].rearrange("p (u m) -> p u m", u=PACK),
+                    acc_a[b, t][:].rearrange("p (m u) -> p u m", u=PACK),
+                    ACT.Copy,
+                    scale=gains[:, PACK * b + t : PACK * b + t + 1],
+                )
+            weave(a_woven[:, PACK * H * b : PACK * H * (b + 1)], a_planes[:, b])
         ac = held("ac", [P, 2 * H], U32)
         asc = held("asc", [P, 2 * H], U8)
-        quantize(ac, asc, a_woven)
+        quantize(ac[:], asc[:], a_woven[:])
 
         list3 = load_list("list3", offs3)
+        wg1_t = placed("wg1", AT_WG1, [P, PACK, S], F32)
+
+        def load_wg1(cols):
+            rows = wg1.rearrange("(q t) m -> q t m", t=PACK)[:, :, cols]
+            for q in (0, 2, 1, 3):
+                nc.sync.dma_start(wg1_t[32 * q : 32 * q + 32, :, cols], rows)
+
         blend_raw.append(load_blend(1))
-        load_wg1(0)
+        load_wg1(low)
         blend_raw.append(load_blend(2))
-        load_wg1(1)
+        load_wg1(high)
         biases = held("biases", [P, PACK], F32)
         nc.sync.dma_start(biases[:], bias.rearrange("(p t) -> p t", t=PACK))
         w3c = held("w3c", [P, N], U32)
@@ -362,14 +359,16 @@ def tile_list_terrain_weave_kernel(
         for q in range(QUADS):
             nc.sync.dma_start(w3s[32 * q : 32 * q + 4, :].bitcast(I32), w3_scales[0, 4 * q : 4 * q + 4, :].bitcast(I32))
 
-        acc_h1 = {}
+        h2_late = placed("h2_late", AT_A_PLANES, [P, UNIT], F32)
+        nc.scalar.activation(h2_late[:], acc_waiting[3][:, BANK - UNIT : BANK], ACT.Abs)
+        place(2, h2_late[:], wg2_t[2][:, late], list4, late)
 
         def blended_sum(i, u):
             width = pieces[i].stop - pieces[i].start
-            acc_h1[i, u] = bank("acc_h1", PACK * ((i + 1) % 2) + u)[:, 0:width]
+            acc = bank("acc_h1", PACK * ((i + 1) % 2) + u)[:, 0:width]
             for b in range(2):
                 nc.tensor.matmul_mx(
-                    out=acc_h1[i, u],
+                    out=acc,
                     lhsT=ac[:, H * b + P * u : H * b + P * (u + 1)].bitcast(FP8X4),
                     lhsT_scale=asc[:, H * b + P * u : H * b + P * (u + 1)],
                     rhs=bc[i][:, width * b : width * (b + 1)].bitcast(FP8X4),
@@ -377,94 +376,104 @@ def tile_list_terrain_weave_kernel(
                     start=(b == 0),
                     stop=(b == 1),
                 )
+            return acc
 
-        def place_blended(i, u, at):
-            cols = pieces[i]
-            h = placed("h1_%d%d" % (i, u), at, [P, cols.stop - cols.start], F32)
-            nc.scalar.copy(h[:], acc_h1[i, u])
-            place(u, h[:], wg1_t[:, u, cols], list3, cols)
-
-        h2_late = placed("h2_late", AT_A_PLANES, [P, HELD_BACK], F32)
-        nc.scalar.activation(h2_late[:], last_acc[:, BANK - HELD_BACK : BANK], ACT.Abs)
-        place(3, h2_late[:], wg2_t[3][:, late], list4, late)
-
-        z_pairs = placed("z_pairs", AT_WG2, [P, 2 * T2 * 2], BF16)
-
-        def z_slot(u, cols):
-            return z_pairs[:].rearrange("p (h t e) -> p h t e", h=2, e=2)[:, u // 2, cols, u % 2]
-
-        def relu(u, cols):
-            nc.scalar.activation(z_slot(u, cols), pages[u][:, cols], ACT.Relu, bias=biases[:, u : u + 1])
-
+        h1_at = [
+            (AT_W1, AT_W1 + 1, blend_at(1, 1), blend_at(1, 1) + 1),
+            (AT_W1 + 4, blend_at(2, 1), blend_at(2, 1) + 1),
+            (AT_W1 + 6, AT_W1 + 8, AT_W1 + 10),
+        ]
+        h1_last = placed("h1_last", AT_W1 + 12, [P, S - UNIT], F32)
         for i, cols in enumerate(pieces):
+            sums = [blended_sum(i, u) for u in range(PACK)]
             for u in range(PACK):
-                blended_sum(i, u)
-            for u in range(PACK):
-                at = AT_H1 + 4 * i + (cols.stop - cols.start) // 256 * u
-                if u >= 2 and i + 1 < len(pieces):
-                    at = blend_at(i + 1, 1) + u - 2
-                place_blended(i, u, at)
+                if u < len(h1_at[i]):
+                    h = placed("h1_%d%d" % (i, u), h1_at[i][u], [P, cols.stop - cols.start], F32)
+                    nc.scalar.copy(h[:], sums[u])
+                    place(u, h[:], wg1_t[:, u, cols], list3, cols)
+                else:
+                    nc.scalar.copy(h1_last[:, cols.start - UNIT : cols.stop - UNIT], sums[u])
                 if u == 0 and i + 1 < len(pieces):
                     quantize_blend(i + 1)
-        for u in range(2):
-            relu(u, slice(0, T2))
-        last_bias = []
-        for half in range(2):
-            relu(2, slice(S * half, S * (half + 1)))
-            last_bias.append(placed("last_bias%d" % half, AT_PAGE[1 + half], [P, 1], F32))
-            nc.scalar.copy(last_bias[half][:], biases[:, 3:4])
+        place(3, h1_last[:], wg1_t[:, 3, UNIT:S], list3, slice(UNIT, S))
+        place(3, h2_last[:], wg2_t[3][:, high], list4, high)
 
-        widths = [128, 128, 256, 512, 512, 512]
-        on_vector = [(), (), (), (), (3,), (1, 3)]
-        chunks = [slice(sum(widths[:c]), sum(widths[: c + 1])) for c in range(len(widths))]
-        out_rows = out.rearrange("(nb p) t -> p nb t", p=P)
+        for u in range(PACK - 1):
+            nc.scalar.activation(
+                z_pairs[:].rearrange("p (h t e) -> p h t e", h=2, e=2)[:, u // 2, :, u % 2],
+                pages[u][:], ACT.Relu, bias=biases[:, u : u + 1],
+            )
         pair_words = z_pairs[:].bitcast(F32).rearrange("p (h t) -> p t h", h=2)
-        z_woven, zc, zs = {}, {}, {}
+        groups = [(128, 128), (256, 256), (256, 512, 512)]
+        widths = [width for group in groups for width in group]
+        parts = [slice(sum(widths[:c]), sum(widths[: c + 1])) for c in range(len(widths))]
+        z_part = []
+        for group in groups:
+            start = parts[len(z_part)].start
+            woven = placed("z_woven%d" % start, AT_TAB + start * PACK * 2 // 1024, [P, PACK * sum(group)], BF16)
+            nc.scalar.copy(
+                woven[:].bitcast(F32).rearrange("p (t h) -> p t h", h=2), pair_words[:, start : start + sum(group), :]
+            )
+            for cols in parts[len(z_part) : len(z_part) + len(group)]:
+                z_part.append(woven[:, PACK * (cols.start - start) : PACK * (cols.stop - start)])
+
+        zc = placed("zc", AT_H2, [P, T2], U32)
+        zs = held("zs", [P, T2], U8)
+        out_rows = out.rearrange("(nb p) t -> p nb t", p=P)
 
         def last_relu(c):
-            cols = chunks[c]
-            nc.vector.tensor_scalar(z_slot(3, cols), pages[3][:, cols], last_bias[cols.start // S][:], 0.0, ADD, MAX)
-
-        def weave_z(c):
-            z_woven[c] = placed("z_woven%d" % c, AT_W1 + chunks[c].start * PACK * 2 // 1024, [P, PACK * widths[c]], BF16)
-            nc.vector.tensor_copy(
-                z_woven[c][:].bitcast(F32).rearrange("p (t h) -> p t h", h=2), pair_words[:, chunks[c], :]
+            nc.vector.tensor_scalar(
+                z_part[c].rearrange("p (t u) -> p t u", u=PACK)[:, :, PACK - 1],
+                pages[PACK - 1][:, parts[c]], biases[:, PACK - 1 : PACK], 0.0, ADD, MAX,
             )
 
-        def quantize_z(c):
-            zc[c] = placed("zc%d" % c, AT_H2 + chunks[c].start * 4 / 1024, [P, widths[c]], U32)
-            zs[c] = held("zs%d" % c, [P, widths[c]], U8)
-            quantize(zc[c], zs[c], z_woven[c])
+        def product(acc, nb, cols):
+            nc.tensor.matmul_mx(
+                out=acc,
+                lhsT=w3c[:, P * nb : P * (nb + 1)].bitcast(FP8X4),
+                lhsT_scale=w3s[:, P * nb : P * (nb + 1)],
+                rhs=zc[:, cols].bitcast(FP8X4),
+                rhs_scale=zs[:, cols],
+                start=True,
+                stop=True,
+            )
 
-        def features(c):
-            cols, width = chunks[c], widths[c]
-            staged = placed("staged%d" % c, AT_BLEND + cols.start * PACK * 4 // 1024, [P, PACK, width], F32)
-            together = BANK // width
-            for g in range(PACK // together):
-                acc = bank("acc_out", (cols.start * PACK // BANK + g) % 8)
-                blocks = slice(together * g, together * (g + 1))
-                for nb in range(blocks.start, blocks.stop):
-                    nc.tensor.matmul_mx(
-                        out=acc[:, width * (nb - blocks.start) : width * (nb - blocks.start + 1)],
-                        lhsT=w3c[:, P * nb : P * (nb + 1)].bitcast(FP8X4),
-                        lhsT_scale=w3s[:, P * nb : P * (nb + 1)],
-                        rhs=zc[c][:].bitcast(FP8X4),
-                        rhs_scale=zs[c][:],
-                        start=True,
-                        stop=True,
-                    )
-                copy = nc.vector.tensor_copy if g in on_vector[c] else nc.scalar.copy
-                copy(staged[:, blocks, :].rearrange("p b t -> p (b t)"), acc[:])
+        filled = []
+
+        def narrow_features(cols, step):
+            staged = placed("staged%d" % cols.start, AT_BLEND + cols.start * PACK * 4 // 1024, [P, PACK, UNIT], F32)
+            for pair in range(2):
+                acc = bank("acc_out", len(filled) % 8)
+                filled.append(acc)
+                for first in range(0, UNIT, step):
+                    for e in range(2):
+                        product(
+                            acc[:, UNIT * e + first : UNIT * e + first + step], 2 * pair + e,
+                            slice(cols.start + first, cols.start + first + step),
+                        )
+                blocks = slice(2 * pair, 2 * pair + 2)
+                nc.scalar.copy(staged[:, blocks, :].rearrange("p b t -> p (b t)"), acc[:])
                 nc.sync.dma_start(out_rows[:, blocks, cols], staged[:, blocks, :])
 
-        last_relu(0)
-        last_relu(1)
-        weave_z(0)
-        weave_z(1)
-        for c in range(len(chunks)):
-            quantize_z(c)
-            if 0 < c < len(chunks) - 1:
-                weave_z(c + 1)
-            if c + 2 < len(chunks):
-                last_relu(c + 2)
-            features(c)
+        def wide_features():
+            staged = placed("staged_wide", AT_BLEND + S * PACK * 4 // 1024, [P, PACK, S], F32)
+            for nb in range(PACK):
+                for half, copy in enumerate((nc.scalar.copy, nc.vector.tensor_copy)):
+                    acc = bank("acc_out", len(filled) % 8)
+                    filled.append(acc)
+                    product(acc[:], nb, slice(S + BANK * half, S + BANK * (half + 1)))
+                    copy(staged[:, nb, BANK * half : BANK * (half + 1)], acc[:])
+                nc.sync.dma_start(out_rows[:, nb, S:T2], staged[:, nb, :])
+
+        done = 0
+        for group in groups:
+            mine = range(done, done + len(group))
+            done = mine.stop
+            for c in mine:
+                last_relu(c)
+            for c in mine:
+                quantize(zc[:, parts[c]], zs[:, parts[c]], z_part[c])
+        narrow_features(slice(0, UNIT), P)
+        for first in range(UNIT, S, UNIT):
+            narrow_features(slice(first, first + UNIT), UNIT)
+        wide_features()

@@ -34,10 +34,11 @@ AT_A_PLANES = 84
 AT_WG2 = 112
 AT_H2 = 128
 AT_V = 144
-AT_W1_WOVEN = 152
-AT_BC = (160, 164, 152)
-AT_WG1 = 168
-AT_BLEND_WOVEN = 184
+AT_SCALES = 152
+AT_BC = (152, 154, 156)
+AT_BLEND_WOVEN = 160
+AT_WG1 = 164
+AT_Z_PAIRS = 180
 
 
 def tile_list_terrain_weave_kernel(
@@ -73,8 +74,7 @@ def tile_list_terrain_weave_kernel(
             engine.memset(dst[:].bitcast(I32), 0)
             return dst
 
-        def load_scale_rows(engine, name, src, first):
-            dst = held(name, [P, src.shape[2]], U8)
+        def load_scale_rows(engine, dst, src, first):
             nc.sync.dma_start(dst[first : first + 32, :].bitcast(I32), src.bitcast(I32).rearrange("a q t -> q a t"))
             for rest in {0: (slice(32, 64), slice(64, P)), 96: (slice(0, 96),)}[first]:
                 engine.memset(dst[rest, :].bitcast(I32), 0)
@@ -106,11 +106,11 @@ def tile_list_terrain_weave_kernel(
 
         low, high = slice(0, BANK), slice(BANK, S)
 
-        w2s_raw = load_scale_rows(nc.vector, "w2s_raw", w2_scales, 96)
+        w2s_raw = load_scale_rows(nc.vector, held("w2s_raw", [P, H], U8), w2_scales, 96)
         list2 = load_list("list2", offs2)
-        sc2 = load_scale_rows(nc.vector, "sc2", tab2_scales, 96)
+        sc2 = load_scale_rows(nc.vector, placed("sc2", AT_SCALES, [P, T], U8), tab2_scales, 96)
         list1 = load_list("list1", offs)
-        sc1 = load_scale_rows(nc.gpsimd, "sc1", tab_scales, 0)
+        sc1 = load_scale_rows(nc.gpsimd, placed("sc1", AT_SCALES + 4, [P, T], U8), tab_scales, 0)
         wg2_rows = [held("wg2_rows%d" % half, [P, BANK], F32) for half in range(2)]
         nc.sync.dma_start(wg2_rows[0][:], wg2[:, low])
         tab2_0 = load_table_words("tab2_0", tab2_words, 0, AT_TAB2)
@@ -214,23 +214,25 @@ def tile_list_terrain_weave_kernel(
         for u in range(2):
             place(u, h[:, UNIT * u : UNIT * (u + 1)], wg2_t[u][:, second], list4, second)
 
+        acc_low3 = bank("acc_h2", 0)
+        plain_sum(acc_low3[:], 3, low)
+        h = placed("h2_first3", AT_H2 + 14, [P, UNIT], F32)
+        nc.scalar.activation(h[:], acc_low3[:, first], ACT.Abs)
+        place(3, h[:], wg2_t[3][:, first], list4, first)
+
         nc.sync.dma_start(wg2_rows[1][:], wg2[:, high])
         w1_raw = [placed("w1_raw%d" % a, AT_W1 + 8 * a, [P, PACK, H], F32) for a in range(2)]
         w1_rows = w1.rearrange("(a p j) c -> a p j c", a=2, j=PACK)
-        w1_woven = placed("w1_woven", AT_W1_WOVEN, [P, 2 * PACK * H], BF16)
+        z_pairs = placed("z_pairs", AT_Z_PAIRS, [P, 2 * T2 * 2], BF16)
+        w1_woven = z_pairs[:, 2 * T2 :]
         for a in range(2):
             nc.sync.dma_start(w1_raw[a][:], w1_rows[a])
             weave(w1_woven[:, PACK * H * a : PACK * H * (a + 1)], w1_raw[a][:])
 
-        waiting = [(3, low), (0, high), (1, high), (2, high)]
-        acc_waiting = []
-        for n, (u, cols) in enumerate(waiting):
-            acc_waiting.append(bank("acc_h2", n))
-            plain_sum(acc_waiting[n][:], u, cols)
-        acc = bank("acc_h2", 6)
-        plain_sum(acc[:], 3, high)
-        h2_last = placed("h2_last", AT_H2 + 13, [P, BANK], F32)
-        nc.scalar.activation(h2_last[:], acc[:], ACT.Abs)
+        acc_high = [bank("acc_h2", at) for at in (1, 2, 3, 6)]
+        for u in range(PACK):
+            plain_sum(acc_high[u][:], u, high)
+        kept, late = slice(BANK, S - UNIT), slice(S - UNIT, S)
 
         turned = turn_wg2(1)
         for u in range(PACK):
@@ -252,7 +254,7 @@ def tile_list_terrain_weave_kernel(
         v = [[[v_0[:, 2 * P * t + P * b : 2 * P * t + P * (b + 1)] for t in range(PACK)] for b in range(2)], []]
         w1c = held("w1c", [P, 2 * H], U32)
         w1s = held("w1s", [P, 2 * H], U8)
-        quantize(w1c[:], w1s[:], w1_woven[:])
+        quantize(w1c[:], w1s[:], w1_woven)
         tab_1 = load_table_words("tab_1", tab_words, 1, AT_TAB)
         for b, cols in enumerate((low, high)):
             v_1 = placed("v_1%d" % b, AT_V + 4 + 2 * b, [P, PASS], U32)
@@ -262,17 +264,14 @@ def tile_list_terrain_weave_kernel(
             v[1].append([v_1[:, P * t : P * (t + 1)] for t in range(PACK)])
         spread_scales(v_scale, v_scale_sorted, 0)
 
-        z_pairs = placed("z_pairs", AT_TAB + 16, [P, 2 * T2 * 2], BF16)
-        nc.gpsimd.memset(z_pairs[:, 2 * T2 :].bitcast(I32), 0)
-
-        h2_waiting = placed("h2_waiting", AT_H2 + 6, [P, 3 * BANK + UNIT], F32)
-        kept, late = slice(BANK, S - UNIT), slice(S - UNIT, S)
-        for n, (u, cols) in enumerate(waiting):
-            if u == 2:
-                cols = kept
+        h2_waiting = placed("h2_waiting", AT_H2 + 6, [P, 4 * BANK], F32)
+        nc.scalar.activation(h2_waiting[:, first], acc_low3[:, second], ACT.Abs)
+        nc.scalar.activation(h2_waiting[:, UNIT : kept.stop], acc_high[3][:], ACT.Abs)
+        place(3, h2_waiting[:, 0 : kept.stop], wg2_t[3][:, UNIT:S], list4, slice(UNIT, S))
+        for u, cols in enumerate((high, high, kept)):
             width = cols.stop - cols.start
-            h = h2_waiting[:, BANK * n : BANK * n + width]
-            nc.scalar.activation(h, acc_waiting[n][:, 0:width], ACT.Abs)
+            h = h2_waiting[:, kept.stop + BANK * u : kept.stop + BANK * u + width]
+            nc.scalar.activation(h, acc_high[u][:, 0:width], ACT.Abs)
             place(u, h, wg2_t[u][:, cols], list4, cols)
 
         pieces = [slice(0, UNIT), slice(UNIT, BANK), high]
@@ -295,20 +294,27 @@ def tile_list_terrain_weave_kernel(
         woven_at = [AT_BLEND_WOVEN, AT_A_PLANES + 4, blend_at(1, 0)]
         bc, bs = [], []
 
+        blend_woven = []
+
+        def weave_blend(i, b):
+            width = pieces[i].stop - pieces[i].start
+            if b == 0:
+                blend_woven.append(placed("blend_woven%d" % i, woven_at[i], [P, 2 * PACK * width], BF16))
+            weave(blend_woven[i][:, PACK * width * b : PACK * width * (b + 1)], blend_raw[i][b][:])
+
         def quantize_blend(i):
             width = pieces[i].stop - pieces[i].start
-            woven = placed("blend_woven%d" % i, woven_at[i], [P, 2 * PACK * width], BF16)
-            for b in range(2):
-                weave(woven[:, PACK * width * b : PACK * width * (b + 1)], blend_raw[i][b][:])
             bc.append(placed("bc%d" % i, AT_BC[i], [P, 2 * width], U32))
             bs.append(held("bs%d" % i, [P, 2 * width], U8))
-            quantize(bc[i][:], bs[i][:], woven[:])
+            quantize(bc[i][:], bs[i][:], blend_woven[i][:])
 
+        weave_blend(0, 0)
+        weave_blend(0, 1)
         quantize_blend(0)
 
         a_planes = placed("a_planes", AT_A_PLANES, [P, 2, PACK, H], BF16)
         a_woven = placed("a_woven", AT_TAB, [P, 2 * PACK * H], BF16)
-        a_banks = (4, 5, 6, 7, 0, 1, 2, 4)
+        a_banks = (4, 5, 7, 0, 6, 1, 2, 4)
         acc_a = {}
 
         def project(b, t, a):
@@ -360,8 +366,12 @@ def tile_list_terrain_weave_kernel(
             nc.sync.dma_start(w3s[32 * q : 32 * q + 4, :].bitcast(I32), w3_scales[0, 4 * q : 4 * q + 4, :].bitcast(I32))
 
         h2_late = placed("h2_late", AT_A_PLANES, [P, UNIT], F32)
-        nc.scalar.activation(h2_late[:], acc_waiting[3][:, BANK - UNIT : BANK], ACT.Abs)
+        nc.scalar.activation(h2_late[:], acc_high[2][:, second], ACT.Abs)
         place(2, h2_late[:], wg2_t[2][:, late], list4, late)
+
+        weave_blend(1, 0)
+        weave_blend(1, 1)
+        quantize_blend(1)
 
         def blended_sum(i, u):
             width = pieces[i].stop - pieces[i].start
@@ -379,24 +389,28 @@ def tile_list_terrain_weave_kernel(
             return acc
 
         h1_at = [
-            (AT_W1, AT_W1 + 1, blend_at(1, 1), blend_at(1, 1) + 1),
-            (AT_W1 + 4, blend_at(2, 1), blend_at(2, 1) + 1),
+            (blend_at(1, 1), blend_at(1, 1) + 1, blend_at(1, 1) + 2),
+            (blend_at(2, 0), blend_at(2, 1), blend_at(2, 1) + 1),
             (AT_W1 + 6, AT_W1 + 8, AT_W1 + 10),
         ]
-        h1_last = placed("h1_last", AT_W1 + 12, [P, S - UNIT], F32)
+        h1_last = placed("h1_last", blend_at(2, 1) + 2, [P, S], F32)
+        last_sums = []
         for i, cols in enumerate(pieces):
             sums = [blended_sum(i, u) for u in range(PACK)]
-            for u in range(PACK):
-                if u < len(h1_at[i]):
-                    h = placed("h1_%d%d" % (i, u), h1_at[i][u], [P, cols.stop - cols.start], F32)
-                    nc.scalar.copy(h[:], sums[u])
-                    place(u, h[:], wg1_t[:, u, cols], list3, cols)
-                else:
-                    nc.scalar.copy(h1_last[:, cols.start - UNIT : cols.stop - UNIT], sums[u])
-                if u == 0 and i + 1 < len(pieces):
-                    quantize_blend(i + 1)
-        place(3, h1_last[:], wg1_t[:, 3, UNIT:S], list3, slice(UNIT, S))
-        place(3, h2_last[:], wg2_t[3][:, high], list4, high)
+            if i == 1:
+                weave_blend(2, 0)
+            last_sums.append(sums[PACK - 1])
+            for u in range(PACK - 1):
+                h = placed("h1_%d%d" % (i, u), h1_at[i][u], [P, cols.stop - cols.start], F32)
+                nc.scalar.copy(h[:], sums[u])
+                place(u, h[:], wg1_t[:, u, cols], list3, cols)
+                if (i, u) == (1, 0):
+                    weave_blend(2, 1)
+                    quantize_blend(2)
+            if i > 0:
+                for done in ([0, 1] if i == 1 else [2]):
+                    nc.scalar.copy(h1_last[:, pieces[done]], last_sums[done])
+        place(3, h1_last[:], wg1_t[:, 3, :], list3, slice(0, S))
 
         for u in range(PACK - 1):
             nc.scalar.activation(

@@ -418,7 +418,7 @@ def tile_list_terrain_weave_kernel(
                 pages[u][:], ACT.Relu, bias=biases[:, u : u + 1],
             )
         pair_words = z_pairs[:].bitcast(F32).rearrange("p (h t) -> p t h", h=2)
-        groups = [(128, 128), (256, 256), (256, 512, 512)]
+        groups = [(128, 128), (256, 512), (512, 512)]
         widths = [width for group in groups for width in group]
         parts = [slice(sum(widths[:c]), sum(widths[: c + 1])) for c in range(len(widths))]
         z_part = []
@@ -459,25 +459,26 @@ def tile_list_terrain_weave_kernel(
             for pair in range(2):
                 acc = bank("acc_out", len(filled) % 8)
                 filled.append(acc)
-                for first in range(0, UNIT, step):
+                for col in range(0, UNIT, step):
                     for e in range(2):
                         product(
-                            acc[:, UNIT * e + first : UNIT * e + first + step], 2 * pair + e,
-                            slice(cols.start + first, cols.start + first + step),
+                            acc[:, UNIT * e + col : UNIT * e + col + step], 2 * pair + e,
+                            slice(cols.start + col, cols.start + col + step),
                         )
                 blocks = slice(2 * pair, 2 * pair + 2)
                 nc.scalar.copy(staged[:, blocks, :].rearrange("p b t -> p (b t)"), acc[:])
                 nc.sync.dma_start(out_rows[:, blocks, cols], staged[:, blocks, :])
 
-        def wide_features():
-            staged = placed("staged_wide", AT_BLEND + S * PACK * 4 // 1024, [P, PACK, S], F32)
+        def wide_features(cols, copies):
+            width = cols.stop - cols.start
+            staged = placed("staged%d" % cols.start, AT_BLEND + cols.start * PACK * 4 // 1024, [P, PACK, width], F32)
             for nb in range(PACK):
-                for half, copy in enumerate((nc.scalar.copy, nc.vector.tensor_copy)):
+                for n, copy in enumerate(copies):
                     acc = bank("acc_out", len(filled) % 8)
                     filled.append(acc)
-                    product(acc[:], nb, slice(S + BANK * half, S + BANK * (half + 1)))
-                    copy(staged[:, nb, BANK * half : BANK * (half + 1)], acc[:])
-                nc.sync.dma_start(out_rows[:, nb, S:T2], staged[:, nb, :])
+                    product(acc[:], nb, slice(cols.start + BANK * n, cols.start + BANK * (n + 1)))
+                    copy(staged[:, nb, BANK * n : BANK * (n + 1)], acc[:])
+                nc.sync.dma_start(out_rows[:, nb, cols], staged[:, nb, :])
 
         done = 0
         for group in groups:
@@ -488,6 +489,6 @@ def tile_list_terrain_weave_kernel(
             for c in mine:
                 quantize(zc[:, parts[c]], zs[:, parts[c]], z_part[c])
         narrow_features(slice(0, UNIT), P)
-        for first in range(UNIT, S, UNIT):
-            narrow_features(slice(first, first + UNIT), UNIT)
-        wide_features()
+        narrow_features(second, UNIT)
+        wide_features(high, [nc.scalar.copy])
+        wide_features(slice(S, T2), [nc.scalar.copy, nc.vector.tensor_copy])

@@ -105,14 +105,16 @@ def tile_list_terrain_weave_kernel(
             nc.vector.quantize_mx(out=codes.bitcast(FP8X4), scales=scales, in_=woven)
 
         low, high = slice(0, BANK), slice(BANK, S)
+        first, second = slice(0, UNIT), slice(UNIT, BANK)
+        middle, late = slice(UNIT, S - UNIT), slice(S - UNIT, S)
 
-        w2s_raw = load_scale_rows(nc.vector, held("w2s_raw", [P, H], U8), w2_scales, 96)
-        list2 = load_list("list2", offs2)
         sc2 = load_scale_rows(nc.vector, placed("sc2", AT_SCALES, [P, T], U8), tab2_scales, 96)
+        list2 = load_list("list2", offs2)
+        w2s_raw = load_scale_rows(nc.vector, held("w2s_raw", [P, H], U8), w2_scales, 96)
         list1 = load_list("list1", offs)
         sc1 = load_scale_rows(nc.gpsimd, placed("sc1", AT_SCALES + 4, [P, T], U8), tab_scales, 0)
-        wg2_rows = [held("wg2_rows%d" % half, [P, BANK], F32) for half in range(2)]
-        nc.sync.dma_start(wg2_rows[0][:], wg2[:, low])
+        wg2_rows = [held("wg2_rows0", [P, UNIT], F32), held("wg2_rows1", [P, S - UNIT], F32)]
+        nc.sync.dma_start(wg2_rows[0][:], wg2[:, first])
         tab2_0 = load_table_words("tab2_0", tab2_words, 0, AT_TAB2)
         w2_raw = held("w2_raw", [P, 2, 2 * H], U8)
         nc.sync.dma_start(w2_raw[:].bitcast(I32), w2_words.bitcast(I32).rearrange("a p c -> p a c"))
@@ -159,28 +161,27 @@ def tile_list_terrain_weave_kernel(
         def place(u, h, factor, lst, cols):
             nc.vector.tensor_tensor(pages[u][:].indirect(entries(lst, cols)), h, factor, MULT)
 
-        wg2_t = [placed("wg2_%d" % u, AT_WG2 + 4 * u, [P, S], F32) for u in range(PACK)]
+        wg2_t = placed("wg2_t", AT_WG2, [P, PACK, S], F32)
 
-        def turn_wg2(half):
-            turned = bank("wg2_turned", 6 + half)
-            for c in range(PACK):
-                nc.tensor.transpose(turned[:, P * c : P * (c + 1)], wg2_rows[half][:, P * c : P * (c + 1)], ident[:])
-            return turned
+        def turn_wg2(rows, at_bank):
+            turned = bank("wg2_turned", at_bank)
+            for c in range(rows.shape[1] // P):
+                nc.tensor.transpose(turned[:, P * c : P * (c + 1)], rows[:, P * c : P * (c + 1)], ident[:])
+            return turned[:, 0 : rows.shape[1]].rearrange("p (c q u) -> p u c q", q=32, u=PACK)
 
-        def deal_wg2(turned, u, cols):
-            repeated = ring("wg2_repeated", [P, PACK, QUADS, 32], F32)
-            src = turned[:].rearrange("p (c q u) -> p c u q", c=PACK, u=PACK)[:, :, u, :]
-            nc.scalar.copy(repeated[:], src.unsqueeze(2).to_broadcast([P, PACK, QUADS, 32]))
-            back = bank("wg2_back", 4 + u % 2)
-            for c in range(PACK):
-                nc.tensor.transpose(
-                    back[:, P * c : P * (c + 1)], repeated[:, c].rearrange("p g q -> p (g q)"), ident[:]
-                )
-            nc.scalar.copy(wg2_t[u][:, cols], back[:])
+        def deal_wg2(turned, us, cols, at_bank):
+            count, blocks = us.stop - us.start, turned.shape[2]
+            repeated = ring("wg2_repeated", [P, count, blocks, QUADS, 32], F32)
+            nc.scalar.copy(repeated[:], turned[:, us].unsqueeze(3).to_broadcast([P, count, blocks, QUADS, 32]))
+            back = bank("wg2_back", at_bank)
+            blocks_in = repeated[:].rearrange("p u c g q -> p (u c) (g q)")
+            for n in range(count * blocks):
+                nc.tensor.transpose(back[:, P * n : P * (n + 1)], blocks_in[:, n], ident[:])
+            nc.scalar.copy(wg2_t[:, us, cols], back[:].rearrange("p (u m) -> p u m", u=count))
 
-        turned = turn_wg2(0)
-        for u in range(PACK):
-            deal_wg2(turned, u, low)
+        turned = turn_wg2(wg2_rows[0][:], 6)
+        for pair in range(2):
+            deal_wg2(turned, slice(2 * pair, 2 * pair + 2), first, 4 + pair)
 
         def plain_sum(acc, u, cols):
             for a in range(2):
@@ -194,33 +195,36 @@ def tile_list_terrain_weave_kernel(
                     stop=(a == 1),
                 )
 
-        first, second = slice(0, UNIT), slice(UNIT, BANK)
-        for u in range(2):
-            acc = bank("acc_h2", u)
-            plain_sum(acc[:, 0:UNIT], u, first)
-            h = placed("h2_first%d" % u, AT_H2 + u, [P, UNIT], F32)
-            nc.scalar.activation(h[:], acc[:, 0:UNIT], ACT.Abs)
-            place(u, h[:], wg2_t[u][:, first], list4, first)
-        acc = bank("acc_h2", 2)
-        plain_sum(acc[:], 2, low)
-        h = placed("h2_low2", AT_H2 + 2, [P, BANK], F32)
-        nc.scalar.activation(h[:], acc[:], ACT.Abs)
-        place(2, h[:], wg2_t[2][:, low], list4, low)
-        acc = bank("acc_h2", 6)
-        for u in range(2):
-            plain_sum(acc[:, UNIT * u : UNIT * (u + 1)], u, second)
-        h = placed("h2_second", AT_H2 + 4, [P, BANK], F32)
-        nc.scalar.activation(h[:], acc[:], ACT.Abs)
-        for u in range(2):
-            place(u, h[:, UNIT * u : UNIT * (u + 1)], wg2_t[u][:, second], list4, second)
+        def paired_sums(us, cols, at_bank):
+            acc = bank("acc_h2", at_bank)
+            for n, u in enumerate(us):
+                plain_sum(acc[:, UNIT * n : UNIT * (n + 1)], u, cols)
+            return acc
 
-        acc_low3 = bank("acc_h2", 0)
-        plain_sum(acc_low3[:], 3, low)
-        h = placed("h2_first3", AT_H2 + 14, [P, UNIT], F32)
-        nc.scalar.activation(h[:], acc_low3[:, first], ACT.Abs)
-        place(3, h[:], wg2_t[3][:, first], list4, first)
+        def place_plain(name, at, acc, us, cols):
+            width = cols.stop - cols.start
+            h = placed(name, at, [P, len(us) * width], F32)
+            nc.scalar.activation(h[:], acc[:, 0 : len(us) * width], ACT.Abs)
+            for n, u in enumerate(us):
+                place(u, h[:, width * n : width * (n + 1)], wg2_t[:, u, cols], list4, cols)
 
-        nc.sync.dma_start(wg2_rows[1][:], wg2[:, high])
+        for n, us in enumerate(((0,), (1,), (2, 3))):
+            place_plain("h2_first%d" % n, AT_H2 + n, paired_sums(us, first, n), us, first)
+
+        nc.sync.dma_start(wg2_rows[1][:], wg2[:, UNIT:S])
+        turned_middle = turn_wg2(wg2_rows[1][:, low], 7)
+        deal_wg2(turned_middle, slice(0, 1), middle, 4)
+        acc_middle = [bank("acc_h2", at) for at in (3, 0, 1, 2)]
+        for u in range(PACK):
+            plain_sum(acc_middle[u][:], u, middle)
+        place_plain("h2_middle0", AT_H2 + 4, acc_middle[0], (0,), middle)
+        turned_late = turn_wg2(wg2_rows[1][:, BANK:], 6)
+        deal_wg2(turned_late, slice(0, 2), late, 5)
+        acc_late = [paired_sums((1, 0), late, 3)]
+        h = placed("h2_late1", AT_H2 + 14, [P, UNIT], F32)
+        nc.scalar.activation(h[:], acc_late[0][:, first], ACT.Abs)
+        place(1, h[:], wg2_t[:, 1, late], list4, late)
+
         w1_raw = [placed("w1_raw%d" % a, AT_W1 + 8 * a, [P, PACK, H], F32) for a in range(2)]
         w1_rows = w1.rearrange("(a p j) c -> a p j c", a=2, j=PACK)
         z_pairs = placed("z_pairs", AT_Z_PAIRS, [P, 2 * T2 * 2], BF16)
@@ -229,14 +233,10 @@ def tile_list_terrain_weave_kernel(
             nc.sync.dma_start(w1_raw[a][:], w1_rows[a])
             weave(w1_woven[:, PACK * H * a : PACK * H * (a + 1)], w1_raw[a][:])
 
-        acc_high = [bank("acc_h2", at) for at in (1, 2, 3, 6)]
-        for u in range(PACK):
-            plain_sum(acc_high[u][:], u, high)
-        kept, late = slice(BANK, S - UNIT), slice(S - UNIT, S)
-
-        turned = turn_wg2(1)
-        for u in range(PACK):
-            deal_wg2(turned, u, high)
+        deal_wg2(turned_late, slice(2, 4), late, 4)
+        acc_late.append(paired_sums((3, 2), late, 6))
+        for u in range(1, PACK):
+            deal_wg2(turned_middle, slice(u, u + 1), middle, 4 + u % 2)
 
         for b in range(2):
             nc.sync.dma_start(
@@ -265,16 +265,16 @@ def tile_list_terrain_weave_kernel(
         spread_scales(v_scale, v_scale_sorted, 0)
 
         h2_waiting = placed("h2_waiting", AT_H2 + 6, [P, 4 * BANK], F32)
-        nc.scalar.activation(h2_waiting[:, first], acc_low3[:, second], ACT.Abs)
-        nc.scalar.activation(h2_waiting[:, UNIT : kept.stop], acc_high[3][:], ACT.Abs)
-        place(3, h2_waiting[:, 0 : kept.stop], wg2_t[3][:, UNIT:S], list4, slice(UNIT, S))
-        for u, cols in enumerate((high, high, kept)):
-            width = cols.stop - cols.start
-            h = h2_waiting[:, kept.stop + BANK * u : kept.stop + BANK * u + width]
-            nc.scalar.activation(h, acc_high[u][:, 0:width], ACT.Abs)
-            place(u, h, wg2_t[u][:, cols], list4, cols)
+        for u in range(1, PACK):
+            h = h2_waiting[:, BANK * (u - 1) : BANK * u]
+            nc.scalar.activation(h, acc_middle[u][:], ACT.Abs)
+            place(u, h, wg2_t[:, u, middle], list4, middle)
+        for n, (u, acc) in enumerate(((0, acc_late[0][:, second]), (3, acc_late[1][:, first]))):
+            h = h2_waiting[:, 3 * BANK + UNIT * n : 3 * BANK + UNIT * (n + 1)]
+            nc.scalar.activation(h, acc, ACT.Abs)
+            place(u, h, wg2_t[:, u, late], list4, late)
 
-        pieces = [slice(0, UNIT), slice(UNIT, BANK), high]
+        pieces = [first, second, high]
 
         def blend_at(i, b):
             return AT_BLEND + ((4, 8), (0, 12), (16, 24))[i][b]
@@ -314,7 +314,7 @@ def tile_list_terrain_weave_kernel(
 
         a_planes = placed("a_planes", AT_A_PLANES, [P, 2, PACK, H], BF16)
         a_woven = placed("a_woven", AT_TAB, [P, 2 * PACK * H], BF16)
-        a_banks = (4, 5, 7, 0, 6, 1, 2, 4)
+        a_banks = (4, 5, 7, 0, 1, 2, 3, 4)
         acc_a = {}
 
         def project(b, t, a):
@@ -366,8 +366,8 @@ def tile_list_terrain_weave_kernel(
             nc.sync.dma_start(w3s[32 * q : 32 * q + 4, :].bitcast(I32), w3_scales[0, 4 * q : 4 * q + 4, :].bitcast(I32))
 
         h2_late = placed("h2_late", AT_A_PLANES, [P, UNIT], F32)
-        nc.scalar.activation(h2_late[:], acc_high[2][:, second], ACT.Abs)
-        place(2, h2_late[:], wg2_t[2][:, late], list4, late)
+        nc.scalar.activation(h2_late[:], acc_late[1][:, second], ACT.Abs)
+        place(2, h2_late[:], wg2_t[:, 2, late], list4, late)
 
         weave_blend(1, 0)
         weave_blend(1, 1)
@@ -375,7 +375,7 @@ def tile_list_terrain_weave_kernel(
 
         def blended_sum(i, u):
             width = pieces[i].stop - pieces[i].start
-            acc = bank("acc_h1", PACK * ((i + 1) % 2) + u)[:, 0:width]
+            acc = bank("acc_h1", PACK * (i % 2) + u)[:, 0:width]
             for b in range(2):
                 nc.tensor.matmul_mx(
                     out=acc,

@@ -358,10 +358,10 @@ def tile_list_terrain_weave_kernel(
         load_wg1(low)
         blend_raw.append(load_blend(2))
         load_wg1(high)
+        early_biases = placed("early_biases", AT_W1, [P, PACK], F32)
         biases = held("biases", [P, PACK], F32)
-        nc.sync.dma_start(biases[:], bias.rearrange("(p t) -> p t", t=PACK))
-        w3c = held("w3c", [P, N], U32)
-        nc.sync.dma_start(w3c[:].bitcast(I32), w3_words[0].rearrange("p c i -> p (c i)").bitcast(I32))
+        for dst in (early_biases, biases):
+            nc.sync.dma_start(dst[:], bias.rearrange("(p t) -> p t", t=PACK))
         for q in range(QUADS):
             nc.sync.dma_start(w3s[32 * q : 32 * q + 4, :].bitcast(I32), w3_scales[0, 4 * q : 4 * q + 4, :].bitcast(I32))
 
@@ -412,10 +412,28 @@ def tile_list_terrain_weave_kernel(
                     nc.scalar.copy(h1_last[:, pieces[done]], last_sums[done])
         place(3, h1_last[:], wg1_t[:, 3, :], list3, slice(0, S))
 
-        for u in range(PACK - 1):
+        def relu(u, cols, source):
             nc.scalar.activation(
-                z_pairs[:].rearrange("p (h t e) -> p h t e", h=2, e=2)[:, u // 2, :, u % 2],
-                pages[u][:], ACT.Relu, bias=biases[:, u : u + 1],
+                z_pairs[:].rearrange("p (h t e) -> p h t e", h=2, e=2)[:, u // 2, cols, u % 2],
+                pages[u][:, cols], ACT.Relu, bias=source[:, u : u + 1],
+            )
+
+        relu(0, slice(0, T2), early_biases)
+        relu(1, slice(0, T2), early_biases)
+        relu(2, slice(0, S), early_biases)
+        relu(2, slice(S, T2), biases)
+        w3c = placed("w3c", AT_W1, [P, N], U32)
+        nc.sync.dma_start(w3c[:].bitcast(I32), w3_words[0].rearrange("p c i -> p (c i)").bitcast(I32))
+        warm = bank("warm", 7)
+        for n in range(5):
+            nc.tensor.matmul_mx(
+                out=warm[:],
+                lhsT=w3c[:, 0:P].bitcast(FP8X4),
+                lhsT_scale=w3s[:, 0:P],
+                rhs=bc[2][:, 0:BANK].bitcast(FP8X4),
+                rhs_scale=bs[2][:, 0:BANK],
+                start=True,
+                stop=True,
             )
         pair_words = z_pairs[:].bitcast(F32).rearrange("p (h t) -> p t h", h=2)
         groups = [(128, 128), (256, 512), (512, 512)]

@@ -425,7 +425,7 @@ def tile_list_terrain_weave_kernel(
         w3c = placed("w3c", AT_W1, [P, N], U32)
         nc.sync.dma_start(w3c[:].bitcast(I32), w3_words[0].rearrange("p c i -> p (c i)").bitcast(I32))
         warm = bank("warm", 7)
-        for n in range(5):
+        for n in range(6):
             nc.tensor.matmul_mx(
                 out=warm[:],
                 lhsT=w3c[:, 0:P].bitcast(FP8X4),
@@ -436,7 +436,7 @@ def tile_list_terrain_weave_kernel(
                 stop=True,
             )
         pair_words = z_pairs[:].bitcast(F32).rearrange("p (h t) -> p t h", h=2)
-        groups = [(128, 128), (256, 512), (512, 512)]
+        groups = [(128, 128), (256, 256), (256, 256), (256, 512)]
         widths = [width for group in groups for width in group]
         parts = [slice(sum(widths[:c]), sum(widths[: c + 1])) for c in range(len(widths))]
         z_part = []
@@ -472,31 +472,26 @@ def tile_list_terrain_weave_kernel(
 
         filled = []
 
-        def narrow_features(cols, step):
-            staged = placed("staged%d" % cols.start, AT_BLEND + cols.start * PACK * 4 // 1024, [P, PACK, UNIT], F32)
-            for pair in range(2):
-                acc = bank("acc_out", len(filled) % 8)
-                filled.append(acc)
-                for col in range(0, UNIT, step):
-                    for e in range(2):
-                        product(
-                            acc[:, UNIT * e + col : UNIT * e + col + step], 2 * pair + e,
-                            slice(cols.start + col, cols.start + col + step),
-                        )
-                blocks = slice(2 * pair, 2 * pair + 2)
-                nc.scalar.copy(staged[:, blocks, :].rearrange("p b t -> p (b t)"), acc[:])
-                nc.sync.dma_start(out_rows[:, blocks, cols], staged[:, blocks, :])
-
-        def wide_features(cols, copies):
+        def features(cols, together):
             width = cols.stop - cols.start
             staged = placed("staged%d" % cols.start, AT_BLEND + cols.start * PACK * 4 // 1024, [P, PACK, width], F32)
-            for nb in range(PACK):
-                for n, copy in enumerate(copies):
+            for nb in range(0, PACK, together):
+                blocks = slice(nb, nb + together)
+                for n, start in enumerate(range(cols.start, cols.stop, BANK)):
+                    stop = min(start + BANK, cols.stop)
                     acc = bank("acc_out", len(filled) % 8)
                     filled.append(acc)
-                    product(acc[:], nb, slice(cols.start + BANK * n, cols.start + BANK * (n + 1)))
-                    copy(staged[:, nb, BANK * n : BANK * (n + 1)], acc[:])
-                nc.sync.dma_start(out_rows[:, nb, cols], staged[:, nb, :])
+                    for part in parts:
+                        if start <= part.start < stop:
+                            for e in range(together):
+                                at = e * width + part.start - start
+                                product(acc[:, at : at + part.stop - part.start], nb + e, part)
+                    copy = nc.vector.tensor_copy if n else nc.scalar.copy
+                    copy(
+                        staged[:, blocks, start - cols.start : stop - cols.start],
+                        acc[:, 0 : together * (stop - start)].rearrange("p (b t) -> p b t", b=together),
+                    )
+                nc.sync.dma_start(out_rows[:, blocks, cols], staged[:, blocks, :])
 
         done = 0
         for group in groups:
@@ -506,7 +501,7 @@ def tile_list_terrain_weave_kernel(
                 last_relu(c)
             for c in mine:
                 quantize(zc[:, parts[c]], zs[:, parts[c]], z_part[c])
-        narrow_features(slice(0, UNIT), P)
-        narrow_features(second, UNIT)
-        wide_features(high, [nc.scalar.copy])
-        wide_features(slice(S, T2), [nc.scalar.copy, nc.vector.tensor_copy])
+        features(first, 1)
+        features(second, 2)
+        features(high, 1)
+        features(slice(S, T2), 1)

@@ -25,6 +25,7 @@ PASS = P * PACK
 BANK = 512
 QUADS = 4
 UNIT = 256
+W3_BEHIND = 640
 
 AT_TAB2 = 0
 AT_TAB = 32
@@ -119,7 +120,6 @@ def tile_list_terrain_weave_kernel(
         w2_raw = held("w2_raw", [P, 2, 2 * H], U8)
         nc.sync.dma_start(w2_raw[:].bitcast(I32), w2_words.bitcast(I32).rearrange("a p c -> p a c"))
         tab2_1 = load_table_words("tab2_1", tab2_words, 1, AT_TAB2)
-        list4 = load_list("list4", offs4)
         ident = held("ident", [P, P], F32)
         make_identity(nc, ident[:])
         plain_scale = zeroed(nc.gpsimd, "plain_scale", 2 * (S + H))
@@ -137,6 +137,7 @@ def tile_list_terrain_weave_kernel(
         nc.vector.tensor_copy(v2_scale_picked[:], sc2[:].indirect(list2[:]))
         nc.vector.tensor_copy(plain_rows[:, 0:S].bitcast(I32), v2_scale_picked[:].bitcast(I32))
         spread_scales(plain_scale, plain_rows, 96)
+        list4 = load_list("list4", offs4)
 
         v_scale_picked = held("v_scale_picked", [P, S], U8)
         nc.vector.tensor_copy(v_scale_picked[:], sc1[:].indirect(list1[:]))
@@ -400,7 +401,7 @@ def tile_list_terrain_weave_kernel(
             if i == 1:
                 weave_blend(2, 0)
             last_sums.append(sums[PACK - 1])
-            for u in range(PACK - 1):
+            for u in (0, 2, 1):
                 h = placed("h1_%d%d" % (i, u), h1_at[i][u], [P, cols.stop - cols.start], F32)
                 nc.scalar.copy(h[:], sums[u])
                 place(u, h[:], wg1_t[:, u, cols], list3, cols)
@@ -419,9 +420,9 @@ def tile_list_terrain_weave_kernel(
             )
 
         relu(0, slice(0, T2), early_biases)
-        relu(1, slice(0, T2), early_biases)
-        relu(2, slice(0, S), early_biases)
-        relu(2, slice(S, T2), biases)
+        relu(2, slice(0, T2), early_biases)
+        relu(1, slice(0, W3_BEHIND), early_biases)
+        relu(1, slice(W3_BEHIND, T2), biases)
         w3c = placed("w3c", AT_W1, [P, N], U32)
         nc.sync.dma_start(w3c[:].bitcast(I32), w3_words[0].rearrange("p c i -> p (c i)").bitcast(I32))
         warm = bank("warm", 7)
@@ -472,26 +473,43 @@ def tile_list_terrain_weave_kernel(
 
         filled = []
 
-        def features(cols, together):
+        def staging(cols):
+            at = AT_BLEND + cols.start * PACK * 4 // 1024
+            return placed("staged%d" % cols.start, at, [P, PACK, cols.stop - cols.start], F32)
+
+        def fill_and_empty(copy, dst, blocks, cols):
             width = cols.stop - cols.start
-            staged = placed("staged%d" % cols.start, AT_BLEND + cols.start * PACK * 4 // 1024, [P, PACK, width], F32)
+            acc = bank("acc_out", len(filled) % 8)
+            filled.append(acc)
+            for part in parts:
+                if cols.start <= part.start < cols.stop:
+                    for e, nb in enumerate(range(blocks.start, blocks.stop)):
+                        at = e * width + part.start - cols.start
+                        product(acc[:, at : at + part.stop - part.start], nb, part)
+            count = blocks.stop - blocks.start
+            copy(dst, acc[:, 0 : count * width].rearrange("p (b t) -> p b t", b=count))
+
+        def narrow_features(cols, together):
+            staged = staging(cols)
             for nb in range(0, PACK, together):
                 blocks = slice(nb, nb + together)
-                for n, start in enumerate(range(cols.start, cols.stop, BANK)):
-                    stop = min(start + BANK, cols.stop)
-                    acc = bank("acc_out", len(filled) % 8)
-                    filled.append(acc)
-                    for part in parts:
-                        if start <= part.start < stop:
-                            for e in range(together):
-                                at = e * width + part.start - start
-                                product(acc[:, at : at + part.stop - part.start], nb + e, part)
-                    copy = nc.vector.tensor_copy if n else nc.scalar.copy
-                    copy(
-                        staged[:, blocks, start - cols.start : stop - cols.start],
-                        acc[:, 0 : together * (stop - start)].rearrange("p (b t) -> p b t", b=together),
-                    )
+                fill_and_empty(nc.scalar.copy, staged[:, blocks, :], blocks, cols)
                 nc.sync.dma_start(out_rows[:, blocks, cols], staged[:, blocks, :])
+
+        def wide_features(cols):
+            staged = staging(cols)
+            halves = [slice(cols.start, cols.start + BANK), slice(cols.start + BANK, cols.stop)]
+            block = slice(0, 1)
+            fill_and_empty(nc.vector.tensor_copy, staged[:, block, low], block, halves[0])
+            nc.sync.dma_start(out_rows[:, block, halves[0]], staged[:, block, low])
+            for nb in range(1, PACK):
+                block = slice(nb, nb + 1)
+                fill_and_empty(nc.scalar.copy, staged[:, block, low], block, halves[0])
+                fill_and_empty(nc.vector.tensor_copy, staged[:, block, high], block, halves[1])
+                nc.sync.dma_start(out_rows[:, block, cols], staged[:, block, :])
+            block = slice(0, 1)
+            fill_and_empty(nc.scalar.copy, staged[:, block, high], block, halves[1])
+            nc.sync.dma_start(out_rows[:, block, halves[1]], staged[:, block, high])
 
         done = 0
         for group in groups:
@@ -501,7 +519,7 @@ def tile_list_terrain_weave_kernel(
                 last_relu(c)
             for c in mine:
                 quantize(zc[:, parts[c]], zs[:, parts[c]], z_part[c])
-        features(first, 1)
-        features(second, 2)
-        features(high, 1)
-        features(slice(S, T2), 1)
+        narrow_features(first, 1)
+        narrow_features(second, 2)
+        narrow_features(high, 1)
+        wide_features(slice(S, T2))

@@ -120,6 +120,11 @@ def tile_list_terrain_weave_kernel(
         w2_raw = held("w2_raw", [P, 2, 2 * H], U8)
         nc.sync.dma_start(w2_raw[:].bitcast(I32), w2_words.bitcast(I32).rearrange("a p c -> p a c"))
         tab2_1 = load_table_words("tab2_1", tab2_words, 1, AT_TAB2)
+        plain_rows = held("plain_rows", [P, S + H], U8)
+        nc.gpsimd.tensor_copy(
+            plain_rows[:, S:].rearrange("p (u m) -> p u m", u=PACK),
+            w2s_raw[:].rearrange("p (m u) -> p u m", u=PACK),
+        )
         ident = held("ident", [P, P], F32)
         make_identity(nc, ident[:])
         plain_scale = zeroed(nc.gpsimd, "plain_scale", 2 * (S + H))
@@ -128,11 +133,6 @@ def tile_list_terrain_weave_kernel(
         gain_rows = held("gain_rows", [P, P], F32)
         nc.gpsimd.memset(gain_rows[:], 0.0)
 
-        plain_rows = held("plain_rows", [P, S + H], U8)
-        nc.vector.tensor_copy(
-            plain_rows[:, S:].rearrange("p (u m) -> p u m", u=PACK),
-            w2s_raw[:].rearrange("p (m u) -> p u m", u=PACK),
-        )
         v2_scale_picked = held("v2_scale_picked", [P, S], U8)
         nc.vector.tensor_copy(v2_scale_picked[:], sc2[:].indirect(list2[:]))
         nc.vector.tensor_copy(plain_rows[:, 0:S].bitcast(I32), v2_scale_picked[:].bitcast(I32))
@@ -150,7 +150,7 @@ def tile_list_terrain_weave_kernel(
         v2 = [placed("v2_%d" % a, AT_V + 4 * a, [P, S], U32) for a in range(2)]
         nc.vector.tensor_copy(v2[0][:], tab2_0[:].indirect(list2[:]))
         w2c = held("w2c", [P, 2, 2 * H], U8)
-        nc.vector.tensor_copy(
+        nc.scalar.copy(
             w2c[:].bitcast(U16).rearrange("p a (u m) -> p a u m", u=PACK),
             w2_raw[:].bitcast(U16).rearrange("p a (m u) -> p a u m", u=PACK),
         )

@@ -425,17 +425,6 @@ def tile_list_terrain_weave_kernel(
         relu(1, slice(W3_BEHIND, T2), biases)
         w3c = placed("w3c", AT_W1, [P, N], U32)
         nc.sync.dma_start(w3c[:].bitcast(I32), w3_words[0].rearrange("p c i -> p (c i)").bitcast(I32))
-        warm = bank("warm", 7)
-        for n in range(6):
-            nc.tensor.matmul_mx(
-                out=warm[:],
-                lhsT=w3c[:, 0:P].bitcast(FP8X4),
-                lhsT_scale=w3s[:, 0:P],
-                rhs=bc[2][:, 0:BANK].bitcast(FP8X4),
-                rhs_scale=bs[2][:, 0:BANK],
-                start=True,
-                stop=True,
-            )
         pair_words = z_pairs[:].bitcast(F32).rearrange("p (h t) -> p t h", h=2)
         groups = [(128, 128), (256, 256), (256, 256), (256, 512)]
         widths = [width for group in groups for width in group]

@@ -25,21 +25,22 @@ PASS = P * PACK
 BANK = 512
 QUADS = 4
 UNIT = 256
-W3_BEHIND = 640
 
 AT_TAB2 = 0
 AT_TAB = 32
+AT_A_WOVEN = 32
+AT_A_PLANES = (40, 58)
 AT_W1 = 64
-AT_BLEND = 80
-AT_A_PLANES = 84
+AT_STAGED = 80
+AT_BLEND_RAW = ((80, 84), (48, 52), (96, 104))
+AT_BLEND_WOVEN = (56, 60, 88)
 AT_WG2 = 112
 AT_H2 = 128
 AT_V = 144
 AT_SCALES = 152
 AT_BC = (152, 154, 156)
-AT_BLEND_WOVEN = 160
-AT_WG1 = 164
-AT_Z_PAIRS = 180
+AT_WG1 = 160
+AT_Z_PAIRS = 176
 
 
 def tile_list_terrain_weave_kernel(
@@ -81,12 +82,17 @@ def tile_list_terrain_weave_kernel(
                 engine.memset(dst[rest, :].bitcast(I32), 0)
             return dst
 
-        def spread_scales(dst, src, first):
+        def spread_scales(dst, src, first, cols):
             for q in range(QUADS):
                 nc.sync.dma_start(
-                    dst[32 * q : 32 * q + 4, :].bitcast(I32).rearrange("r (a c) -> r a c", a=2),
-                    src[first + 8 * q : first + 8 * q + 8, :].bitcast(I32),
+                    dst[32 * q : 32 * q + 4, :].rearrange("r (a c) -> r a c", a=2)[:, :, cols].bitcast(I32),
+                    src[first + 8 * q : first + 8 * q + 8, cols].bitcast(I32),
                 )
+
+        def load_dealt(dst, src, cols):
+            rows = src.rearrange("(q t) m -> q t m", t=PACK)[:, :, cols]
+            for q in (0, 2, 1, 3):
+                nc.sync.dma_start(dst[32 * q : 32 * q + 32], rows)
 
         def load_table_words(name, src, a, at):
             dst = placed(name, at + 16 * a, [P, T], U32)
@@ -107,27 +113,26 @@ def tile_list_terrain_weave_kernel(
 
         low, high = slice(0, BANK), slice(BANK, S)
         first, second = slice(0, UNIT), slice(UNIT, BANK)
-        middle, late = slice(UNIT, S - UNIT), slice(S - UNIT, S)
 
         sc2 = load_scale_rows(nc.vector, placed("sc2", AT_SCALES, [P, T], U8), tab2_scales, 96)
         list2 = load_list("list2", offs2)
         w2s_raw = load_scale_rows(nc.vector, held("w2s_raw", [P, H], U8), w2_scales, 96)
         list1 = load_list("list1", offs)
         sc1 = load_scale_rows(nc.gpsimd, placed("sc1", AT_SCALES + 4, [P, T], U8), tab_scales, 0)
-        wg2_rows = [held("wg2_rows0", [P, UNIT], F32), held("wg2_rows1", [P, S - UNIT], F32)]
+        wg2_rows = [held("wg2_rows%d" % n, [P, UNIT], F32) for n in range(2)]
         nc.sync.dma_start(wg2_rows[0][:], wg2[:, first])
         tab2_0 = load_table_words("tab2_0", tab2_words, 0, AT_TAB2)
         w2_raw = held("w2_raw", [P, 2, 2 * H], U8)
         nc.sync.dma_start(w2_raw[:].bitcast(I32), w2_words.bitcast(I32).rearrange("a p c -> p a c"))
         tab2_1 = load_table_words("tab2_1", tab2_words, 1, AT_TAB2)
-        plain_rows = held("plain_rows", [P, S + H], U8)
+        plain_rows = held("plain_rows", [P, H + S], U8)
         nc.gpsimd.tensor_copy(
-            plain_rows[:, S:].rearrange("p (u m) -> p u m", u=PACK),
+            plain_rows[:, 0:H].rearrange("p (u m) -> p u m", u=PACK),
             w2s_raw[:].rearrange("p (m u) -> p u m", u=PACK),
         )
         ident = held("ident", [P, P], F32)
         make_identity(nc, ident[:])
-        plain_scale = zeroed(nc.gpsimd, "plain_scale", 2 * (S + H))
+        plain_scale = zeroed(nc.gpsimd, "plain_scale", 2 * (H + S))
         v_scale = zeroed(nc.gpsimd, "v_scale", 2 * S)
         w3s = zeroed(nc.gpsimd, "w3s", N)
         gain_rows = held("gain_rows", [P, P], F32)
@@ -135,13 +140,13 @@ def tile_list_terrain_weave_kernel(
 
         v2_scale_picked = held("v2_scale_picked", [P, S], U8)
         nc.vector.tensor_copy(v2_scale_picked[:], sc2[:].indirect(list2[:]))
-        nc.vector.tensor_copy(plain_rows[:, 0:S].bitcast(I32), v2_scale_picked[:].bitcast(I32))
-        spread_scales(plain_scale, plain_rows, 96)
+        nc.vector.tensor_copy(plain_rows[:, H:].bitcast(I32), v2_scale_picked[:].bitcast(I32))
+        spread_scales(plain_scale, plain_rows, 96, slice(0, H + UNIT))
         list4 = load_list("list4", offs4)
 
         v_scale_picked = held("v_scale_picked", [P, S], U8)
         nc.vector.tensor_copy(v_scale_picked[:], sc1[:].indirect(list1[:]))
-        v_scale_sorted = placed("v_scale_sorted", AT_H2 + 6, [P, S], U8)
+        v_scale_sorted = placed("v_scale_sorted", AT_H2 + 7, [P, S], U8)
         nc.vector.tensor_copy(
             v_scale_sorted[:].bitcast(I32).rearrange("p (t q w) -> p t q w", t=PACK, w=2),
             v_scale_picked[:].bitcast(I32).rearrange("p (q t w) -> p t q w", t=PACK, w=2),
@@ -162,89 +167,85 @@ def tile_list_terrain_weave_kernel(
         def place(u, h, factor, lst, cols):
             nc.vector.tensor_tensor(pages[u][:].indirect(entries(lst, cols)), h, factor, MULT)
 
-        wg2_t = placed("wg2_t", AT_WG2, [P, PACK, S], F32)
+        wg2_low = placed("wg2_low", AT_WG2, [P, PACK, BANK], F32)
+        wg2_high = placed("wg2_high", AT_WG2 + 8, [P, PACK, BANK], F32)
 
         def turn_wg2(rows, at_bank):
             turned = bank("wg2_turned", at_bank)
-            for c in range(rows.shape[1] // P):
+            for c in range(UNIT // P):
                 nc.tensor.transpose(turned[:, P * c : P * (c + 1)], rows[:, P * c : P * (c + 1)], ident[:])
-            return turned[:, 0 : rows.shape[1]].rearrange("p (c q u) -> p u c q", q=32, u=PACK)
+            return turned[:, 0:UNIT].rearrange("p (c q u) -> p u c q", q=32, u=PACK)
 
-        def deal_wg2(turned, us, cols, at_bank):
-            count, blocks = us.stop - us.start, turned.shape[2]
-            repeated = ring("wg2_repeated", [P, count, blocks, QUADS, 32], F32)
-            nc.scalar.copy(repeated[:], turned[:, us].unsqueeze(3).to_broadcast([P, count, blocks, QUADS, 32]))
+        def deal_wg2(turned, pair, cols, at_bank):
+            us, blocks = slice(2 * pair, 2 * pair + 2), UNIT // P
+            repeated = ring("wg2_repeated", [P, 2, blocks, QUADS, 32], F32)
+            nc.scalar.copy(repeated[:], turned[:, us].unsqueeze(3).to_broadcast([P, 2, blocks, QUADS, 32]))
             back = bank("wg2_back", at_bank)
             blocks_in = repeated[:].rearrange("p u c g q -> p (u c) (g q)")
-            for n in range(count * blocks):
+            for n in range(2 * blocks):
                 nc.tensor.transpose(back[:, P * n : P * (n + 1)], blocks_in[:, n], ident[:])
-            nc.scalar.copy(wg2_t[:, us, cols], back[:].rearrange("p (u m) -> p u m", u=count))
+            nc.scalar.copy(wg2_low[:, us, cols], back[:].rearrange("p (u m) -> p u m", u=2))
 
         turned = turn_wg2(wg2_rows[0][:], 6)
         for pair in range(2):
-            deal_wg2(turned, slice(2 * pair, 2 * pair + 2), first, 4 + pair)
+            deal_wg2(turned, pair, first, 4 + pair)
 
         def plain_sum(acc, u, cols):
             for a in range(2):
+                at = (H + S) * a
                 nc.tensor.matmul_mx(
                     out=acc,
                     lhsT=w2c[:, a, 256 * u : 256 * (u + 1)].bitcast(FP4X4),
-                    lhsT_scale=plain_scale[:, (S + H) * a + S + P * u : (S + H) * a + S + P * (u + 1)],
+                    lhsT_scale=plain_scale[:, at + P * u : at + P * (u + 1)],
                     rhs=v2[a][:, cols].bitcast(FP8X4),
-                    rhs_scale=plain_scale[:, (S + H) * a + cols.start : (S + H) * a + cols.stop],
+                    rhs_scale=plain_scale[:, at + H + cols.start : at + H + cols.stop],
                     start=(a == 0),
                     stop=(a == 1),
                 )
 
-        def paired_sums(us, cols, at_bank):
-            acc = bank("acc_h2", at_bank)
+        def sums_in_bank(us, cols, at_bank):
+            acc, width = bank("acc_h2", at_bank), cols.stop - cols.start
             for n, u in enumerate(us):
-                plain_sum(acc[:, UNIT * n : UNIT * (n + 1)], u, cols)
+                plain_sum(acc[:, width * n : width * (n + 1)], u, cols)
             return acc
 
         def place_plain(name, at, acc, us, cols):
             width = cols.stop - cols.start
             h = placed(name, at, [P, len(us) * width], F32)
-            nc.scalar.activation(h[:], acc[:, 0 : len(us) * width], ACT.Abs)
+            nc.scalar.activation(h[:], acc, ACT.Abs)
             for n, u in enumerate(us):
-                place(u, h[:, width * n : width * (n + 1)], wg2_t[:, u, cols], list4, cols)
+                factor = wg2_low[:, u, cols] if cols.stop <= BANK else wg2_high[:, u, cols.start - BANK : cols.stop - BANK]
+                place(u, h[:, width * n : width * (n + 1)], factor, list4, cols)
 
         for n, us in enumerate(((0,), (1,), (2, 3))):
-            place_plain("h2_first%d" % n, AT_H2 + n, paired_sums(us, first, n), us, first)
-
-        nc.sync.dma_start(wg2_rows[1][:], wg2[:, UNIT:S])
-        turned_middle = turn_wg2(wg2_rows[1][:, low], 7)
-        deal_wg2(turned_middle, slice(0, 1), middle, 4)
-        acc_middle = [bank("acc_h2", at) for at in (3, 0, 1, 2)]
-        for u in range(PACK):
-            plain_sum(acc_middle[u][:], u, middle)
-        place_plain("h2_middle0", AT_H2 + 4, acc_middle[0], (0,), middle)
-        turned_late = turn_wg2(wg2_rows[1][:, BANK:], 6)
-        deal_wg2(turned_late, slice(0, 2), late, 5)
-        acc_late = [paired_sums((1, 0), late, 3)]
-        h = placed("h2_late1", AT_H2 + 14, [P, UNIT], F32)
-        nc.scalar.activation(h[:], acc_late[0][:, first], ACT.Abs)
-        place(1, h[:], wg2_t[:, 1, late], list4, late)
+            place_plain("h2_first%d" % n, AT_H2 + n, sums_in_bank(us, first, n)[:, 0 : UNIT * len(us)], us, first)
 
         w1_raw = [placed("w1_raw%d" % a, AT_W1 + 8 * a, [P, PACK, H], F32) for a in range(2)]
         w1_rows = w1.rearrange("(a p j) c -> a p j c", a=2, j=PACK)
+        nc.sync.dma_start(wg2_rows[1][:], wg2[:, second])
+        nc.sync.dma_start(w1_raw[0][:], w1_rows[0])
+        spread_scales(plain_scale, plain_rows, 96, slice(H + UNIT, H + S))
+        nc.sync.dma_start(w1_raw[1][:], w1_rows[1])
+
+        turned = turn_wg2(wg2_rows[1][:], 7)
+        deal_wg2(turned, 0, second, 4)
+        place_plain("h2_second0", AT_H2 + 4, sums_in_bank((0, 1), second, 3)[:], (0, 1), second)
+        deal_wg2(turned, 1, second, 5)
+        acc_second = sums_in_bank((2, 3), second, 6)
+        place_plain("h2_second2", AT_H2 + 6, acc_second[:, first], (2,), second)
+
         z_pairs = placed("z_pairs", AT_Z_PAIRS, [P, 2 * T2 * 2], BF16)
         w1_woven = z_pairs[:, 2 * T2 :]
         for a in range(2):
-            nc.sync.dma_start(w1_raw[a][:], w1_rows[a])
             weave(w1_woven[:, PACK * H * a : PACK * H * (a + 1)], w1_raw[a][:])
-
-        deal_wg2(turned_late, slice(2, 4), late, 4)
-        acc_late.append(paired_sums((3, 2), late, 6))
-        for u in range(1, PACK):
-            deal_wg2(turned_middle, slice(u, u + 1), middle, 4 + u % 2)
+        acc_high = [sums_in_bank((u,), high, at) for u, at in enumerate((0, 1, 2, 7))]
 
         for b in range(2):
             nc.sync.dma_start(
                 gain_rows[PACK * b : PACK * (b + 1), :].rearrange("t (q i) -> t q i", i=8),
                 gain[PASS * b : PASS * (b + 1)].rearrange("(q t i) -> t q i", t=PACK, i=8),
             )
-        gain_turned = bank("gain_turned", 5)
+        gain_turned = bank("gain_turned", 4)
         nc.tensor.transpose(gain_turned[:, 0:P], gain_rows[:], ident[:])
         gains = held("gains", [P, 2 * PACK], F32)
         nc.scalar.copy(gains[:], gain_turned[:, 0 : 2 * PACK])
@@ -263,59 +264,46 @@ def tile_list_terrain_weave_kernel(
                 v_1[:].rearrange("p (t q i) -> p q t i", t=PACK, i=8), tab_1[:].indirect(entries(list1, cols))
             )
             v[1].append([v_1[:, P * t : P * (t + 1)] for t in range(PACK)])
-        spread_scales(v_scale, v_scale_sorted, 0)
+        spread_scales(v_scale, v_scale_sorted, 0, slice(0, S))
 
-        h2_waiting = placed("h2_waiting", AT_H2 + 6, [P, 4 * BANK], F32)
-        for u in range(1, PACK):
-            h = h2_waiting[:, BANK * (u - 1) : BANK * u]
-            nc.scalar.activation(h, acc_middle[u][:], ACT.Abs)
-            place(u, h, wg2_t[:, u, middle], list4, middle)
-        for n, (u, acc) in enumerate(((0, acc_late[0][:, second]), (3, acc_late[1][:, first]))):
-            h = h2_waiting[:, 3 * BANK + UNIT * n : 3 * BANK + UNIT * (n + 1)]
-            nc.scalar.activation(h, acc, ACT.Abs)
-            place(u, h, wg2_t[:, u, late], list4, late)
+        load_dealt(wg2_high[:], wg2, high)
+
+        place_plain("h2_second3", AT_H2 + 7, acc_second[:, second], (3,), second)
+        for u in range(PACK - 1):
+            place_plain("h2_high%d" % u, AT_H2 + 8 + 2 * u, acc_high[u][:], (u,), high)
+        place_plain("h2_third3", AT_H2 + 14, acc_high[3][:, first], (3,), slice(BANK, S - UNIT))
 
         pieces = [first, second, high]
-
-        def blend_at(i, b):
-            return AT_BLEND + ((4, 8), (0, 12), (16, 24))[i][b]
+        blend_raw, blend_woven, bc, bs = [], [], [], []
 
         def load_blend(i):
             raw = []
             cols = pieces[i]
             for b in range(2):
-                raw.append(placed("blend_raw%d%d" % (i, b), blend_at(i, b), [P, PACK, cols.stop - cols.start], F32))
+                raw.append(placed("blend_raw%d%d" % (i, b), AT_BLEND_RAW[i][b], [P, PACK, cols.stop - cols.start], F32))
                 rows = blend[PASS * b : PASS * (b + 1), cols]
                 rows = rows.rearrange("(q t i) m -> t q i m", t=PACK, i=8)
                 for t in range(PACK):
                     nc.sync.dma_start(raw[b][:, t, :], rows[t])
-            return raw
-
-        blend_raw = [load_blend(0)]
-        woven_at = [AT_BLEND_WOVEN, AT_A_PLANES + 4, blend_at(1, 0)]
-        bc, bs = [], []
-
-        blend_woven = []
+            blend_raw.append(raw)
 
         def weave_blend(i, b):
             width = pieces[i].stop - pieces[i].start
             if b == 0:
-                blend_woven.append(placed("blend_woven%d" % i, woven_at[i], [P, 2 * PACK * width], BF16))
+                blend_woven.append(placed("blend_woven%d" % i, AT_BLEND_WOVEN[i], [P, 2 * PACK * width], BF16))
             weave(blend_woven[i][:, PACK * width * b : PACK * width * (b + 1)], blend_raw[i][b][:])
 
         def quantize_blend(i):
             width = pieces[i].stop - pieces[i].start
             bc.append(placed("bc%d" % i, AT_BC[i], [P, 2 * width], U32))
-            bs.append(held("bs%d" % i, [P, 2 * width], U8))
+            if i == 0:
+                bs.append(placed("bs0", AT_H2 + 13, [P, 2 * width], U8))
+            else:
+                bs.append(held("bs%d" % i, [P, 2 * width], U8))
             quantize(bc[i][:], bs[i][:], blend_woven[i][:])
 
-        weave_blend(0, 0)
-        weave_blend(0, 1)
-        quantize_blend(0)
-
-        a_planes = placed("a_planes", AT_A_PLANES, [P, 2, PACK, H], BF16)
-        a_woven = placed("a_woven", AT_TAB, [P, 2 * PACK * H], BF16)
-        a_banks = (4, 5, 7, 0, 1, 2, 3, 4)
+        a_woven = placed("a_woven", AT_A_WOVEN, [P, 2 * PACK * H], BF16)
+        a_banks = (3, 5, 4, 0, 1, 2, 6, 3)
         acc_a = {}
 
         def project(b, t, a):
@@ -333,43 +321,39 @@ def tile_list_terrain_weave_kernel(
             )
 
         for b in range(2):
+            a_planes = placed("a_planes%d" % b, AT_A_PLANES[b], [P, PACK, H], BF16)
             for t in range(PACK):
                 project(b, t, 0)
                 project(b, t, 1)
                 nc.scalar.activation(
-                    a_planes[:, b, t, :].rearrange("p (u m) -> p u m", u=PACK),
+                    a_planes[:, t, :].rearrange("p (u m) -> p u m", u=PACK),
                     acc_a[b, t][:].rearrange("p (m u) -> p u m", u=PACK),
                     ACT.Copy,
                     scale=gains[:, PACK * b + t : PACK * b + t + 1],
                 )
-            weave(a_woven[:, PACK * H * b : PACK * H * (b + 1)], a_planes[:, b])
+            weave(a_woven[:, PACK * H * b : PACK * H * (b + 1)], a_planes[:])
         ac = held("ac", [P, 2 * H], U32)
-        asc = held("asc", [P, 2 * H], U8)
+        asc = placed("asc", AT_H2 + 12, [P, 2 * H], U8)
         quantize(ac[:], asc[:], a_woven[:])
 
+        load_blend(0)
         list3 = load_list("list3", offs3)
         wg1_t = placed("wg1", AT_WG1, [P, PACK, S], F32)
-
-        def load_wg1(cols):
-            rows = wg1.rearrange("(q t) m -> q t m", t=PACK)[:, :, cols]
-            for q in (0, 2, 1, 3):
-                nc.sync.dma_start(wg1_t[32 * q : 32 * q + 32, :, cols], rows)
-
-        blend_raw.append(load_blend(1))
-        load_wg1(low)
-        blend_raw.append(load_blend(2))
-        load_wg1(high)
-        early_biases = placed("early_biases", AT_W1, [P, PACK], F32)
+        load_blend(1)
+        load_dealt(wg1_t[:, :, low], wg1, low)
+        load_blend(2)
+        load_dealt(wg1_t[:, :, high], wg1, high)
         biases = held("biases", [P, PACK], F32)
-        for dst in (early_biases, biases):
-            nc.sync.dma_start(dst[:], bias.rearrange("(p t) -> p t", t=PACK))
+        nc.sync.dma_start(biases[:], bias.rearrange("(p t) -> p t", t=PACK))
         for q in range(QUADS):
             nc.sync.dma_start(w3s[32 * q : 32 * q + 4, :].bitcast(I32), w3_scales[0, 4 * q : 4 * q + 4, :].bitcast(I32))
+        w3c = held("w3c", [P, N], U32)
+        nc.sync.dma_start(w3c[:].bitcast(I32), w3_words[0].rearrange("p c i -> p (c i)").bitcast(I32))
 
-        h2_late = placed("h2_late", AT_A_PLANES, [P, UNIT], F32)
-        nc.scalar.activation(h2_late[:], acc_late[1][:, second], ACT.Abs)
-        place(2, h2_late[:], wg2_t[:, 2, late], list4, late)
-
+        weave_blend(0, 0)
+        weave_blend(0, 1)
+        quantize_blend(0)
+        place_plain("h2_last3", AT_BLEND_RAW[0][1] + 2, acc_high[3][:, second], (3,), slice(S - UNIT, S))
         weave_blend(1, 0)
         weave_blend(1, 1)
         quantize_blend(1)
@@ -390,11 +374,11 @@ def tile_list_terrain_weave_kernel(
             return acc
 
         h1_at = [
-            (blend_at(1, 1), blend_at(1, 1) + 1, blend_at(1, 1) + 2),
-            (blend_at(2, 0), blend_at(2, 1), blend_at(2, 1) + 1),
-            (AT_W1 + 6, AT_W1 + 8, AT_W1 + 10),
+            [AT_BLEND_RAW[1][1] + n for n in range(3)],
+            [AT_BLEND_RAW[2][0], AT_BLEND_RAW[2][1], AT_BLEND_RAW[2][1] + 1],
+            [AT_W1 + 6, AT_W1 + 8, AT_W1 + 10],
         ]
-        h1_last = placed("h1_last", blend_at(2, 1) + 2, [P, S], F32)
+        h1_last = placed("h1_last", AT_BLEND_RAW[2][1] + 2, [P, S], F32)
         last_sums = []
         for i, cols in enumerate(pieces):
             sums = [blended_sum(i, u) for u in range(PACK)]
@@ -413,18 +397,14 @@ def tile_list_terrain_weave_kernel(
                     nc.scalar.copy(h1_last[:, pieces[done]], last_sums[done])
         place(3, h1_last[:], wg1_t[:, 3, :], list3, slice(0, S))
 
-        def relu(u, cols, source):
+        def relu(u):
             nc.scalar.activation(
-                z_pairs[:].rearrange("p (h t e) -> p h t e", h=2, e=2)[:, u // 2, cols, u % 2],
-                pages[u][:, cols], ACT.Relu, bias=source[:, u : u + 1],
+                z_pairs[:].rearrange("p (h t e) -> p h t e", h=2, e=2)[:, u // 2, :, u % 2],
+                pages[u][:], ACT.Relu, bias=biases[:, u : u + 1],
             )
 
-        relu(0, slice(0, T2), early_biases)
-        relu(2, slice(0, T2), early_biases)
-        relu(1, slice(0, W3_BEHIND), early_biases)
-        relu(1, slice(W3_BEHIND, T2), biases)
-        w3c = placed("w3c", AT_W1, [P, N], U32)
-        nc.sync.dma_start(w3c[:].bitcast(I32), w3_words[0].rearrange("p c i -> p (c i)").bitcast(I32))
+        for u in (0, 2, 1):
+            relu(u)
         pair_words = z_pairs[:].bitcast(F32).rearrange("p (h t) -> p t h", h=2)
         groups = [(128, 128), (256, 256), (256, 256), (256, 512)]
         widths = [width for group in groups for width in group]
@@ -460,10 +440,19 @@ def tile_list_terrain_weave_kernel(
                 stop=True,
             )
 
+        done = 0
+        for group in groups:
+            mine = range(done, done + len(group))
+            done = mine.stop
+            for c in mine:
+                last_relu(c)
+            for c in mine:
+                quantize(zc[:, parts[c]], zs[:, parts[c]], z_part[c])
+
         filled = []
 
         def staging(cols):
-            at = AT_BLEND + cols.start * PACK * 4 // 1024
+            at = AT_STAGED + cols.start * PACK * 4 // 1024
             return placed("staged%d" % cols.start, at, [P, PACK, cols.stop - cols.start], F32)
 
         def fill_and_empty(copy, dst, blocks, cols):
@@ -500,14 +489,6 @@ def tile_list_terrain_weave_kernel(
             fill_and_empty(nc.scalar.copy, staged[:, block, high], block, halves[1])
             nc.sync.dma_start(out_rows[:, block, halves[1]], staged[:, block, high])
 
-        done = 0
-        for group in groups:
-            mine = range(done, done + len(group))
-            done = mine.stop
-            for c in mine:
-                last_relu(c)
-            for c in mine:
-                quantize(zc[:, parts[c]], zs[:, parts[c]], z_part[c])
         narrow_features(first, 1)
         narrow_features(second, 2)
         narrow_features(high, 1)

@@ -168,7 +168,8 @@ def tile_list_terrain_weave_kernel(
             nc.vector.tensor_tensor(pages[u][:].indirect(entries(lst, cols)), h, factor, MULT)
 
         wg2_low = placed("wg2_low", AT_WG2, [P, PACK, BANK], F32)
-        wg2_high = placed("wg2_high", AT_WG2 + 8, [P, PACK, BANK], F32)
+        third, fourth = slice(BANK, S - UNIT), slice(S - UNIT, S)
+        wg2_high = [placed("wg2_high%d" % n, AT_WG2 + 8 + 4 * n, [P, PACK, UNIT], F32) for n in range(2)]
 
         def turn_wg2(rows, at_bank):
             turned = bank("wg2_turned", at_bank)
@@ -214,7 +215,7 @@ def tile_list_terrain_weave_kernel(
             h = placed(name, at, [P, len(us) * width], F32)
             nc.scalar.activation(h[:], acc, ACT.Abs)
             for n, u in enumerate(us):
-                factor = wg2_low[:, u, cols] if cols.stop <= BANK else wg2_high[:, u, cols.start - BANK : cols.stop - BANK]
+                factor = wg2_low[:, u, cols] if cols.stop <= BANK else wg2_high[(cols.start - BANK) // UNIT][:, u, :]
                 place(u, h[:, width * n : width * (n + 1)], factor, list4, cols)
 
         for n, us in enumerate(((0,), (1,), (2, 3))):
@@ -238,7 +239,7 @@ def tile_list_terrain_weave_kernel(
         w1_woven = z_pairs[:, 2 * T2 :]
         for a in range(2):
             weave(w1_woven[:, PACK * H * a : PACK * H * (a + 1)], w1_raw[a][:])
-        acc_high = [sums_in_bank((u,), high, at) for u, at in enumerate((0, 1, 2, 7))]
+        acc_high = [sums_in_bank(us, cols, at) for us, cols, at in (((0, 1), third, 0), ((2, 3), third, 1), ((0, 1), fourth, 2), ((2, 3), fourth, 7))]
 
         for b in range(2):
             nc.sync.dma_start(
@@ -266,12 +267,14 @@ def tile_list_terrain_weave_kernel(
             v[1].append([v_1[:, P * t : P * (t + 1)] for t in range(PACK)])
         spread_scales(v_scale, v_scale_sorted, 0, slice(0, S))
 
-        load_dealt(wg2_high[:], wg2, high)
+        for n, cols in enumerate((third, fourth)):
+            load_dealt(wg2_high[n][:], wg2, cols)
 
         place_plain("h2_second3", AT_H2 + 7, acc_second[:, second], (3,), second)
-        for u in range(PACK - 1):
-            place_plain("h2_high%d" % u, AT_H2 + 8 + 2 * u, acc_high[u][:], (u,), high)
-        place_plain("h2_third3", AT_H2 + 14, acc_high[3][:, first], (3,), slice(BANK, S - UNIT))
+        for pair in range(2):
+            place_plain("h2_third%d" % pair, AT_H2 + 8 + 2 * pair, acc_high[pair][:], (2 * pair, 2 * pair + 1), third)
+        place_plain("h2_fourth0", AT_H2 + 12, acc_high[2][:], (0, 1), fourth)
+        place_plain("h2_fourth2", AT_H2 + 14, acc_high[3][:, first], (2,), fourth)
 
         pieces = [first, second, high]
         blend_raw, blend_woven, bc, bs = [], [], [], []
@@ -353,7 +356,7 @@ def tile_list_terrain_weave_kernel(
         weave_blend(0, 0)
         weave_blend(0, 1)
         quantize_blend(0)
-        place_plain("h2_last3", AT_BLEND_RAW[0][1] + 2, acc_high[3][:, second], (3,), slice(S - UNIT, S))
+        place_plain("h2_last3", AT_BLEND_RAW[0][1] + 2, acc_high[3][:, second], (3,), fourth)
         weave_blend(1, 0)
         weave_blend(1, 1)
         quantize_blend(1)

@@ -89,8 +89,8 @@ def tile_list_terrain_weave_kernel(
                     src[first + 8 * q : first + 8 * q + 8, cols].bitcast(I32),
                 )
 
-        def load_dealt(dst, src, cols):
-            rows = src.rearrange("(q t) m -> q t m", t=PACK)[:, :, cols]
+        def load_dealt(dst, src, us, cols):
+            rows = src.rearrange("(q t) m -> q t m", t=PACK)[:, us, cols]
             for q in (0, 2, 1, 3):
                 nc.sync.dma_start(dst[32 * q : 32 * q + 32], rows)
 
@@ -112,6 +112,7 @@ def tile_list_terrain_weave_kernel(
             nc.vector.quantize_mx(out=codes.bitcast(FP8X4), scales=scales, in_=woven)
 
         low, high = slice(0, BANK), slice(BANK, S)
+        all_pages = slice(0, PACK)
         first, second = slice(0, UNIT), slice(UNIT, BANK)
 
         sc2 = load_scale_rows(nc.vector, placed("sc2", AT_SCALES, [P, T], U8), tab2_scales, 96)
@@ -268,7 +269,7 @@ def tile_list_terrain_weave_kernel(
         spread_scales(v_scale, v_scale_sorted, 0, slice(0, S))
 
         for n, cols in enumerate((third, fourth)):
-            load_dealt(wg2_high[n][:], wg2, cols)
+            load_dealt(wg2_high[n][:], wg2, all_pages, cols)
 
         place_plain("h2_second3", AT_H2 + 7, acc_second[:, second], (3,), second)
         for pair in range(2):
@@ -343,9 +344,12 @@ def tile_list_terrain_weave_kernel(
         list3 = load_list("list3", offs3)
         wg1_t = placed("wg1", AT_WG1, [P, PACK, S], F32)
         load_blend(1)
-        load_dealt(wg1_t[:, :, low], wg1, low)
+        load_dealt(wg1_t[:, :, first], wg1, all_pages, first)
+        load_dealt(wg1_t[:, 0:1, second], wg1, slice(0, 1), second)
         load_blend(2)
-        load_dealt(wg1_t[:, :, high], wg1, high)
+        load_dealt(wg1_t[:, 1:PACK, second], wg1, slice(1, PACK), second)
+        load_dealt(wg1_t[:, 0:1, high], wg1, slice(0, 1), high)
+        load_dealt(wg1_t[:, 1:PACK, high], wg1, slice(1, PACK), high)
         biases = held("biases", [P, PACK], F32)
         nc.sync.dma_start(biases[:], bias.rearrange("(p t) -> p t", t=PACK))
         for q in range(QUADS):

@@ -416,13 +416,21 @@ def tile_list_terrain_weave_kernel(
         groups = [(128, 128), (256, 256), (256, 256), (256, 512)]
         widths = [width for group in groups for width in group]
         parts = [slice(sum(widths[:c]), sum(widths[: c + 1])) for c in range(len(widths))]
+        shared = slice(T2 - P, T2)
         z_part = []
         for group in groups:
             start = parts[len(z_part)].start
+            stop = start + sum(group)
             woven = placed("z_woven%d" % start, AT_TAB + start * PACK * 2 // 1024, [P, PACK * sum(group)], BF16)
-            nc.scalar.copy(
-                woven[:].bitcast(F32).rearrange("p (t h) -> p t h", h=2), pair_words[:, start : start + sum(group), :]
-            )
+            words = woven[:].bitcast(F32).rearrange("p (t h) -> p t h", h=2)
+            cut = min(stop, T2 - UNIT)
+            nc.scalar.copy(words[:, 0 : cut - start], pair_words[:, start:cut, :])
+            if cut < stop:
+                nc.vector.tensor_copy(words[:, cut - start :], pair_words[:, cut:stop, :])
+                nc.scalar.activation(
+                    woven[:].rearrange("p (t u) -> p t u", u=PACK)[:, shared.start - start :, PACK - 1],
+                    pages[PACK - 1][:, shared], ACT.Relu, bias=biases[:, PACK - 1 : PACK],
+                )
             for cols in parts[len(z_part) : len(z_part) + len(group)]:
                 z_part.append(woven[:, PACK * (cols.start - start) : PACK * (cols.stop - start)])
 
@@ -431,9 +439,10 @@ def tile_list_terrain_weave_kernel(
         out_rows = out.rearrange("(nb p) t -> p nb t", p=P)
 
         def last_relu(c):
+            cols = slice(parts[c].start, min(parts[c].stop, shared.start))
             nc.vector.tensor_scalar(
-                z_part[c].rearrange("p (t u) -> p t u", u=PACK)[:, :, PACK - 1],
-                pages[PACK - 1][:, parts[c]], biases[:, PACK - 1 : PACK], 0.0, ADD, MAX,
+                z_part[c].rearrange("p (t u) -> p t u", u=PACK)[:, 0 : cols.stop - cols.start, PACK - 1],
+                pages[PACK - 1][:, cols], biases[:, PACK - 1 : PACK], 0.0, ADD, MAX,
             )
 
         def product(acc, nb, cols):
@@ -484,17 +493,20 @@ def tile_list_terrain_weave_kernel(
         def wide_features(cols):
             staged = staging(cols)
             halves = [slice(cols.start, cols.start + BANK), slice(cols.start + BANK, cols.stop)]
-            block = slice(0, 1)
-            fill_and_empty(nc.vector.tensor_copy, staged[:, block, low], block, halves[0])
-            nc.sync.dma_start(out_rows[:, block, halves[0]], staged[:, block, low])
-            for nb in range(1, PACK):
+            early, copies = slice(0, 2), (nc.vector.tensor_copy, nc.scalar.copy)
+            for nb in range(early.stop):
+                block = slice(nb, nb + 1)
+                fill_and_empty(copies[nb], staged[:, block, low], block, halves[0])
+                nc.sync.dma_start(out_rows[:, block, halves[0]], staged[:, block, low])
+            for nb in range(early.stop, PACK):
                 block = slice(nb, nb + 1)
                 fill_and_empty(nc.scalar.copy, staged[:, block, low], block, halves[0])
                 fill_and_empty(nc.vector.tensor_copy, staged[:, block, high], block, halves[1])
                 nc.sync.dma_start(out_rows[:, block, cols], staged[:, block, :])
-            block = slice(0, 1)
-            fill_and_empty(nc.scalar.copy, staged[:, block, high], block, halves[1])
-            nc.sync.dma_start(out_rows[:, block, halves[1]], staged[:, block, high])
+            for nb in range(early.stop):
+                block = slice(nb, nb + 1)
+                fill_and_empty(copies[nb], staged[:, block, high], block, halves[1])
+            nc.sync.dma_start(out_rows[:, early, halves[1]], staged[:, early, high])
 
         narrow_features(first, 1)
         narrow_features(second, 2)

@@ -127,10 +127,9 @@ def tile_list_terrain_weave_kernel(
         nc.sync.dma_start(w2_raw[:].bitcast(I32), w2_words.bitcast(I32).rearrange("a p c -> p a c"))
         tab2_1 = load_table_words("tab2_1", tab2_words, 1, AT_TAB2)
         plain_rows = held("plain_rows", [P, H + S], U8)
-        nc.gpsimd.tensor_copy(
-            plain_rows[:, 0:H].rearrange("p (u m) -> p u m", u=PACK),
-            w2s_raw[:].rearrange("p (m u) -> p u m", u=PACK),
-        )
+        w2s_by_page = w2s_raw[:].rearrange("p (m u) -> p u m", u=PACK)
+        nc.gpsimd.tensor_copy(plain_rows[:, 0:P], w2s_by_page[:, 0])
+        nc.gpsimd.tensor_copy(plain_rows[:, P + S :].rearrange("p (u m) -> p u m", u=PACK - 1), w2s_by_page[:, 1:PACK])
         ident = held("ident", [P, P], F32)
         make_identity(nc, ident[:])
         plain_scale = zeroed(nc.gpsimd, "plain_scale", 2 * (H + S))
@@ -141,9 +140,10 @@ def tile_list_terrain_weave_kernel(
 
         v2_scale_picked = held("v2_scale_picked", [P, S], U8)
         nc.vector.tensor_copy(v2_scale_picked[:], sc2[:].indirect(list2[:]))
-        nc.vector.tensor_copy(plain_rows[:, H:].bitcast(I32), v2_scale_picked[:].bitcast(I32))
-        spread_scales(plain_scale, plain_rows, 96, slice(0, H + UNIT))
+        nc.vector.tensor_copy(plain_rows[:, P : P + S].bitcast(I32), v2_scale_picked[:].bitcast(I32))
+        spread_scales(plain_scale, plain_rows, 96, slice(0, P + UNIT))
         list4 = load_list("list4", offs4)
+        spread_scales(plain_scale, plain_rows, 96, slice(P + UNIT, H + S))
 
         v_scale_picked = held("v_scale_picked", [P, S], U8)
         nc.vector.tensor_copy(v_scale_picked[:], sc1[:].indirect(list1[:]))
@@ -195,12 +195,13 @@ def tile_list_terrain_weave_kernel(
         def plain_sum(acc, u, cols):
             for a in range(2):
                 at = (H + S) * a
+                w2s_at = at + (S + P * u if u else 0)
                 nc.tensor.matmul_mx(
                     out=acc,
                     lhsT=w2c[:, a, 256 * u : 256 * (u + 1)].bitcast(FP4X4),
-                    lhsT_scale=plain_scale[:, at + P * u : at + P * (u + 1)],
+                    lhsT_scale=plain_scale[:, w2s_at : w2s_at + P],
                     rhs=v2[a][:, cols].bitcast(FP8X4),
-                    rhs_scale=plain_scale[:, at + H + cols.start : at + H + cols.stop],
+                    rhs_scale=plain_scale[:, at + P + cols.start : at + P + cols.stop],
                     start=(a == 0),
                     stop=(a == 1),
                 )
@@ -226,8 +227,6 @@ def tile_list_terrain_weave_kernel(
         w1_rows = w1.rearrange("(a p j) c -> a p j c", a=2, j=PACK)
         nc.sync.dma_start(wg2_rows[1][:], wg2[:, second])
         nc.sync.dma_start(w1_raw[0][:], w1_rows[0])
-        spread_scales(plain_scale, plain_rows, 96, slice(H + UNIT, H + S))
-        nc.sync.dma_start(w1_raw[1][:], w1_rows[1])
 
         turned = turn_wg2(wg2_rows[1][:], 7)
         deal_wg2(turned, 0, second, 4)
@@ -238,8 +237,7 @@ def tile_list_terrain_weave_kernel(
 
         z_pairs = placed("z_pairs", AT_Z_PAIRS, [P, 2 * T2 * 2], BF16)
         w1_woven = z_pairs[:, 2 * T2 :]
-        for a in range(2):
-            weave(w1_woven[:, PACK * H * a : PACK * H * (a + 1)], w1_raw[a][:])
+        weave(w1_woven[:, 0 : PACK * H], w1_raw[0][:])
         acc_high = [sums_in_bank(us, cols, at) for us, cols, at in (((0, 1), third, 0), ((2, 3), third, 1), ((0, 1), fourth, 2), ((2, 3), fourth, 7))]
 
         for b in range(2):
@@ -253,6 +251,8 @@ def tile_list_terrain_weave_kernel(
         nc.scalar.copy(gains[:], gain_turned[:, 0 : 2 * PACK])
 
         tab_0 = load_table_words("tab_0", tab_words, 0, AT_TAB)
+        nc.sync.dma_start(w1_raw[1][:], w1_rows[1])
+        weave(w1_woven[:, PACK * H :], w1_raw[1][:])
         v_0 = placed("v_0", AT_V, [P, S], U32)
         nc.vector.tensor_copy(v_0[:].rearrange("p (t q i) -> p q t i", t=PACK, i=8), tab_0[:].indirect(list1[:]))
         v = [[[v_0[:, 2 * P * t + P * b : 2 * P * t + P * (b + 1)] for t in range(PACK)] for b in range(2)], []]

@@ -132,7 +132,7 @@ def tile_list_terrain_weave_kernel(
         nc.gpsimd.tensor_copy(plain_rows[:, P + S :].rearrange("p (u m) -> p u m", u=PACK - 1), w2s_by_page[:, 1:PACK])
         ident = held("ident", [P, P], F32)
         make_identity(nc, ident[:])
-        plain_scale = zeroed(nc.gpsimd, "plain_scale", 2 * (H + S))
+        plain_scale = zeroed(nc.vector, "plain_scale", 2 * (H + S))
         v_scale = zeroed(nc.gpsimd, "v_scale", 2 * S)
         w3s = zeroed(nc.gpsimd, "w3s", N)
         gain_rows = held("gain_rows", [P, P], F32)

from contextlib import ExitStack

import concourse.mybir as mybir
from concourse.masks import make_identity

K, H, N, T, S, T2 = 1024, 512, 512, 4096, 1024, 2048
FLOPS = 2 * (K * S * H + S * H * S + K * H * S + H * N * T2)

F32 = mybir.dt.float32
BF16 = mybir.dt.bfloat16
I32 = mybir.dt.int32
U32 = mybir.dt.uint32
U16 = mybir.dt.uint16
U8 = mybir.dt.uint8
FP8X4 = mybir.dt.float8_e4m3fn_x4
FP4X4 = mybir.dt.float4_e2m1fn_x4
ACT = mybir.ActivationFunctionType
MULT = mybir.AluOpType.mult
ADD = mybir.AluOpType.add
MAX = mybir.AluOpType.max

P = 128
PACK = 4
PASS = P * PACK
BANK = 512
QUADS = 4
UNIT = 256

AT_TAB2 = 0
AT_TAB = 32
AT_A_WOVEN = 32
AT_A_PLANES = (40, 58)
AT_W1 = 64
AT_STAGED = 80
AT_BLEND_RAW = ((80, 84), (48, 52), (96, 104))
AT_BLEND_WOVEN = (56, 60, 88)
AT_WG2 = 112
AT_H2 = 128
AT_V = 144
AT_SCALES = 152
AT_BC = (152, 154, 156)
AT_WG1 = 160
AT_Z_PAIRS = 176


def tile_list_terrain_weave_kernel(
    tc, tab_words, tab_scales, tab2_words, tab2_scales, offs, offs2, offs3, offs4, w1, gain, blend,
    w2_words, w2_scales, wg1, wg2, bias, w3_words, w3_scales, out,
):
    nc = tc.nc
    with ExitStack() as ctx:
        lists = ctx.enter_context(tc.tile_pool(name="lists", bufs=1))
        sb = ctx.enter_context(tc.tile_pool(name="sb", bufs=1))
        reuse = ctx.enter_context(tc.tile_pool(name="reuse", bufs=1))
        psum = ctx.enter_context(tc.psum_pool(name="psum", bufs=1))

        def held(name, shape, dtype):
            return sb.tile(shape, dtype, name=name, align_bytes=64)

        def ring(tag, shape, dtype):
            return sb.tile(shape, dtype, name=tag, tag=tag, bufs=2, align_bytes=64)

        def placed(name, kib, shape, dtype):
            return reuse.tile(shape, dtype, name=name, align_bytes=64, offset=int(kib * 1024))

        def bank(name, index):
            return psum.tile([P, BANK], F32, name=name, tag="bank%d" % index)

        def load_list(name, src):
            dst = lists.tile([P, S // 16], U16, name=name)
            nc.sync.dma_start(dst[:], src)
            return dst

        def zeroed(engine, name, width):
            dst = held(name, [P, width], U8)
            engine.memset(dst[:].bitcast(I32), 0)
            return dst

        def load_scale_rows(engine, dst, src, first):
            nc.sync.dma_start(dst[first : first + 32, :].bitcast(I32), src.bitcast(I32).rearrange("a q t -> q a t"))
            for rest in {0: (slice(32, 64), slice(64, P)), 96: (slice(0, 96),)}[first]:
                engine.memset(dst[rest, :].bitcast(I32), 0)
            return dst

        def spread_scales(dst, src, first, cols):
            for q in range(QUADS):
                nc.sync.dma_start(
                    dst[32 * q : 32 * q + 4, :].rearrange("r (a c) -> r a c", a=2)[:, :, cols].bitcast(I32),
                    src[first + 8 * q : first + 8 * q + 8, cols].bitcast(I32),
                )

        def load_dealt(dst, src, us, cols):
            rows = src.rearrange("(q t) m -> q t m", t=PACK)[:, us, cols]
            for q in (0, 2, 1, 3):
                nc.sync.dma_start(dst[32 * q : 32 * q + 32], rows)

        def load_table_words(name, src, a, at):
            dst = placed(name, at + 16 * a, [P, T], U32)
            nc.sync.dma_start(dst[:].bitcast(I32), src[a].rearrange("p t i -> p (t i)").bitcast(I32))
            return dst

        def entries(lst, cols):
            return lst[:, cols.start // 16 : cols.stop // 16]

        def weave(dst, planes):
            nc.scalar.copy(
                dst.rearrange("p (c i t) -> p c t i", i=4, t=PACK),
                planes.rearrange("p t (c i) -> p c t i", i=4),
            )

        def quantize(codes, scales, woven):
            nc.vector.quantize_mx(out=codes.bitcast(FP8X4), scales=scales, in_=woven)

        low, high = slice(0, BANK), slice(BANK, S)
        all_pages = slice(0, PACK)
        first, second = slice(0, UNIT), slice(UNIT, BANK)

        sc2 = load_scale_rows(nc.vector, placed("sc2", AT_SCALES, [P, T], U8), tab2_scales, 96)
        list2 = load_list("list2", offs2)
        w2s_raw = load_scale_rows(nc.vector, held("w2s_raw", [P, H], U8), w2_scales, 96)
        list1 = load_list("list1", offs)
        sc1 = load_scale_rows(nc.gpsimd, placed("sc1", AT_SCALES + 4, [P, T], U8), tab_scales, 0)
        wg2_rows = [held("wg2_rows%d" % n, [P, UNIT], F32) for n in range(2)]
        nc.sync.dma_start(wg2_rows[0][:], wg2[:, first])
        tab2_0 = load_table_words("tab2_0", tab2_words, 0, AT_TAB2)
        w2_raw = held("w2_raw", [P, 2, 2 * H], U8)
        nc.sync.dma_start(w2_raw[:].bitcast(I32), w2_words.bitcast(I32).rearrange("a p c -> p a c"))
        tab2_1 = load_table_words("tab2_1", tab2_words, 1, AT_TAB2)
        plain_rows = held("plain_rows", [P, H + S], U8)
        w2s_by_page = w2s_raw[:].rearrange("p (m u) -> p u m", u=PACK)
        nc.gpsimd.tensor_copy(plain_rows[:, 0:P], w2s_by_page[:, 0])
        nc.gpsimd.tensor_copy(plain_rows[:, P + S :].rearrange("p (u m) -> p u m", u=PACK - 1), w2s_by_page[:, 1:PACK])
        ident = held("ident", [P, P], F32)
        make_identity(nc, ident[:])
        plain_scale = zeroed(nc.vector, "plain_scale", 2 * (H + S))
        v_scale = zeroed(nc.gpsimd, "v_scale", 2 * S)
        w3s = zeroed(nc.gpsimd, "w3s", N)
        gain_rows = held("gain_rows", [P, P], F32)
        nc.gpsimd.memset(gain_rows[:], 0.0)

        v2_scale_picked = held("v2_scale_picked", [P, S], U8)
        nc.vector.tensor_copy(v2_scale_picked[:], sc2[:].indirect(list2[:]))
        nc.vector.tensor_copy(plain_rows[:, P : P + S].bitcast(I32), v2_scale_picked[:].bitcast(I32))
        spread_scales(plain_scale, plain_rows, 96, slice(0, P + UNIT))
        list4 = load_list("list4", offs4)
        spread_scales(plain_scale, plain_rows, 96, slice(P + UNIT, H + S))

        v_scale_picked = held("v_scale_picked", [P, S], U8)
        nc.vector.tensor_copy(v_scale_picked[:], sc1[:].indirect(list1[:]))
        v_scale_sorted = placed("v_scale_sorted", AT_H2 + 7, [P, S], U8)
        nc.vector.tensor_copy(
            v_scale_sorted[:].bitcast(I32).rearrange("p (t q w) -> p t q w", t=PACK, w=2),
            v_scale_picked[:].bitcast(I32).rearrange("p (q t w) -> p t q w", t=PACK, w=2),
        )

        v2 = [placed("v2_%d" % a, AT_V + 4 * a, [P, S], U32) for a in range(2)]
        nc.vector.tensor_copy(v2[0][:], tab2_0[:].indirect(list2[:]))
        w2c = held("w2c", [P, 2, 2 * H], U8)
        nc.scalar.copy(
            w2c[:].bitcast(U16).rearrange("p a (u m) -> p a u m", u=PACK),
            w2_raw[:].bitcast(U16).rearrange("p a (m u) -> p a u m", u=PACK),
        )
        for cols in (slice(0, UNIT), slice(UNIT, S)):
            nc.vector.tensor_copy(v2[1][:, cols], tab2_1[:].indirect(entries(list2, cols)))

        pages = [placed("page%d" % u, AT_TAB2 + 8 * u, [P, T2], F32) for u in range(PACK)]

        def place(u, h, factor, lst, cols):
            nc.vector.tensor_tensor(pages[u][:].indirect(entries(lst, cols)), h, factor, MULT)

        wg2_low = placed("wg2_low", AT_WG2, [P, PACK, BANK], F32)
        third, fourth = slice(BANK, S - UNIT), slice(S - UNIT, S)
        wg2_high = [placed("wg2_high%d" % n, AT_WG2 + 8 + 4 * n, [P, PACK, UNIT], F32) for n in range(2)]

        def turn_wg2(rows, at_bank):
            turned = bank("wg2_turned", at_bank)
            for c in range(UNIT // P):
                nc.tensor.transpose(turned[:, P * c : P * (c + 1)], rows[:, P * c : P * (c + 1)], ident[:])
            return turned[:, 0:UNIT].rearrange("p (c q u) -> p u c q", q=32, u=PACK)

        def deal_wg2(turned, pair, cols, at_bank):
            us, blocks = slice(2 * pair, 2 * pair + 2), UNIT // P
            repeated = ring("wg2_repeated", [P, 2, blocks, QUADS, 32], F32)
            nc.scalar.copy(repeated[:], turned[:, us].unsqueeze(3).to_broadcast([P, 2, blocks, QUADS, 32]))
            back = bank("wg2_back", at_bank)
            blocks_in = repeated[:].rearrange("p u c g q -> p (u c) (g q)")
            for n in range(2 * blocks):
                nc.tensor.transpose(back[:, P * n : P * (n + 1)], blocks_in[:, n], ident[:])
            nc.scalar.copy(wg2_low[:, us, cols], back[:].rearrange("p (u m) -> p u m", u=2))

        turned = turn_wg2(wg2_rows[0][:], 6)
        for pair in range(2):
            deal_wg2(turned, pair, first, 4 + pair)

        def plain_sum(acc, u, cols):
            for a in range(2):
                at = (H + S) * a
                w2s_at = at + (S + P * u if u else 0)
                nc.tensor.matmul_mx(
                    out=acc,
                    lhsT=w2c[:, a, 256 * u : 256 * (u + 1)].bitcast(FP4X4),
                    lhsT_scale=plain_scale[:, w2s_at : w2s_at + P],
                    rhs=v2[a][:, cols].bitcast(FP8X4),
                    rhs_scale=plain_scale[:, at + P + cols.start : at + P + cols.stop],
                    start=(a == 0),
                    stop=(a == 1),
                )

        def sums_in_bank(us, cols, at_bank):
            acc, width = bank("acc_h2", at_bank), cols.stop - cols.start
            for n, u in enumerate(us):
                plain_sum(acc[:, width * n : width * (n + 1)], u, cols)
            return acc

        def place_plain(name, at, acc, us, cols):
            width = cols.stop - cols.start
            h = placed(name, at, [P, len(us) * width], F32)
            nc.scalar.activation(h[:], acc, ACT.Abs)
            for n, u in enumerate(us):
                factor = wg2_low[:, u, cols] if cols.stop <= BANK else wg2_high[(cols.start - BANK) // UNIT][:, u, :]
                place(u, h[:, width * n : width * (n + 1)], factor, list4, cols)

        for n, us in enumerate(((0,), (1,), (2, 3))):
            place_plain("h2_first%d" % n, AT_H2 + n, sums_in_bank(us, first, n)[:, 0 : UNIT * len(us)], us, first)

        w1_raw = [placed("w1_raw%d" % a, AT_W1 + 8 * a, [P, PACK, H], F32) for a in range(2)]
        w1_rows = w1.rearrange("(a p j) c -> a p j c", a=2, j=PACK)
        nc.sync.dma_start(wg2_rows[1][:], wg2[:, second])
        nc.sync.dma_start(w1_raw[0][:], w1_rows[0])

        turned = turn_wg2(wg2_rows[1][:], 7)
        deal_wg2(turned, 0, second, 4)
        place_plain("h2_second0", AT_H2 + 4, sums_in_bank((0, 1), second, 3)[:], (0, 1), second)
        deal_wg2(turned, 1, second, 5)
        acc_second = sums_in_bank((2, 3), second, 6)
        place_plain("h2_second2", AT_H2 + 6, acc_second[:, first], (2,), second)

        z_pairs = placed("z_pairs", AT_Z_PAIRS, [P, 2 * T2 * 2], BF16)
        w1_woven = z_pairs[:, 2 * T2 :]
        weave(w1_woven[:, 0 : PACK * H], w1_raw[0][:])
        acc_high = [sums_in_bank(us, cols, at) for us, cols, at in (((0, 1), third, 0), ((2, 3), third, 1), ((0, 1), fourth, 2), ((2, 3), fourth, 7))]

        for b in range(2):
            nc.sync.dma_start(
                gain_rows[PACK * b : PACK * (b + 1), :].rearrange("t (q i) -> t q i", i=8),
                gain[PASS * b : PASS * (b + 1)].rearrange("(q t i) -> t q i", t=PACK, i=8),
            )
        gain_turned = bank("gain_turned", 4)
        nc.tensor.transpose(gain_turned[:, 0:P], gain_rows[:], ident[:])
        gains = held("gains", [P, 2 * PACK], F32)
        nc.scalar.copy(gains[:], gain_turned[:, 0 : 2 * PACK])

        tab_0 = load_table_words("tab_0", tab_words, 0, AT_TAB)
        nc.sync.dma_start(w1_raw[1][:], w1_rows[1])
        weave(w1_woven[:, PACK * H :], w1_raw[1][:])
        v_0 = placed("v_0", AT_V, [P, S], U32)
        nc.vector.tensor_copy(v_0[:].rearrange("p (t q i) -> p q t i", t=PACK, i=8), tab_0[:].indirect(list1[:]))
        v = [[[v_0[:, 2 * P * t + P * b : 2 * P * t + P * (b + 1)] for t in range(PACK)] for b in range(2)], []]
        w1c = held("w1c", [P, 2 * H], U32)
        w1s = held("w1s", [P, 2 * H], U8)
        quantize(w1c[:], w1s[:], w1_woven)
        tab_1 = load_table_words("tab_1", tab_words, 1, AT_TAB)
        for b, cols in enumerate((low, high)):
            v_1 = placed("v_1%d" % b, AT_V + 4 + 2 * b, [P, PASS], U32)
            nc.vector.tensor_copy(
                v_1[:].rearrange("p (t q i) -> p q t i", t=PACK, i=8), tab_1[:].indirect(entries(list1, cols))
            )
            v[1].append([v_1[:, P * t : P * (t + 1)] for t in range(PACK)])
        spread_scales(v_scale, v_scale_sorted, 0, slice(0, S))

        for n, cols in enumerate((third, fourth)):
            load_dealt(wg2_high[n][:], wg2, all_pages, cols)

        place_plain("h2_second3", AT_H2 + 7, acc_second[:, second], (3,), second)
        for pair in range(2):
            place_plain("h2_third%d" % pair, AT_H2 + 8 + 2 * pair, acc_high[pair][:], (2 * pair, 2 * pair + 1), third)
        place_plain("h2_fourth0", AT_H2 + 12, acc_high[2][:], (0, 1), fourth)
        place_plain("h2_fourth2", AT_H2 + 14, acc_high[3][:, first], (2,), fourth)

        pieces = [first, second, high]
        blend_raw, blend_woven, bc, bs = [], [], [], []

        def load_blend(i):
            raw = []
            cols = pieces[i]
            for b in range(2):
                raw.append(placed("blend_raw%d%d" % (i, b), AT_BLEND_RAW[i][b], [P, PACK, cols.stop - cols.start], F32))
                rows = blend[PASS * b : PASS * (b + 1), cols]
                rows = rows.rearrange("(q t i) m -> t q i m", t=PACK, i=8)
                for t in range(PACK):
                    nc.sync.dma_start(raw[b][:, t, :], rows[t])
            blend_raw.append(raw)

        def weave_blend(i, b):
            width = pieces[i].stop - pieces[i].start
            if b == 0:
                blend_woven.append(placed("blend_woven%d" % i, AT_BLEND_WOVEN[i], [P, 2 * PACK * width], BF16))
            weave(blend_woven[i][:, PACK * width * b : PACK * width * (b + 1)], blend_raw[i][b][:])

        def quantize_blend(i):
            width = pieces[i].stop - pieces[i].start
            bc.append(placed("bc%d" % i, AT_BC[i], [P, 2 * width], U32))
            if i == 0:
                bs.append(placed("bs0", AT_H2 + 13, [P, 2 * width], U8))
            else:
                bs.append(held("bs%d" % i, [P, 2 * width], U8))
            quantize(bc[i][:], bs[i][:], blend_woven[i][:])

        a_woven = placed("a_woven", AT_A_WOVEN, [P, 2 * PACK * H], BF16)
        a_banks = (3, 5, 4, 0, 1, 2, 6, 3)
        acc_a = {}

        def project(b, t, a):
            cols = slice(2 * P * t + P * b, 2 * P * t + P * (b + 1))
            if a == 0:
                acc_a[b, t] = bank("acc_a", a_banks[PACK * b + t])
            nc.tensor.matmul_mx(
                out=acc_a[b, t][:],
                lhsT=v[a][b][t].bitcast(FP8X4),
                lhsT_scale=v_scale[:, S * a + cols.start : S * a + cols.stop],
                rhs=w1c[:, H * a : H * (a + 1)].bitcast(FP8X4),
                rhs_scale=w1s[:, H * a : H * (a + 1)],
                start=(a == 0),
                stop=(a == 1),
            )

        for b in range(2):
            a_planes = placed("a_planes%d" % b, AT_A_PLANES[b], [P, PACK, H], BF16)
            for t in range(PACK):
                project(b, t, 0)
                project(b, t, 1)
                nc.scalar.activation(
                    a_planes[:, t, :].rearrange("p (u m) -> p u m", u=PACK),
                    acc_a[b, t][:].rearrange("p (m u) -> p u m", u=PACK),
                    ACT.Copy,
                    scale=gains[:, PACK * b + t : PACK * b + t + 1],
                )
            weave(a_woven[:, PACK * H * b : PACK * H * (b + 1)], a_planes[:])
        ac = held("ac", [P, 2 * H], U32)
        asc = placed("asc", AT_H2 + 12, [P, 2 * H], U8)
        quantize(ac[:], asc[:], a_woven[:])

        load_blend(0)
        list3 = load_list("list3", offs3)
        wg1_t = placed("wg1", AT_WG1, [P, PACK, S], F32)
        load_blend(1)
        load_dealt(wg1_t[:, :, first], wg1, all_pages, first)
        load_dealt(wg1_t[:, 0:1, second], wg1, slice(0, 1), second)
        load_blend(2)
        load_dealt(wg1_t[:, 1:PACK, second], wg1, slice(1, PACK), second)
        load_dealt(wg1_t[:, 0:1, high], wg1, slice(0, 1), high)
        load_dealt(wg1_t[:, 1:PACK, high], wg1, slice(1, PACK), high)
        biases = held("biases", [P, PACK], F32)
        nc.sync.dma_start(biases[:], bias.rearrange("(p t) -> p t", t=PACK))
        for q in range(QUADS):
            nc.sync.dma_start(w3s[32 * q : 32 * q + 4, :].bitcast(I32), w3_scales[0, 4 * q : 4 * q + 4, :].bitcast(I32))
        w3c = held("w3c", [P, N], U32)
        nc.sync.dma_start(w3c[:].bitcast(I32), w3_words[0].rearrange("p c i -> p (c i)").bitcast(I32))

        weave_blend(0, 0)
        weave_blend(0, 1)
        quantize_blend(0)
        place_plain("h2_last3", AT_BLEND_RAW[0][1] + 2, acc_high[3][:, second], (3,), fourth)
        weave_blend(1, 0)
        weave_blend(1, 1)
        quantize_blend(1)

        def blended_sum(i, u):
            width = pieces[i].stop - pieces[i].start
            acc = bank("acc_h1", PACK * (i % 2) + u)[:, 0:width]
            for b in range(2):
                nc.tensor.matmul_mx(
                    out=acc,
                    lhsT=ac[:, H * b + P * u : H * b + P * (u + 1)].bitcast(FP8X4),
                    lhsT_scale=asc[:, H * b + P * u : H * b + P * (u + 1)],
                    rhs=bc[i][:, width * b : width * (b + 1)].bitcast(FP8X4),
                    rhs_scale=bs[i][:, width * b : width * (b + 1)],
                    start=(b == 0),
                    stop=(b == 1),
                )
            return acc

        h1_at = [
            [AT_BLEND_RAW[1][1] + n for n in range(3)],
            [AT_BLEND_RAW[2][0], AT_BLEND_RAW[2][1], AT_BLEND_RAW[2][1] + 1],
            [AT_W1 + 6, AT_W1 + 8, AT_W1 + 10],
        ]
        h1_last = placed("h1_last", AT_BLEND_RAW[2][1] + 2, [P, S], F32)
        last_sums = []
        for i, cols in enumerate(pieces):
            sums = [blended_sum(i, u) for u in range(PACK)]
            if i == 1:
                weave_blend(2, 0)
            last_sums.append(sums[PACK - 1])
            for u in (0, 2, 1):
                h = placed("h1_%d%d" % (i, u), h1_at[i][u], [P, cols.stop - cols.start], F32)
                nc.scalar.copy(h[:], sums[u])
                place(u, h[:], wg1_t[:, u, cols], list3, cols)
                if (i, u) == (1, 0):
                    weave_blend(2, 1)
                    quantize_blend(2)
            if i > 0:
                for done in ([0, 1] if i == 1 else [2]):
                    nc.scalar.copy(h1_last[:, pieces[done]], last_sums[done])
        place(3, h1_last[:], wg1_t[:, 3, :], list3, slice(0, S))

        def relu(u):
            nc.scalar.activation(
                z_pairs[:].rearrange("p (h t e) -> p h t e", h=2, e=2)[:, u // 2, :, u % 2],
                pages[u][:], ACT.Relu, bias=biases[:, u : u + 1],
            )

        for u in (0, 2, 1):
            relu(u)
        pair_words = z_pairs[:].bitcast(F32).rearrange("p (h t) -> p t h", h=2)
        groups = [(128, 128), (256, 256), (256, 256), (256, 512)]
        widths = [width for group in groups for width in group]
        parts = [slice(sum(widths[:c]), sum(widths[: c + 1])) for c in range(len(widths))]
        shared = slice(T2 - P, T2)
        z_part = []
        for group in groups:
            start = parts[len(z_part)].start
            stop = start + sum(group)
            woven = placed("z_woven%d" % start, AT_TAB + start * PACK * 2 // 1024, [P, PACK * sum(group)], BF16)
            words = woven[:].bitcast(F32).rearrange("p (t h) -> p t h", h=2)
            cut = min(stop, T2 - UNIT)
            nc.scalar.copy(words[:, 0 : cut - start], pair_words[:, start:cut, :])
            if cut < stop:
                nc.vector.tensor_copy(words[:, cut - start :], pair_words[:, cut:stop, :])
                nc.scalar.activation(
                    woven[:].rearrange("p (t u) -> p t u", u=PACK)[:, shared.start - start :, PACK - 1],
                    pages[PACK - 1][:, shared], ACT.Relu, bias=biases[:, PACK - 1 : PACK],
                )
            for cols in parts[len(z_part) : len(z_part) + len(group)]:
                z_part.append(woven[:, PACK * (cols.start - start) : PACK * (cols.stop - start)])

        zc = placed("zc", AT_H2, [P, T2], U32)
        zs = held("zs", [P, T2], U8)
        out_rows = out.rearrange("(nb p) t -> p nb t", p=P)

        def last_relu(c):
            cols = slice(parts[c].start, min(parts[c].stop, shared.start))
            nc.vector.tensor_scalar(
                z_part[c].rearrange("p (t u) -> p t u", u=PACK)[:, 0 : cols.stop - cols.start, PACK - 1],
                pages[PACK - 1][:, cols], biases[:, PACK - 1 : PACK], 0.0, ADD, MAX,
            )

        def product(acc, nb, cols):
            nc.tensor.matmul_mx(
                out=acc,
                lhsT=w3c[:, P * nb : P * (nb + 1)].bitcast(FP8X4),
                lhsT_scale=w3s[:, P * nb : P * (nb + 1)],
                rhs=zc[:, cols].bitcast(FP8X4),
                rhs_scale=zs[:, cols],
                start=True,
                stop=True,
            )

        done = 0
        for group in groups:
            mine = range(done, done + len(group))
            done = mine.stop
            for c in mine:
                last_relu(c)
            for c in mine:
                quantize(zc[:, parts[c]], zs[:, parts[c]], z_part[c])

        filled = []

        def staging(cols):
            at = AT_STAGED + cols.start * PACK * 4 // 1024
            return placed("staged%d" % cols.start, at, [P, PACK, cols.stop - cols.start], F32)

        def fill_and_empty(copy, dst, blocks, cols):
            width = cols.stop - cols.start
            acc = bank("acc_out", len(filled) % 8)
            filled.append(acc)
            for part in parts:
                if cols.start <= part.start < cols.stop:
                    for e, nb in enumerate(range(blocks.start, blocks.stop)):
                        at = e * width + part.start - cols.start
                        product(acc[:, at : at + part.stop - part.start], nb, part)
            count = blocks.stop - blocks.start
            copy(dst, acc[:, 0 : count * width].rearrange("p (b t) -> p b t", b=count))

        def narrow_features(cols, together):
            staged = staging(cols)
            for nb in range(0, PACK, together):
                blocks = slice(nb, nb + together)
                fill_and_empty(nc.scalar.copy, staged[:, blocks, :], blocks, cols)
                nc.sync.dma_start(out_rows[:, blocks, cols], staged[:, blocks, :])

        def wide_features(cols):
            staged = staging(cols)
            halves = [slice(cols.start, cols.start + BANK), slice(cols.start + BANK, cols.stop)]
            early, copies = slice(0, 2), (nc.vector.tensor_copy, nc.scalar.copy)
            for nb in range(early.stop):
                block = slice(nb, nb + 1)
                fill_and_empty(copies[nb], staged[:, block, low], block, halves[0])
                nc.sync.dma_start(out_rows[:, block, halves[0]], staged[:, block, low])
            for nb in range(early.stop, PACK):
                block = slice(nb, nb + 1)
                fill_and_empty(nc.scalar.copy, staged[:, block, low], block, halves[0])
                fill_and_empty(nc.vector.tensor_copy, staged[:, block, high], block, halves[1])
                nc.sync.dma_start(out_rows[:, block, cols], staged[:, block, :])
            for nb in range(early.stop):
                block = slice(nb, nb + 1)
                fill_and_empty(copies[nb], staged[:, block, high], block, halves[1])
            nc.sync.dma_start(out_rows[:, early, halves[1]], staged[:, early, high])

        narrow_features(first, 1)
        narrow_features(second, 2)
        narrow_features(high, 1)
        wide_features(slice(S, T2))
